import numpy as np
import ml_dtypes


def mxq(x, axis, fmt="e4m3"):
    dtype, down = {"e4m3": (ml_dtypes.float8_e4m3fn, 7), "e5m2": (ml_dtypes.float8_e5m2, 14)}[fmt]
    v = np.moveaxis(np.asarray(x, np.float32).astype(ml_dtypes.bfloat16).astype(np.float64), axis, -1)
    blocks = v.reshape(v.shape[:-1] + (-1, 32))
    amax = np.abs(blocks).max(-1, keepdims=True)
    byte = np.maximum(np.where(amax > 0, np.frexp(amax)[1] - 1 + 127, 0) - down, 1)
    scale = np.exp2(byte - 127.0)
    codes = (blocks / scale).astype(np.float32).astype(dtype).astype(np.float64)
    return np.moveaxis((codes * scale).reshape(v.shape), -1, axis)


WIDE = False


def mx_kscale(k):
    if not WIDE:
        return np.ones(k)
    levels = np.array([10, -10, 5, -5, 0])
    if k % 512:
        return np.exp2(np.random.permutation(np.resize(levels, k // 32))).repeat(32)
    a = np.empty((k // 512, 16))
    for p in range(k // 512):
        a[p, :8] = np.random.permutation(np.resize(levels, 8))
        for g in range(8):
            far = levels[np.abs(levels - a[p, g]) >= 10]
            a[p, g + 8] = far[np.random.randint(len(far))]
    return np.exp2(a.ravel()).repeat(32)


def f64(x):
    return np.asarray(x).astype(np.float64)


def striped(idx):
    return np.tile(idx.reshape(-1, 16).T, (8, 1)).astype(np.uint16)


def unstriped(offs):
    return offs[:16].T.reshape(-1).astype(np.int64)


def relu(v):
    return np.maximum(v, 0.0)

def planes(y):
    n, m = y.shape
    v = y.astype(np.float32).astype(ml_dtypes.bfloat16).astype(np.float64).reshape(n // 32, 32, m)
    top = np.abs(v).max(1)
    byte = np.clip(np.where(top > 0, np.frexp(top)[1] - 1 + 127 - 7, 1), 1, 254)
    codes = (v * np.exp2(127.0 - byte)[:, None, :]).reshape(n, m).astype(np.float32).astype(ml_dtypes.float8_e4m3fn).view(np.uint8)
    words = codes.reshape(n // 512, 128, 4, m).transpose(0, 1, 3, 2)
    return np.ascontiguousarray(words), np.ascontiguousarray(byte.astype(np.uint8).reshape(n // 512, 16, m))


K, T, S, H = 512, 2048, 1024, 512
P = 2 ** 7


def setup_inputs():
    n = np.random.standard_normal
    s = mx_kscale(K)[:, None]
    u = mx_kscale(H)
    return {
        "xT": (n((K, T)) * s).astype(np.float32),
        "w1": (n((K, H)) / np.sqrt(K) / s * u).astype(np.float32),
        "w2": (n((H, H)) / np.sqrt(H) / u[:, None]).astype(np.float32),
        "share": np.tile(np.random.uniform(0.1, 0.9, S), (P, 1)).astype(np.float32),
        "offs": striped(np.random.permutation(T)[:S]),
        "par": striped(np.random.permutation(S)[(S * np.random.uniform(0, 1, S) ** 4).astype(np.int64)]),
    }


def reference(xT, w1, w2, share, offs, par):
    xq = mxq(f64(xT)[:, unstriped(offs)], 0, "e4m3")
    h = relu(mxq(f64(w1), 0, "e4m3").T @ xq)
    z = h + h[:, unstriped(par)] * f64(share)[:1]
    out_0 = mxq(f64(w2), 0, "e4m3").T @ mxq(z, 0, "e4m3")
    return (out_0,) + planes(out_0)

@@ -1,0 +1,174 @@
+from contextlib import ExitStack
+
+import concourse.mybir as mybir
+
+K, T, S, H = 512, 2048, 1024, 512
+FLOPS = 2 * K * H * S + 2 * H * H * S
+
+F32 = mybir.dt.float32
+BF16 = mybir.dt.bfloat16
+I32 = mybir.dt.int32
+U32 = mybir.dt.uint32
+U16 = mybir.dt.uint16
+U8 = mybir.dt.uint8
+FP8X4 = mybir.dt.float8_e4m3fn_x4
+MULT = mybir.AluOpType.mult
+ADD = mybir.AluOpType.add
+COPY = mybir.ActivationFunctionType.Copy
+RELU = mybir.ActivationFunctionType.Relu
+
+P = 128
+PACK = 4
+LIST_COL = 16
+X_PIECE = 256
+HALF = 512
+BLOCK = 128
+CHUNKS = (256, 256, 256, 128, 128)
+SLOT_ORDER = (2, 3, 1, 0)
+
+
+def entries(list_tile, start, count):
+    return list_tile[:, start // LIST_COL : (start + count) // LIST_COL]
+
+
+def woven(ap):
+    return ap.rearrange("p (c i t) -> p c t i", i=4, t=PACK)
+
+
+def planar(ap):
+    return ap.rearrange("p t (c i) -> p c t i", i=4)
+
+
+def tile_picked_treeup_relu_lo_kernel(tc, xT, w1, w2, share, offs, par, out_0, out_1, out_2):
+    nc = tc.nc
+    with ExitStack() as ctx:
+        keep = ctx.enter_context(tc.tile_pool(name="keep", bufs=1))
+        ring = ctx.enter_context(tc.tile_pool(name="ring", bufs=3))
+        psum = ctx.enter_context(tc.psum_pool(name="psum", bufs=8))
+
+        offs_sb = keep.tile([P, S // LIST_COL], U16, name="offs_sb")
+        par_sb = keep.tile([P, S // LIST_COL], U16, name="par_sb")
+        x_rows = [keep.tile([P, T], F32, name="x_rows%d" % j) for j in range(PACK)]
+        w1_raw = keep.tile([P, PACK, H], F32, name="w1_raw")
+        w2_raw = keep.tile([P, PACK, H], F32, name="w2_raw")
+        share_sb = keep.tile([P, S], F32, name="share_sb")
+
+        x_view = xT.rearrange("(p j) s -> j p s", j=PACK)
+        nc.sync.dma_start(offs_sb[:], offs)
+        for j in range(PACK):
+            nc.sync.dma_start(x_rows[j][:], x_view[j])
+        nc.sync.dma_start(w1_raw[:], w1.rearrange("(p j) c -> p j c", j=PACK))
+        nc.sync.dma_start(par_sb[:], par)
+        nc.sync.dma_start(share_sb[:], share)
+        nc.sync.dma_start(w2_raw[:], w2.rearrange("(p j) c -> p j c", j=PACK))
+
+        n_pieces = S // X_PIECE
+        picked = keep.tile([P, PACK, S], BF16, name="picked", align_bytes=64)
+        x_woven = [keep.tile([P, PACK * X_PIECE], BF16, name="x_woven%d" % q, align_bytes=64) for q in range(n_pieces)]
+        x_codes = keep.tile([P, S], U32, name="x_codes", align_bytes=64)
+        x_scales = keep.tile([P, S], U8, name="x_scales", align_bytes=64)
+        for j in range(PACK - 1):
+            nc.vector.tensor_copy(picked[:, j, :], x_rows[j][:].indirect(offs_sb[:]))
+        for q in range(n_pieces):
+            cols = slice(q * X_PIECE, (q + 1) * X_PIECE)
+            nc.vector.tensor_copy(picked[:, PACK - 1, cols], x_rows[PACK - 1][:].indirect(entries(offs_sb, q * X_PIECE, X_PIECE)))
+        for q in range(n_pieces):
+            cols = slice(q * X_PIECE, (q + 1) * X_PIECE)
+            if q == 0:
+                nc.scalar.activation(woven(x_woven[q][:]), planar(picked[:, :, cols]), COPY)
+            elif q == 1:
+                nc.scalar.copy(woven(x_woven[q][:]), planar(picked[:, :, cols]))
+            else:
+                nc.vector.tensor_copy(woven(x_woven[q][:]), planar(picked[:, :, cols]))
+
+        def deal(engine_copy, raw, dealt, t0, nt):
+            engine_copy(
+                dealt.rearrange("p (t m j) -> p m j t", t=nt, j=PACK),
+                raw[:].rearrange("p j (m t) -> p m j t", t=PACK)[:, :, :, t0 : t0 + nt],
+            )
+
+        w1_dealt = [keep.tile([P, 2 * P * PACK], BF16, name="w1_dealt%d" % u, align_bytes=64) for u in range(2)]
+        w1_codes = [keep.tile([P, 2 * P], U32, name="w1_codes%d" % u, align_bytes=64) for u in range(2)]
+        w1_scales = [keep.tile([P, 2 * P], U8, name="w1_scales%d" % u, align_bytes=64) for u in range(2)]
+        deal(nc.scalar.copy, w1_raw, w1_dealt[1][:], 2, 2)
+        for q in range(n_pieces):
+            cols = slice(q * X_PIECE, (q + 1) * X_PIECE)
+            nc.vector.quantize_mx(out=x_codes[:, cols].bitcast(FP8X4), scales=x_scales[:, cols], in_=x_woven[q][:])
+        nc.vector.quantize_mx(out=w1_codes[1][:].bitcast(FP8X4), scales=w1_scales[1][:], in_=w1_dealt[1][:])
+        deal(nc.vector.tensor_copy, w1_raw, w1_dealt[0][:], 0, 2)
+        nc.vector.quantize_mx(out=w1_codes[0][:].bitcast(FP8X4), scales=w1_scales[0][:], in_=w1_dealt[0][:])
+
+        h_all = keep.tile([P, PACK * S], F32, name="h_all")
+        h_rows = {t: keep.tile([P, S], F32, name="h_rows%d" % t) for t in range(1, PACK)}
+        for t in SLOT_ORDER:
+            target = h_rows[t] if t > 0 else h_all
+            w_cols = slice((t % 2) * P, (t % 2 + 1) * P)
+            for s0 in range(0, S, HALF):
+                cols = slice(s0, s0 + HALF)
+                bank = psum.tile([P, HALF], F32, name="bank")
+                nc.tensor.matmul_mx(
+                    out=bank[:],
+                    lhsT=w1_codes[t // 2][:, w_cols].bitcast(FP8X4),
+                    lhsT_scale=w1_scales[t // 2][:, w_cols],
+                    rhs=x_codes[:, cols].bitcast(FP8X4),
+                    rhs_scale=x_scales[:, cols],
+                    start=True,
+                    stop=True,
+                )
+                nc.scalar.activation(target[:, cols], bank[:], RELU)
+            if t > 0:
+                nc.sync.dma_start(h_all[:, t * S : (t + 1) * S], h_rows[t][:])
+
+        w2_dealt = keep.tile([P, H * PACK], BF16, name="w2_dealt", align_bytes=64)
+        w2_codes = keep.tile([P, H], U32, name="w2_codes", align_bytes=64)
+        w2_scales = keep.tile([P, H], U8, name="w2_scales", align_bytes=64)
+        deal(nc.scalar.copy, w2_raw, w2_dealt[:], 0, PACK)
+        nc.vector.quantize_mx(out=w2_codes[:].bitcast(FP8X4), scales=w2_scales[:], in_=w2_dealt[:])
+
+        y_codes = keep.tile([P, S], U32, name="y_codes", align_bytes=64)
+        y_scales = keep.tile([P, S], U8, name="y_scales", align_bytes=64)
+        h_planes = h_all[:].rearrange("p (t s) -> p t s", t=PACK)
+        y_view = out_0.rearrange("(p t) s -> p t s", t=PACK)
+        words_view = out_1[0].rearrange("p c r -> p (c r)").bitcast(I32)
+        s0 = 0
+        for c, n in enumerate(CHUNKS):
+            cols = slice(s0, s0 + n)
+            taken = ring.tile([P, PACK, n], F32, name="taken")
+            for t in SLOT_ORDER:
+                window = h_rows[t] if t > 0 else h_all
+                nc.vector.tensor_tensor(taken[:, t, :], window[:].indirect(entries(par_sb, s0, n)), share_sb[:, cols], MULT)
+            z_woven = keep.tile([P, PACK * n], BF16, name="z_woven%d" % c, align_bytes=64)
+            nc.vector.tensor_tensor(woven(z_woven[:]), planar(taken[:]), planar(h_planes[:, :, cols]), ADD)
+            z_codes = keep.tile([P, n], U32, name="z_codes%d" % c, align_bytes=64)
+            z_scales = keep.tile([P, n], U8, name="z_scales%d" % c, align_bytes=64)
+            nc.vector.quantize_mx(out=z_codes[:].bitcast(FP8X4), scales=z_scales[:], in_=z_woven[:])
+
+            y_rows = keep.tile([P, PACK, n], F32, name="y_rows%d" % c)
+            y_woven = keep.tile([P, PACK * n], BF16, name="y_woven%d" % c, align_bytes=64)
+            for b0 in range(0, n, BLOCK):
+                block = slice(b0, b0 + BLOCK)
+                bank = psum.tile([P, PACK, BLOCK], F32, name="bank")
+                for t in range(PACK):
+                    w_cols = slice(t * P, (t + 1) * P)
+                    nc.tensor.matmul_mx(
+                        out=bank[:, t, :],
+                        lhsT=w2_codes[:, w_cols].bitcast(FP8X4),
+                        lhsT_scale=w2_scales[:, w_cols],
+                        rhs=z_codes[:, block].bitcast(FP8X4),
+                        rhs_scale=z_scales[:, block],
+                        start=True,
+                        stop=True,
+                    )
+                nc.scalar.copy(
+                    y_woven[:, PACK * b0 : PACK * (b0 + BLOCK)].rearrange("p (s t) -> p s t", t=PACK),
+                    bank[:].rearrange("p t s -> p s t"),
+                )
+                nc.scalar.copy(y_rows[:, :, block], bank[:])
+            nc.vector.quantize_mx(out=y_codes[:, cols].bitcast(FP8X4), scales=y_scales[:, cols], in_=y_woven[:])
+            nc.sync.dma_start(y_view[:, :, cols], y_rows[:])
+            nc.sync.dma_start(words_view[:, cols], y_codes[:, cols].bitcast(I32))
+            s0 += n
+
+        scales_view = out_2[0].bitcast(I32)
+        for q in range(4):
+            nc.sync.dma_start(scales_view[4 * q : 4 * q + 4, :], y_scales[32 * q : 32 * q + 4, :].bitcast(I32))

@@ -1,6 +1,7 @@
 from contextlib import ExitStack
 
 import concourse.mybir as mybir
+from concourse.masks import make_identity
 
 K, T, S, H = 512, 2048, 1024, 512
 FLOPS = 2 * K * H * S + 2 * H * H * S
@@ -24,6 +25,11 @@ X_PIECE = 256
 HALF = 512
 BLOCK = 128
 CHUNKS = (256, 256, 256, 128, 128)
+TAKEN_TAGS = ("A", "B", "A", "Z1", "Z1")
+TURNED_CHUNKS = 2
+WOVEN_TAGS = ("Z0", "Z1", "Z0", "Z3", "Z4")
+WOVEN_BY_VECTOR = (2, 3,)
+BANK_ORDER = (0, 1, 2, 3, 4, 5, 6, 7, 0, 1, 2, 3, 4, 5, 6, 5, 7, 0, 1, 2, 3, 4, 6)
 SLOT_ORDER = (2, 3, 1, 0)
 
 
@@ -43,8 +49,7 @@ def tile_picked_treeup_relu_lo_kernel(tc, xT, w1, w2, share, offs, par, out_0, o
     nc = tc.nc
     with ExitStack() as ctx:
         keep = ctx.enter_context(tc.tile_pool(name="keep", bufs=1))
-        ring = ctx.enter_context(tc.tile_pool(name="ring", bufs=3))
-        psum = ctx.enter_context(tc.psum_pool(name="psum", bufs=8))
+        psum = ctx.enter_context(tc.psum_pool(name="psum", bufs=1))
 
         offs_sb = keep.tile([P, S // LIST_COL], U16, name="offs_sb")
         par_sb = keep.tile([P, S // LIST_COL], U16, name="par_sb")
@@ -58,15 +63,14 @@ def tile_picked_treeup_relu_lo_kernel(tc, xT, w1, w2, share, offs, par, out_0, o
         for j in range(PACK):
             nc.sync.dma_start(x_rows[j][:], x_view[j])
         nc.sync.dma_start(w1_raw[:], w1.rearrange("(p j) c -> p j c", j=PACK))
+        nc.sync.dma_start(w2_raw[:], w2.rearrange("(p j) c -> p j c", j=PACK))
         nc.sync.dma_start(par_sb[:], par)
         nc.sync.dma_start(share_sb[:], share)
-        nc.sync.dma_start(w2_raw[:], w2.rearrange("(p j) c -> p j c", j=PACK))
 
         n_pieces = S // X_PIECE
         picked = keep.tile([P, PACK, S], BF16, name="picked", align_bytes=64)
-        x_woven = [keep.tile([P, PACK * X_PIECE], BF16, name="x_woven%d" % q, align_bytes=64) for q in range(n_pieces)]
+        x_woven = [keep.tile([P, PACK * X_PIECE], BF16, name="x_woven%d" % q, tag="x_woven%d" % q, align_bytes=64) for q in range(n_pieces)]
         x_codes = keep.tile([P, S], U32, name="x_codes", align_bytes=64)
-        x_scales = keep.tile([P, S], U8, name="x_scales", align_bytes=64)
         for j in range(PACK - 1):
             nc.vector.tensor_copy(picked[:, j, :], x_rows[j][:].indirect(offs_sb[:]))
         for q in range(n_pieces):
@@ -87,67 +91,116 @@ def tile_picked_treeup_relu_lo_kernel(tc, xT, w1, w2, share, offs, par, out_0, o
                 raw[:].rearrange("p j (m t) -> p m j t", t=PACK)[:, :, :, t0 : t0 + nt],
             )
 
-        w1_dealt = [keep.tile([P, 2 * P * PACK], BF16, name="w1_dealt%d" % u, align_bytes=64) for u in range(2)]
+        w1_dealt = {1: keep.tile([P, 2 * P * PACK], BF16, name="w1_dealt1", tag="w1_first", align_bytes=64)}
         w1_codes = [keep.tile([P, 2 * P], U32, name="w1_codes%d" % u, align_bytes=64) for u in range(2)]
         w1_scales = [keep.tile([P, 2 * P], U8, name="w1_scales%d" % u, align_bytes=64) for u in range(2)]
         deal(nc.scalar.copy, w1_raw, w1_dealt[1][:], 2, 2)
+        x_scales = [keep.tile([P, HALF], U8, name="x_scales0", align_bytes=64)]
         for q in range(n_pieces):
             cols = slice(q * X_PIECE, (q + 1) * X_PIECE)
-            nc.vector.quantize_mx(out=x_codes[:, cols].bitcast(FP8X4), scales=x_scales[:, cols], in_=x_woven[q][:])
-        nc.vector.quantize_mx(out=w1_codes[1][:].bitcast(FP8X4), scales=w1_scales[1][:], in_=w1_dealt[1][:])
+            if q == 2:
+                nc.vector.quantize_mx(out=w1_codes[1][:].bitcast(FP8X4), scales=w1_scales[1][:], in_=w1_dealt[1][:])
+                x_scales.append(keep.tile([P, HALF], U8, name="x_scales1", tag="w1_first", align_bytes=64))
+            part = slice((q % 2) * X_PIECE, (q % 2 + 1) * X_PIECE)
+            nc.vector.quantize_mx(out=x_codes[:, cols].bitcast(FP8X4), scales=x_scales[q // 2][:, part], in_=x_woven[q][:])
+        w1_dealt[0] = keep.tile([P, 2 * P * PACK], BF16, name="w1_dealt0", tag="x_woven3", align_bytes=64)
         deal(nc.vector.tensor_copy, w1_raw, w1_dealt[0][:], 0, 2)
         nc.vector.quantize_mx(out=w1_codes[0][:].bitcast(FP8X4), scales=w1_scales[0][:], in_=w1_dealt[0][:])
 
-        h_all = keep.tile([P, PACK * S], F32, name="h_all")
-        h_rows = {t: keep.tile([P, S], F32, name="h_rows%d" % t) for t in range(1, PACK)}
+        identity = keep.tile([P, P], F32, name="identity")
+        make_identity(nc, identity[:])
+
+        w2_dealt = keep.tile([P, H * PACK], BF16, name="w2_dealt", align_bytes=64)
+        w2_codes = keep.tile([P, H], U32, name="w2_codes", align_bytes=64)
+        w2_scales = keep.tile([P, H], U8, name="w2_scales", align_bytes=64)
+
+        bank_order = list(BANK_ORDER)
+
+        def next_bank(shape):
+            return psum.tile(shape, F32, name="bank", tag="bank%d" % bank_order.pop(0))
+
+        turned = sum(CHUNKS[:TURNED_CHUNKS])
+        h_rows = [keep.tile([P, S], F32, name="h_rows%d" % t) for t in range(PACK)]
+        h_late = keep.tile([P, PACK, S - turned], F32, name="h_late")
         for t in SLOT_ORDER:
-            target = h_rows[t] if t > 0 else h_all
             w_cols = slice((t % 2) * P, (t % 2 + 1) * P)
-            for s0 in range(0, S, HALF):
-                cols = slice(s0, s0 + HALF)
-                bank = psum.tile([P, HALF], F32, name="bank")
+            widths = (HALF, X_PIECE, X_PIECE) if t == SLOT_ORDER[0] else (HALF, HALF)
+            for k, width in enumerate(widths):
+                s0 = sum(widths[:k])
+                cols = slice(s0, s0 + width)
+                bank = next_bank([P, width])
                 nc.tensor.matmul_mx(
                     out=bank[:],
                     lhsT=w1_codes[t // 2][:, w_cols].bitcast(FP8X4),
                     lhsT_scale=w1_scales[t // 2][:, w_cols],
                     rhs=x_codes[:, cols].bitcast(FP8X4),
-                    rhs_scale=x_scales[:, cols],
+                    rhs_scale=x_scales[s0 // HALF][:, s0 % HALF : s0 % HALF + width],
                     start=True,
                     stop=True,
                 )
-                nc.scalar.activation(target[:, cols], bank[:], RELU)
-            if t > 0:
-                nc.sync.dma_start(h_all[:, t * S : (t + 1) * S], h_rows[t][:])
+                nc.scalar.activation(h_rows[t][:, cols], bank[:], RELU)
+            nc.sync.dma_start(h_late[:, t, :], h_rows[t][:, turned:])
 
-        w2_dealt = keep.tile([P, H * PACK], BF16, name="w2_dealt", align_bytes=64)
-        w2_codes = keep.tile([P, H], U32, name="w2_codes", align_bytes=64)
-        w2_scales = keep.tile([P, H], U8, name="w2_scales", align_bytes=64)
-        deal(nc.scalar.copy, w2_raw, w2_dealt[:], 0, PACK)
+        for u in range(2):
+            deal(nc.scalar.copy, w2_raw, w2_dealt[:, 2 * u * P * PACK : 2 * (u + 1) * P * PACK], 2 * u, 2)
         nc.vector.quantize_mx(out=w2_codes[:].bitcast(FP8X4), scales=w2_scales[:], in_=w2_dealt[:])
 
         y_codes = keep.tile([P, S], U32, name="y_codes", align_bytes=64)
         y_scales = keep.tile([P, S], U8, name="y_scales", align_bytes=64)
-        h_planes = h_all[:].rearrange("p (t s) -> p t s", t=PACK)
         y_view = out_0.rearrange("(p t) s -> p t s", t=PACK)
         words_view = out_1[0].rearrange("p c r -> p (c r)").bitcast(I32)
-        s0 = 0
-        for c, n in enumerate(CHUNKS):
-            cols = slice(s0, s0 + n)
-            taken = ring.tile([P, PACK, n], F32, name="taken")
+        starts = [sum(CHUNKS[:c]) for c in range(len(CHUNKS))]
+        taken, z_woven, y_woven, y_rows = {}, {}, {}, {}
+
+        def gather(c):
+            n = CHUNKS[c]
+            taken[c] = keep.tile([P, PACK, n], F32, name="taken%d" % c, tag=TAKEN_TAGS[c], align_bytes=64)
             for t in SLOT_ORDER:
-                window = h_rows[t] if t > 0 else h_all
-                nc.vector.tensor_tensor(taken[:, t, :], window[:].indirect(entries(par_sb, s0, n)), share_sb[:, cols], MULT)
-            z_woven = keep.tile([P, PACK * n], BF16, name="z_woven%d" % c, align_bytes=64)
-            nc.vector.tensor_tensor(woven(z_woven[:]), planar(taken[:]), planar(h_planes[:, :, cols]), ADD)
+                nc.vector.tensor_tensor(
+                    taken[c][:, t, :], h_rows[t][:].indirect(entries(par_sb, starts[c], n)), share_sb[:, starts[c] : starts[c] + n], MULT
+                )
+
+        def add_turned(c):
+            n = CHUNKS[c]
+            z_woven[c] = keep.tile([P, PACK * n], BF16, name="z_woven%d" % c, tag=WOVEN_TAGS[c], align_bytes=64)
+            pairs = []
+            for b0 in range(0, n, BLOCK):
+                bank = next_bank([P, PACK, P])
+                for t in SLOT_ORDER:
+                    own = h_rows[t][:, starts[c] + b0 : starts[c] + b0 + BLOCK]
+                    nc.tensor.matmul(bank[:, t, :], own, identity[:], start=True, stop=False, is_transpose=True)
+                    nc.tensor.matmul(bank[:, t, :], taken[c][:, t, b0 : b0 + BLOCK], identity[:], start=False, stop=True, is_transpose=True)
+                pair = keep.tile([P, H], BF16, name="pair%d_%d" % (c, b0))
+                nc.scalar.copy(
+                    pair[:].rearrange("s (u p e) -> s u p e", u=2, e=2),
+                    bank[:].rearrange("s (u e) p -> s u p e", e=2),
+                )
+                pairs.append(pair)
+            back = next_bank([P, len(pairs), 2, BLOCK])
+            for b, pair in enumerate(pairs):
+                for u in range(2):
+                    nc.tensor.transpose(back[:, b, u, :], pair[:].bitcast(F32)[:, u * P : (u + 1) * P], identity[:])
+            nc.scalar.copy(
+                z_woven[c][:].bitcast(F32).rearrange("p (b s u) -> p b s u", s=BLOCK, u=2),
+                back[:].rearrange("p b u s -> p b s u"),
+            )
+
+        def add_direct(c):
+            n = CHUNKS[c]
+            z_woven[c] = keep.tile([P, PACK * n], BF16, name="z_woven%d" % c, tag=WOVEN_TAGS[c], align_bytes=64)
+            own = h_late[:, :, starts[c] - turned : starts[c] - turned + n]
+            nc.vector.tensor_tensor(woven(z_woven[c][:]), planar(taken[c][:]), planar(own), ADD)
+
+        def second_layer(c):
+            n = CHUNKS[c]
             z_codes = keep.tile([P, n], U32, name="z_codes%d" % c, align_bytes=64)
             z_scales = keep.tile([P, n], U8, name="z_scales%d" % c, align_bytes=64)
-            nc.vector.quantize_mx(out=z_codes[:].bitcast(FP8X4), scales=z_scales[:], in_=z_woven[:])
-
-            y_rows = keep.tile([P, PACK, n], F32, name="y_rows%d" % c)
-            y_woven = keep.tile([P, PACK * n], BF16, name="y_woven%d" % c, align_bytes=64)
+            nc.vector.quantize_mx(out=z_codes[:].bitcast(FP8X4), scales=z_scales[:], in_=z_woven[c][:])
+            y_rows[c] = keep.tile([P, PACK, n], F32, name="y_rows%d" % c)
+            y_woven[c] = keep.tile([P, PACK * n], BF16, name="y_woven%d" % c, align_bytes=64)
             for b0 in range(0, n, BLOCK):
                 block = slice(b0, b0 + BLOCK)
-                bank = psum.tile([P, PACK, BLOCK], F32, name="bank")
+                bank = next_bank([P, PACK, BLOCK])
                 for t in range(PACK):
                     w_cols = slice(t * P, (t + 1) * P)
                     nc.tensor.matmul_mx(
@@ -159,16 +212,43 @@ def tile_picked_treeup_relu_lo_kernel(tc, xT, w1, w2, share, offs, par, out_0, o
                         start=True,
                         stop=True,
                     )
-                nc.scalar.copy(
-                    y_woven[:, PACK * b0 : PACK * (b0 + BLOCK)].rearrange("p (s t) -> p s t", t=PACK),
-                    bank[:].rearrange("p t s -> p s t"),
-                )
-                nc.scalar.copy(y_rows[:, :, block], bank[:])
-            nc.vector.quantize_mx(out=y_codes[:, cols].bitcast(FP8X4), scales=y_scales[:, cols], in_=y_woven[:])
-            nc.sync.dma_start(y_view[:, :, cols], y_rows[:])
+                if c not in WOVEN_BY_VECTOR:
+                    nc.scalar.copy(
+                        y_woven[c][:, PACK * b0 : PACK * (b0 + BLOCK)].rearrange("p (s t) -> p s t", t=PACK),
+                        bank[:].rearrange("p t s -> p s t"),
+                    )
+                nc.scalar.copy(y_rows[c][:, :, block], bank[:])
+            nc.sync.dma_start(y_view[:, :, starts[c] : starts[c] + n], y_rows[c][:])
+
+        def hand_on(c):
+            cols = slice(starts[c], starts[c] + CHUNKS[c])
+            if c in WOVEN_BY_VECTOR:
+                nc.vector.tensor_copy(woven(y_woven[c][:]), planar(y_rows[c][:]))
+            nc.vector.quantize_mx(out=y_codes[:, cols].bitcast(FP8X4), scales=y_scales[:, cols], in_=y_woven[c][:])
             nc.sync.dma_start(words_view[:, cols], y_codes[:, cols].bitcast(I32))
-            s0 += n
+
+        gather(0)
+        gather(1)
+        add_turned(0)
+        add_turned(1)
+        gather(2)
+        second_layer(0)
+        add_direct(2)
+        second_layer(1)
+        second_layer(2)
+        gather(3)
+        add_direct(3)
+        second_layer(3)
+        gather(4)
+        add_direct(4)
+        second_layer(4)
+        hand_on(0)
+        hand_on(1)
+        hand_on(2)
+        hand_on(3)
+        hand_on(4)
 
         scales_view = out_2[0].bitcast(I32)
         for q in range(4):
-            nc.sync.dma_start(scales_view[4 * q : 4 * q + 4, :], y_scales[32 * q : 32 * q + 4, :].bitcast(I32))
+            queue = nc.sync if q % 2 == 0 else nc.scalar
+            queue.dma_start(scales_view[4 * q : 4 * q + 4, :], y_scales[32 * q : 32 * q + 4, :].bitcast(I32))

@@ -21,16 +21,11 @@ RELU = mybir.ActivationFunctionType.Relu
 P = 128
 PACK = 4
 LIST_COL = 16
-X_PIECE = 256
 HALF = 512
+QUARTER = 256
 BLOCK = 128
-CHUNKS = (256, 256, 256, 128, 128)
-TAKEN_TAGS = ("A", "B", "A", "Z1", "Z1")
-TURNED_CHUNKS = 2
-WOVEN_TAGS = ("Z0", "Z1", "Z0", "Z3", "Z4")
-WOVEN_BY_VECTOR = (2, 3,)
-BANK_ORDER = (0, 1, 2, 3, 4, 5, 6, 7, 0, 1, 2, 3, 4, 5, 6, 5, 7, 0, 1, 2, 3, 4, 6)
-SLOT_ORDER = (2, 3, 1, 0)
+BANKS = 8
+LAST_SPLIT = 384
 
 
 def entries(list_tile, start, count):
@@ -53,200 +48,241 @@ def tile_picked_treeup_relu_lo_kernel(tc, xT, w1, w2, share, offs, par, out_0, o
 
         offs_sb = keep.tile([P, S // LIST_COL], U16, name="offs_sb")
         par_sb = keep.tile([P, S // LIST_COL], U16, name="par_sb")
-        x_rows = [keep.tile([P, T], F32, name="x_rows%d" % j) for j in range(PACK)]
         w1_raw = keep.tile([P, PACK, H], F32, name="w1_raw")
         w2_raw = keep.tile([P, PACK, H], F32, name="w2_raw")
         share_sb = keep.tile([P, S], F32, name="share_sb")
 
-        x_view = xT.rearrange("(p j) s -> j p s", j=PACK)
+        x_view = xT.rearrange("(p u e) s -> u p e s", u=2, e=2)
+        x_pieces = [(0, 0, 2 * HALF), (0, 2 * HALF, 2 * HALF)] + [(1, c0, HALF) for c0 in range(0, T, HALF)]
+        x_raw = [keep.tile([P, 2, n], F32, name="x_raw%d" % k) for k, (u, c0, n) in enumerate(x_pieces)]
         nc.sync.dma_start(offs_sb[:], offs)
-        for j in range(PACK):
-            nc.sync.dma_start(x_rows[j][:], x_view[j])
+        for k, (u, c0, n) in enumerate(x_pieces):
+            nc.sync.dma_start(x_raw[k][:], x_view[u][:, :, c0 : c0 + n])
         nc.sync.dma_start(w1_raw[:], w1.rearrange("(p j) c -> p j c", j=PACK))
         nc.sync.dma_start(w2_raw[:], w2.rearrange("(p j) c -> p j c", j=PACK))
         nc.sync.dma_start(par_sb[:], par)
         nc.sync.dma_start(share_sb[:], share)
 
-        n_pieces = S // X_PIECE
-        picked = keep.tile([P, PACK, S], BF16, name="picked", align_bytes=64)
-        x_woven = [keep.tile([P, PACK * X_PIECE], BF16, name="x_woven%d" % q, tag="x_woven%d" % q, align_bytes=64) for q in range(n_pieces)]
-        x_codes = keep.tile([P, S], U32, name="x_codes", align_bytes=64)
-        for j in range(PACK - 1):
-            nc.vector.tensor_copy(picked[:, j, :], x_rows[j][:].indirect(offs_sb[:]))
-        for q in range(n_pieces):
-            cols = slice(q * X_PIECE, (q + 1) * X_PIECE)
-            nc.vector.tensor_copy(picked[:, PACK - 1, cols], x_rows[PACK - 1][:].indirect(entries(offs_sb, q * X_PIECE, X_PIECE)))
-        for q in range(n_pieces):
-            cols = slice(q * X_PIECE, (q + 1) * X_PIECE)
-            if q == 0:
-                nc.scalar.activation(woven(x_woven[q][:]), planar(picked[:, :, cols]), COPY)
-            elif q == 1:
-                nc.scalar.copy(woven(x_woven[q][:]), planar(picked[:, :, cols]))
-            else:
-                nc.vector.tensor_copy(woven(x_woven[q][:]), planar(picked[:, :, cols]))
+        x_pairs = [keep.tile([P, 2 * T], BF16, name="x_pairs%d" % u, align_bytes=64) for u in range(2)]
 
-        def deal(engine_copy, raw, dealt, t0, nt):
-            engine_copy(
-                dealt.rearrange("p (t m j) -> p m j t", t=nt, j=PACK),
-                raw[:].rearrange("p j (m t) -> p m j t", t=PACK)[:, :, :, t0 : t0 + nt],
+        def pair_up(copy, k, lo, hi):
+            u, c0, n = x_pieces[k]
+            copy(
+                x_pairs[u][:, 2 * (c0 + lo) : 2 * (c0 + hi)].rearrange("p (s e) -> p s e", e=2),
+                x_raw[k][:, :, lo:hi].rearrange("p e s -> p s e"),
             )
 
-        w1_dealt = {1: keep.tile([P, 2 * P * PACK], BF16, name="w1_dealt1", tag="w1_first", align_bytes=64)}
-        w1_codes = [keep.tile([P, 2 * P], U32, name="w1_codes%d" % u, align_bytes=64) for u in range(2)]
+        node_parts = [(0, HALF), (HALF, QUARTER), (HALF + QUARTER, QUARTER)]
+        x_woven = [keep.tile([P, PACK * n], BF16, name="x_woven%d" % q, align_bytes=64) for q, (s0, n) in enumerate(node_parts)]
+
+        def pick(u):
+            for q, (s0, n) in enumerate(node_parts):
+                words = x_woven[q][:].bitcast(U32).rearrange("p (s u) -> p s u", u=2)
+                nc.vector.tensor_copy(words[:, :, u], x_pairs[u][:].bitcast(U32).indirect(entries(offs_sb, s0, n)))
+
+        pair_up(lambda out, in_: nc.scalar.activation(out, in_, COPY), 0, 0, 2 * HALF)
+        pair_up(nc.vector.tensor_copy, 1, 0, 2 * HALF)
+        pick(0)
+        for k in range(2, 5):
+            pair_up(nc.scalar.copy, k, 0, HALF)
+        pair_up(nc.vector.tensor_copy, 5, 0, LAST_SPLIT)
+        pair_up(nc.scalar.copy, 5, LAST_SPLIT, HALF)
+        pick(1)
+
+        def deal(engine_copy, raw, dealt, t0, nt, rows=slice(0, P)):
+            engine_copy(
+                dealt.rearrange("p (t m j) -> p m j t", t=nt, j=PACK)[:, rows],
+                raw[:].rearrange("p j (m t) -> p m j t", t=PACK)[:, rows, :, t0 : t0 + nt],
+            )
+
+        w2_dealt = keep.tile([P, H * PACK], BF16, name="w2_dealt", align_bytes=64)
+        w1_first = keep.tile([P, 2 * P * PACK], BF16, name="w1_first", tag="w1_dealt0", align_bytes=64)
+        w1_dealt = [w1_first[:], w2_dealt[:, 2 * P * PACK :]]
+        w1_codes = [keep.tile([P, 2 * P], U32, name="w1_codes%d" % u, tag="w1_codes%d" % u, align_bytes=64) for u in range(2)]
         w1_scales = [keep.tile([P, 2 * P], U8, name="w1_scales%d" % u, align_bytes=64) for u in range(2)]
-        deal(nc.scalar.copy, w1_raw, w1_dealt[1][:], 2, 2)
+        x_codes = keep.tile([P, S], U32, name="x_codes", align_bytes=64)
         x_scales = [keep.tile([P, HALF], U8, name="x_scales0", align_bytes=64)]
-        for q in range(n_pieces):
-            cols = slice(q * X_PIECE, (q + 1) * X_PIECE)
-            if q == 2:
-                nc.vector.quantize_mx(out=w1_codes[1][:].bitcast(FP8X4), scales=w1_scales[1][:], in_=w1_dealt[1][:])
-                x_scales.append(keep.tile([P, HALF], U8, name="x_scales1", tag="w1_first", align_bytes=64))
-            part = slice((q % 2) * X_PIECE, (q % 2 + 1) * X_PIECE)
-            nc.vector.quantize_mx(out=x_codes[:, cols].bitcast(FP8X4), scales=x_scales[q // 2][:, part], in_=x_woven[q][:])
-        w1_dealt[0] = keep.tile([P, 2 * P * PACK], BF16, name="w1_dealt0", tag="x_woven3", align_bytes=64)
-        deal(nc.vector.tensor_copy, w1_raw, w1_dealt[0][:], 0, 2)
-        nc.vector.quantize_mx(out=w1_codes[0][:].bitcast(FP8X4), scales=w1_scales[0][:], in_=w1_dealt[0][:])
+        for u in range(2):
+            deal(nc.scalar.copy, w1_raw, w1_dealt[u], 2 * u, 2)
+        nc.vector.quantize_mx(out=x_codes[:, :HALF].bitcast(FP8X4), scales=x_scales[0][:], in_=x_woven[0][:])
+        nc.vector.quantize_mx(out=w1_codes[0][:].bitcast(FP8X4), scales=w1_scales[0][:], in_=w1_dealt[0])
+        x_scales.append(keep.tile([P, HALF], U8, name="x_scales1", tag="w1_dealt0", align_bytes=64))
+        for q in (1, 2):
+            s0, n = node_parts[q]
+            nc.vector.quantize_mx(out=x_codes[:, s0 : s0 + n].bitcast(FP8X4), scales=x_scales[1][:, s0 - HALF : s0 - HALF + n], in_=x_woven[q][:])
+        nc.vector.quantize_mx(out=w1_codes[1][:].bitcast(FP8X4), scales=w1_scales[1][:], in_=w1_dealt[1])
 
         identity = keep.tile([P, P], F32, name="identity")
         make_identity(nc, identity[:])
 
-        w2_dealt = keep.tile([P, H * PACK], BF16, name="w2_dealt", align_bytes=64)
         w2_codes = keep.tile([P, H], U32, name="w2_codes", align_bytes=64)
         w2_scales = keep.tile([P, H], U8, name="w2_scales", align_bytes=64)
+        deal(nc.vector.tensor_copy, w2_raw, w2_dealt[:, : 2 * P * PACK], 0, 2)
 
-        bank_order = list(BANK_ORDER)
+        bank_turn = [k % BANKS for k in range(4 * BANKS)]
 
         def next_bank(shape):
-            return psum.tile(shape, F32, name="bank", tag="bank%d" % bank_order.pop(0))
+            return psum.tile(shape, F32, name="bank", tag="bank%d" % bank_turn.pop(0))
 
-        turned = sum(CHUNKS[:TURNED_CHUNKS])
         h_rows = [keep.tile([P, S], F32, name="h_rows%d" % t) for t in range(PACK)]
-        h_late = keep.tile([P, PACK, S - turned], F32, name="h_late")
-        for t in SLOT_ORDER:
+        h_late = keep.tile([P, PACK, HALF], F32, name="h_late")
+        for t in range(PACK):
             w_cols = slice((t % 2) * P, (t % 2 + 1) * P)
-            widths = (HALF, X_PIECE, X_PIECE) if t == SLOT_ORDER[0] else (HALF, HALF)
-            for k, width in enumerate(widths):
-                s0 = sum(widths[:k])
-                cols = slice(s0, s0 + width)
-                bank = next_bank([P, width])
+            for s0, n in node_parts if t == 0 else [(0, HALF), (HALF, HALF)]:
+                cols = slice(s0, s0 + n)
+                bank = next_bank([P, n])
                 nc.tensor.matmul_mx(
                     out=bank[:],
                     lhsT=w1_codes[t // 2][:, w_cols].bitcast(FP8X4),
                     lhsT_scale=w1_scales[t // 2][:, w_cols],
                     rhs=x_codes[:, cols].bitcast(FP8X4),
-                    rhs_scale=x_scales[s0 // HALF][:, s0 % HALF : s0 % HALF + width],
+                    rhs_scale=x_scales[s0 // HALF][:, s0 % HALF : s0 % HALF + n],
                     start=True,
                     stop=True,
                 )
                 nc.scalar.activation(h_rows[t][:, cols], bank[:], RELU)
-            nc.sync.dma_start(h_late[:, t, :], h_rows[t][:, turned:])
+            nc.sync.dma_start(h_late[:, t, :], h_rows[t][:, HALF:])
+        for m0 in (0, P // 2):
+            deal(nc.scalar.copy, w2_raw, w2_dealt[:, 2 * P * PACK :], 2, 2, slice(m0, m0 + P // 2))
 
-        for u in range(2):
-            deal(nc.scalar.copy, w2_raw, w2_dealt[:, 2 * u * P * PACK : 2 * (u + 1) * P * PACK], 2 * u, 2)
+        def take(out, t, s0, n):
+            nc.vector.tensor_tensor(out, h_rows[t][:].indirect(entries(par_sb, s0, n)), share_sb[:, s0 : s0 + n], MULT)
+
+        sum_banks = [next_bank([P, PACK, P]) for b in range(HALF // BLOCK)]
+
+        def take_and_turn(taken, t, s0, n):
+            take(taken, t, s0, n)
+            for b0 in range(0, n, BLOCK):
+                bank = sum_banks[(s0 + b0) // BLOCK]
+                nc.tensor.matmul(bank[:, t, :], h_rows[t][:, s0 + b0 : s0 + b0 + BLOCK], identity[:], start=True, stop=False, is_transpose=True)
+                nc.tensor.matmul(bank[:, t, :], taken[:, b0 : b0 + BLOCK], identity[:], start=False, stop=True, is_transpose=True)
+
+        for t in range(2):
+            wide = keep.tile([P, HALF], F32, name="taken_wide%d" % t)
+            take_and_turn(wide[:], t, 0, HALF)
+        narrow = keep.tile([P, 2, QUARTER], F32, name="taken_narrow", tag="ring", align_bytes=64)
+        for t in range(2, PACK):
+            take_and_turn(narrow[:, t - 2, :], t, 0, QUARTER)
+        taken_last = keep.tile([P, QUARTER], F32, name="taken_last")
+        take_and_turn(taken_last[:], 3, QUARTER, QUARTER)
+        take_and_turn(w2_raw[:, 0, :QUARTER], 2, QUARTER, QUARTER)
         nc.vector.quantize_mx(out=w2_codes[:].bitcast(FP8X4), scales=w2_scales[:], in_=w2_dealt[:])
 
-        y_codes = keep.tile([P, S], U32, name="y_codes", align_bytes=64)
-        y_scales = keep.tile([P, S], U8, name="y_scales", align_bytes=64)
-        y_view = out_0.rearrange("(p t) s -> p t s", t=PACK)
-        words_view = out_1[0].rearrange("p c r -> p (c r)").bitcast(I32)
-        starts = [sum(CHUNKS[:c]) for c in range(len(CHUNKS))]
-        taken, z_woven, y_woven, y_rows = {}, {}, {}, {}
-
-        def gather(c):
-            n = CHUNKS[c]
-            taken[c] = keep.tile([P, PACK, n], F32, name="taken%d" % c, tag=TAKEN_TAGS[c], align_bytes=64)
-            for t in SLOT_ORDER:
-                nc.vector.tensor_tensor(
-                    taken[c][:, t, :], h_rows[t][:].indirect(entries(par_sb, starts[c], n)), share_sb[:, starts[c] : starts[c] + n], MULT
-                )
-
-        def add_turned(c):
-            n = CHUNKS[c]
-            z_woven[c] = keep.tile([P, PACK * n], BF16, name="z_woven%d" % c, tag=WOVEN_TAGS[c], align_bytes=64)
-            pairs = []
-            for b0 in range(0, n, BLOCK):
-                bank = next_bank([P, PACK, P])
-                for t in SLOT_ORDER:
-                    own = h_rows[t][:, starts[c] + b0 : starts[c] + b0 + BLOCK]
-                    nc.tensor.matmul(bank[:, t, :], own, identity[:], start=True, stop=False, is_transpose=True)
-                    nc.tensor.matmul(bank[:, t, :], taken[c][:, t, b0 : b0 + BLOCK], identity[:], start=False, stop=True, is_transpose=True)
-                pair = keep.tile([P, H], BF16, name="pair%d_%d" % (c, b0))
-                nc.scalar.copy(
-                    pair[:].rearrange("s (u p e) -> s u p e", u=2, e=2),
-                    bank[:].rearrange("s (u e) p -> s u p e", e=2),
-                )
-                pairs.append(pair)
-            back = next_bank([P, len(pairs), 2, BLOCK])
-            for b, pair in enumerate(pairs):
-                for u in range(2):
-                    nc.tensor.transpose(back[:, b, u, :], pair[:].bitcast(F32)[:, u * P : (u + 1) * P], identity[:])
+        def round_block(b, pair, back):
             nc.scalar.copy(
-                z_woven[c][:].bitcast(F32).rearrange("p (b s u) -> p b s u", s=BLOCK, u=2),
-                back[:].rearrange("p b u s -> p b s u"),
+                pair.rearrange("s (u p e) -> s u p e", u=2, e=2),
+                sum_banks[b][:].rearrange("s (u e) p -> s u p e", e=2),
+            )
+            for u in range(2):
+                nc.tensor.transpose(back[:, u, :], pair.bitcast(F32)[:, u * P : (u + 1) * P], identity[:])
+
+        def weave_back(back, z_woven):
+            nc.scalar.copy(
+                z_woven.bitcast(F32).rearrange("p (b s u) -> p b s u", s=BLOCK, u=2),
+                back.rearrange("p b u s -> p b s u"),
             )
 
-        def add_direct(c):
-            n = CHUNKS[c]
-            z_woven[c] = keep.tile([P, PACK * n], BF16, name="z_woven%d" % c, tag=WOVEN_TAGS[c], align_bytes=64)
-            own = h_late[:, :, starts[c] - turned : starts[c] - turned + n]
-            nc.vector.tensor_tensor(woven(z_woven[c][:]), planar(taken[c][:]), planar(own), ADD)
+        y_codes = keep.tile([P, S], U32, name="y_codes", align_bytes=64)
+        y_view = out_0.rearrange("(p t) s -> p t s", t=PACK)
+        words_view = out_1[0].rearrange("p c r -> p (c r)").bitcast(I32)
+        y_woven = keep.tile([P, PACK * S], BF16, name="y_woven", align_bytes=64)
+        last_rows = []
+        unwoven = []
 
-        def second_layer(c):
-            n = CHUNKS[c]
-            z_codes = keep.tile([P, n], U32, name="z_codes%d" % c, align_bytes=64)
-            z_scales = keep.tile([P, n], U8, name="z_scales%d" % c, align_bytes=64)
-            nc.vector.quantize_mx(out=z_codes[:].bitcast(FP8X4), scales=z_scales[:], in_=z_woven[c][:])
-            y_rows[c] = keep.tile([P, PACK, n], F32, name="y_rows%d" % c)
-            y_woven[c] = keep.tile([P, PACK * n], BF16, name="y_woven%d" % c, align_bytes=64)
+        def product(bank, t, z_codes, z_scales):
+            w_cols = slice(t * P, (t + 1) * P)
+            nc.tensor.matmul_mx(
+                out=bank,
+                lhsT=w2_codes[:, w_cols].bitcast(FP8X4),
+                lhsT_scale=w2_scales[:, w_cols],
+                rhs=z_codes.bitcast(FP8X4),
+                rhs_scale=z_scales,
+                start=True,
+                stop=True,
+            )
+
+        def second_layer(s0, n, z_woven):
+            z_codes = keep.tile([P, n], U32, name="z_codes%d" % s0, align_bytes=64)
+            z_scales = keep.tile([P, n], U8, name="z_scales%d" % s0, align_bytes=64)
+            nc.vector.quantize_mx(out=z_codes[:].bitcast(FP8X4), scales=z_scales[:], in_=z_woven)
+            y_rows = keep.tile([P, PACK, n], F32, name="y_rows%d" % s0)
             for b0 in range(0, n, BLOCK):
                 block = slice(b0, b0 + BLOCK)
+                y_block = y_woven[:, PACK * (s0 + b0) : PACK * (s0 + b0 + BLOCK)]
+                if s0 + b0 == S - BLOCK:
+                    for u in range(2):
+                        bank = next_bank([P, 2, BLOCK])
+                        for e in range(2):
+                            product(bank[:, e, :], 2 * u + e, z_codes[:, block], z_scales[:, block])
+                        nc.scalar.copy(y_rows[:, 2 * u : 2 * u + 2, :], bank[:])
+                    last_rows.append(y_rows)
+                    continue
                 bank = next_bank([P, PACK, BLOCK])
                 for t in range(PACK):
-                    w_cols = slice(t * P, (t + 1) * P)
-                    nc.tensor.matmul_mx(
-                        out=bank[:, t, :],
-                        lhsT=w2_codes[:, w_cols].bitcast(FP8X4),
-                        lhsT_scale=w2_scales[:, w_cols],
-                        rhs=z_codes[:, block].bitcast(FP8X4),
-                        rhs_scale=z_scales[:, block],
-                        start=True,
-                        stop=True,
-                    )
-                if c not in WOVEN_BY_VECTOR:
-                    nc.scalar.copy(
-                        y_woven[c][:, PACK * b0 : PACK * (b0 + BLOCK)].rearrange("p (s t) -> p s t", t=PACK),
-                        bank[:].rearrange("p t s -> p s t"),
-                    )
-                nc.scalar.copy(y_rows[c][:, :, block], bank[:])
-            nc.sync.dma_start(y_view[:, :, starts[c] : starts[c] + n], y_rows[c][:])
+                    product(bank[:, t, :], t, z_codes[:, block], z_scales[:, block])
+                nc.scalar.copy(y_rows[:, :, block], bank[:])
+                unwoven.append((y_block, bank))
+            queue = nc.scalar if s0 + n == S else nc.sync
+            queue.dma_start(y_view[:, :, s0 : s0 + n], y_rows[:])
 
-        def hand_on(c):
-            cols = slice(starts[c], starts[c] + CHUNKS[c])
-            if c in WOVEN_BY_VECTOR:
-                nc.vector.tensor_copy(woven(y_woven[c][:]), planar(y_rows[c][:]))
-            nc.vector.quantize_mx(out=y_codes[:, cols].bitcast(FP8X4), scales=y_scales[:, cols], in_=y_woven[c][:])
-            nc.sync.dma_start(words_view[:, cols], y_codes[:, cols].bitcast(I32))
+        def weave_waiting():
+            for y_block, bank in unwoven:
+                nc.scalar.copy(y_block.rearrange("p (s t) -> p s t", t=PACK), bank[:].rearrange("p t s -> p s t"))
+            unwoven.clear()
 
-        gather(0)
-        gather(1)
-        add_turned(0)
-        add_turned(1)
-        gather(2)
-        second_layer(0)
-        add_direct(2)
-        second_layer(1)
-        second_layer(2)
-        gather(3)
-        add_direct(3)
-        second_layer(3)
-        gather(4)
-        add_direct(4)
-        second_layer(4)
-        hand_on(0)
-        hand_on(1)
-        hand_on(2)
-        hand_on(3)
-        hand_on(4)
+        def hand_on(s0, n):
+            cols = slice(s0, s0 + n)
+            nc.vector.quantize_mx(out=y_codes[:, cols].bitcast(FP8X4), scales=y_scales[:, cols], in_=y_woven[:, PACK * s0 : PACK * (s0 + n)])
+
+        def store_words(s0, n):
+            nc.sync.dma_start(words_view[:, s0 : s0 + n], y_codes[:, s0 : s0 + n].bitcast(I32))
+
+        def take_all(ring, s0, n):
+            for t in range(PACK):
+                take(ring[:, t * n : (t + 1) * n], t, s0, n)
+
+        def add_direct(ring, s0, n, z_woven):
+            taken = ring[:].rearrange("p (t s) -> p t s", t=PACK)
+            nc.vector.tensor_tensor(woven(z_woven), planar(taken), planar(h_late[:, :, s0 - HALF : s0 - HALF + n]), ADD)
+
+        ring = keep.tile([P, PACK * QUARTER], F32, name="ring0", tag="ring", align_bytes=64)
+        z_first = ring[:, HALF:].bitcast(BF16)
+        pair_tiles = [keep.tile([P, H], BF16, name="pair%d" % b) for b in range(3)]
+        pairs = [pair_tiles[b][:] for b in (0, 1, 2, 1)]
+        z_second = keep.tile([P, PACK * QUARTER], BF16, name="z_second", tag="z", align_bytes=64)
+        back_first = next_bank([P, 2, 2, BLOCK])
+        backs = [next_bank([P, 1, 2, BLOCK]) for b in range(2)]
+        round_block(0, pairs[0], back_first[:, 0])
+        round_block(1, pairs[1], back_first[:, 1])
+        round_block(2, pairs[2], backs[0][:, 0])
+        weave_back(back_first[:], z_first)
+        round_block(3, pairs[3], backs[1][:, 0])
+        for b in range(2):
+            weave_back(backs[b][:], z_second[:, b * H : (b + 1) * H])
+        second_layer(0, QUARTER, z_first)
+        weave_waiting()
+        take_all(ring, HALF, QUARTER)
+        second_layer(QUARTER, QUARTER, z_second[:])
+        weave_waiting()
+        z_third = keep.tile([P, PACK * QUARTER], BF16, name="z_third", tag="z", align_bytes=64)
+        add_direct(ring, HALF, QUARTER, z_third[:])
+        second_layer(HALF, QUARTER, z_third[:])
+        for s0 in (S - QUARTER, S - BLOCK):
+            ring = keep.tile([P, PACK * BLOCK], F32, name="ring%d" % s0, tag="ring", align_bytes=64)
+            z_woven = keep.tile([P, PACK * BLOCK], BF16, name="z_woven%d" % s0, tag="z_woven%d" % s0, align_bytes=64)
+            take_all(ring, s0, BLOCK)
+            add_direct(ring, s0, BLOCK, z_woven[:])
+            second_layer(s0, BLOCK, z_woven[:])
+            weave_waiting()
+        y_scales = keep.tile([P, S], U8, name="y_scales", tag="ring", align_bytes=64)
+        hand_on(0, HALF)
+        store_words(0, HALF)
+        hand_on(HALF, QUARTER)
+        hand_on(S - QUARTER, BLOCK)
+        store_words(HALF, QUARTER + BLOCK)
+        nc.vector.tensor_copy(woven(y_woven[:, PACK * (S - BLOCK) :]), planar(last_rows[0][:]))
+        hand_on(S - BLOCK, BLOCK)
+        store_words(S - BLOCK, BLOCK)
 
         scales_view = out_2[0].bitcast(I32)
         for q in range(4):

@@ -25,6 +25,7 @@ HALF = 512
 QUARTER = 256
 BLOCK = 128
 BANKS = 8
+FIRST_SPLIT = 640
 LAST_SPLIT = 384
 
 
@@ -48,78 +49,97 @@ def tile_picked_treeup_relu_lo_kernel(tc, xT, w1, w2, share, offs, par, out_0, o
 
         offs_sb = keep.tile([P, S // LIST_COL], U16, name="offs_sb")
         par_sb = keep.tile([P, S // LIST_COL], U16, name="par_sb")
-        w1_raw = keep.tile([P, PACK, H], F32, name="w1_raw")
-        w2_raw = keep.tile([P, PACK, H], F32, name="w2_raw")
+        w1_raw = [keep.tile([P, PACK, QUARTER], F32, name="w1_raw%d" % u) for u in range(2)]
+        w2_early = keep.tile([P, PACK, BLOCK], F32, name="w2_early")
+        w2_late = keep.tile([P, PACK * (H - BLOCK)], F32, name="w2_late", align_bytes=64)
+        w2_rest = w2_late[:].rearrange("p (j c) -> p j c", j=PACK)
         share_sb = keep.tile([P, S], F32, name="share_sb")
 
         x_view = xT.rearrange("(p u e) s -> u p e s", u=2, e=2)
-        x_pieces = [(0, 0, 2 * HALF), (0, 2 * HALF, 2 * HALF)] + [(1, c0, HALF) for c0 in range(0, T, HALF)]
+        x_pieces = [(0, 0, 2 * HALF), (0, 2 * HALF, 2 * HALF), (1, 0, 2 * HALF), (1, 2 * HALF, HALF), (1, 3 * HALF, HALF)]
         x_raw = [keep.tile([P, 2, n], F32, name="x_raw%d" % k) for k, (u, c0, n) in enumerate(x_pieces)]
         nc.sync.dma_start(offs_sb[:], offs)
         for k, (u, c0, n) in enumerate(x_pieces):
             nc.sync.dma_start(x_raw[k][:], x_view[u][:, :, c0 : c0 + n])
-        nc.sync.dma_start(w1_raw[:], w1.rearrange("(p j) c -> p j c", j=PACK))
-        nc.sync.dma_start(w2_raw[:], w2.rearrange("(p j) c -> p j c", j=PACK))
+        w1_view = w1.rearrange("(p j) c -> p j c", j=PACK)
+        for u in range(2):
+            nc.sync.dma_start(w1_raw[u][:], w1_view[:, :, u * QUARTER : (u + 1) * QUARTER])
+        w2_view = w2.rearrange("(p j) c -> p j c", j=PACK)
+        nc.sync.dma_start(w2_early[:], w2_view[:, :, :BLOCK])
         nc.sync.dma_start(par_sb[:], par)
         nc.sync.dma_start(share_sb[:], share)
+        nc.sync.dma_start(w2_rest, w2_view[:, :, BLOCK:])
 
         x_pairs = [keep.tile([P, 2 * T], BF16, name="x_pairs%d" % u, align_bytes=64) for u in range(2)]
 
         def pair_up(copy, k, lo, hi):
             u, c0, n = x_pieces[k]
             copy(
-                x_pairs[u][:, 2 * (c0 + lo) : 2 * (c0 + hi)].rearrange("p (s e) -> p s e", e=2),
-                x_raw[k][:, :, lo:hi].rearrange("p e s -> p s e"),
+                x_pairs[u][:, 2 * (c0 + lo) : 2 * (c0 + hi)].rearrange("p (c i e) -> p c e i", i=4, e=2),
+                x_raw[k][:, :, lo:hi].rearrange("p e (c i) -> p c e i", i=4),
             )
 
         node_parts = [(0, HALF), (HALF, QUARTER), (HALF + QUARTER, QUARTER)]
-        x_woven = [keep.tile([P, PACK * n], BF16, name="x_woven%d" % q, align_bytes=64) for q, (s0, n) in enumerate(node_parts)]
+        x_woven = [keep.tile([P, PACK * n], BF16, name="x_woven%d" % q, align_bytes=64)[:] for q, (s0, n) in enumerate(node_parts)]
+
+        picked = [keep.tile([P, 2, QUARTER], U32, name="picked%d" % r) for r in range(S // QUARTER)]
 
         def pick(u):
-            for q, (s0, n) in enumerate(node_parts):
-                words = x_woven[q][:].bitcast(U32).rearrange("p (s u) -> p s u", u=2)
-                nc.vector.tensor_copy(words[:, :, u], x_pairs[u][:].bitcast(U32).indirect(entries(offs_sb, s0, n)))
+            for r in range(S // QUARTER):
+                nc.vector.tensor_copy(picked[r][:, u, :], x_pairs[u][:].bitcast(U32).indirect(entries(offs_sb, r * QUARTER, QUARTER)))
 
-        pair_up(lambda out, in_: nc.scalar.activation(out, in_, COPY), 0, 0, 2 * HALF)
-        pair_up(nc.vector.tensor_copy, 1, 0, 2 * HALF)
-        pick(0)
-        for k in range(2, 5):
-            pair_up(nc.scalar.copy, k, 0, HALF)
-        pair_up(nc.vector.tensor_copy, 5, 0, LAST_SPLIT)
-        pair_up(nc.scalar.copy, 5, LAST_SPLIT, HALF)
-        pick(1)
-
-        def deal(engine_copy, raw, dealt, t0, nt, rows=slice(0, P)):
-            engine_copy(
-                dealt.rearrange("p (t m j) -> p m j t", t=nt, j=PACK)[:, rows],
-                raw[:].rearrange("p j (m t) -> p m j t", t=PACK)[:, rows, :, t0 : t0 + nt],
+        def weave_words(copy, dtype, q, lo, n):
+            s0 = node_parts[q][0] + lo
+            copy(
+                x_woven[q].bitcast(dtype)[:, 2 * lo : 2 * (lo + n)].rearrange("p (c i u) -> p c u i", i=4, u=2),
+                picked[s0 // QUARTER][:].bitcast(dtype).rearrange("p u (c i) -> p c u i", i=4),
             )
 
-        w2_dealt = keep.tile([P, H * PACK], BF16, name="w2_dealt", align_bytes=64)
+        pair_up(lambda out, in_: nc.scalar.activation(out, in_, COPY), 0, 0, 2 * HALF)
+        pair_up(nc.vector.tensor_copy, 1, 0, FIRST_SPLIT)
+        pair_up(nc.scalar.copy, 1, FIRST_SPLIT, 2 * HALF)
+        pick(0)
+        pair_up(nc.scalar.copy, 2, 0, 2 * HALF)
+        pair_up(nc.vector.tensor_copy, 3, 0, HALF)
+        pair_up(nc.vector.tensor_copy, 4, 0, LAST_SPLIT)
+        pair_up(nc.scalar.copy, 4, LAST_SPLIT, HALF)
+        pick(1)
+        for lo in (0, QUARTER):
+            weave_words(nc.scalar.copy, U32, 0, lo, QUARTER)
+        weave_words(nc.vector.tensor_copy, I32, 1, 0, QUARTER)
+
+        def deal(engine_copy, raw, dealt, t0, nt, m0=0):
+            columns = raw.rearrange("p j (m t) -> p m j t", t=PACK)[:, :, :, t0 : t0 + nt]
+            engine_copy(dealt.rearrange("p (t m j) -> p m j t", t=nt, j=PACK)[:, m0 : m0 + columns.shape[1]], columns)
+
         w1_first = keep.tile([P, 2 * P * PACK], BF16, name="w1_first", tag="w1_dealt0", align_bytes=64)
-        w1_dealt = [w1_first[:], w2_dealt[:, 2 * P * PACK :]]
+        w1_dealt = [w1_first[:], x_woven[1]]
         w1_codes = [keep.tile([P, 2 * P], U32, name="w1_codes%d" % u, tag="w1_codes%d" % u, align_bytes=64) for u in range(2)]
         w1_scales = [keep.tile([P, 2 * P], U8, name="w1_scales%d" % u, align_bytes=64) for u in range(2)]
         x_codes = keep.tile([P, S], U32, name="x_codes", align_bytes=64)
         x_scales = [keep.tile([P, HALF], U8, name="x_scales0", align_bytes=64)]
         for u in range(2):
-            deal(nc.scalar.copy, w1_raw, w1_dealt[u], 2 * u, 2)
-        nc.vector.quantize_mx(out=x_codes[:, :HALF].bitcast(FP8X4), scales=x_scales[0][:], in_=x_woven[0][:])
+            deal(nc.scalar.copy, w1_raw[u][:], w1_dealt[0], 0, 2, u * QUARTER // PACK)
+        weave_words(nc.scalar.copy, U32, 2, 0, QUARTER)
+        nc.vector.quantize_mx(out=x_codes[:, :HALF].bitcast(FP8X4), scales=x_scales[0][:], in_=x_woven[0])
         nc.vector.quantize_mx(out=w1_codes[0][:].bitcast(FP8X4), scales=w1_scales[0][:], in_=w1_dealt[0])
         x_scales.append(keep.tile([P, HALF], U8, name="x_scales1", tag="w1_dealt0", align_bytes=64))
         for q in (1, 2):
             s0, n = node_parts[q]
-            nc.vector.quantize_mx(out=x_codes[:, s0 : s0 + n].bitcast(FP8X4), scales=x_scales[1][:, s0 - HALF : s0 - HALF + n], in_=x_woven[q][:])
+            nc.vector.quantize_mx(out=x_codes[:, s0 : s0 + n].bitcast(FP8X4), scales=x_scales[1][:, s0 - HALF : s0 - HALF + n], in_=x_woven[q])
+        for u in range(2):
+            deal(nc.vector.tensor_copy, w1_raw[u][:], w1_dealt[1], 2, 2, u * QUARTER // PACK)
         nc.vector.quantize_mx(out=w1_codes[1][:].bitcast(FP8X4), scales=w1_scales[1][:], in_=w1_dealt[1])
 
         identity = keep.tile([P, P], F32, name="identity")
         make_identity(nc, identity[:])
 
+        w2_dealt = keep.tile([P, H * PACK], BF16, name="w2_dealt", align_bytes=64)
+        deal(nc.scalar.copy, w2_early[:], w2_dealt[:], 0, PACK)
         w2_codes = keep.tile([P, H], U32, name="w2_codes", align_bytes=64)
         w2_scales = keep.tile([P, H], U8, name="w2_scales", align_bytes=64)
-        deal(nc.vector.tensor_copy, w2_raw, w2_dealt[:, : 2 * P * PACK], 0, 2)
 
-        bank_turn = [k % BANKS for k in range(4 * BANKS)]
+        bank_turn = [0, 1, 2, 3, 1, 4, 5, 6, 7, 0] + 2 * [2, 3, 1, 4, 5, 6, 7, 0]
 
         def next_bank(shape):
             return psum.tile(shape, F32, name="bank", tag="bank%d" % bank_turn.pop(0))
@@ -128,7 +148,7 @@ def tile_picked_treeup_relu_lo_kernel(tc, xT, w1, w2, share, offs, par, out_0, o
         h_late = keep.tile([P, PACK, HALF], F32, name="h_late")
         for t in range(PACK):
             w_cols = slice((t % 2) * P, (t % 2 + 1) * P)
-            for s0, n in node_parts if t == 0 else [(0, HALF), (HALF, HALF)]:
+            for s0, n in [(s0, QUARTER) for s0 in range(0, S, QUARTER)] if t == 0 else [(0, HALF), (HALF, HALF)]:
                 cols = slice(s0, s0 + n)
                 bank = next_bank([P, n])
                 nc.tensor.matmul_mx(
@@ -142,8 +162,8 @@ def tile_picked_treeup_relu_lo_kernel(tc, xT, w1, w2, share, offs, par, out_0, o
                 )
                 nc.scalar.activation(h_rows[t][:, cols], bank[:], RELU)
             nc.sync.dma_start(h_late[:, t, :], h_rows[t][:, HALF:])
-        for m0 in (0, P // 2):
-            deal(nc.scalar.copy, w2_raw, w2_dealt[:, 2 * P * PACK :], 2, 2, slice(m0, m0 + P // 2))
+        deal(nc.scalar.copy, w2_rest[:, :, :QUARTER], w2_dealt[:], 0, PACK, BLOCK // PACK)
+        deal(nc.scalar.copy, w2_rest[:, :, QUARTER:], w2_dealt[:], 0, PACK, (BLOCK + QUARTER) // PACK)
 
         def take(out, t, s0, n):
             nc.vector.tensor_tensor(out, h_rows[t][:].indirect(entries(par_sb, s0, n)), share_sb[:, s0 : s0 + n], MULT)
@@ -160,12 +180,12 @@ def tile_picked_treeup_relu_lo_kernel(tc, xT, w1, w2, share, offs, par, out_0, o
         for t in range(2):
             wide = keep.tile([P, HALF], F32, name="taken_wide%d" % t)
             take_and_turn(wide[:], t, 0, HALF)
-        narrow = keep.tile([P, 2, QUARTER], F32, name="taken_narrow", tag="ring", align_bytes=64)
+        narrow = keep.tile([P, 2, QUARTER], F32, name="taken_narrow")
         for t in range(2, PACK):
             take_and_turn(narrow[:, t - 2, :], t, 0, QUARTER)
         taken_last = keep.tile([P, QUARTER], F32, name="taken_last")
         take_and_turn(taken_last[:], 3, QUARTER, QUARTER)
-        take_and_turn(w2_raw[:, 0, :QUARTER], 2, QUARTER, QUARTER)
+        take_and_turn(w2_late[:, :QUARTER], 2, QUARTER, QUARTER)
         nc.vector.quantize_mx(out=w2_codes[:].bitcast(FP8X4), scales=w2_scales[:], in_=w2_dealt[:])
 
         def round_block(b, pair, back):
@@ -242,10 +262,10 @@ def tile_picked_treeup_relu_lo_kernel(tc, xT, w1, w2, share, offs, par, out_0, o
                 take(ring[:, t * n : (t + 1) * n], t, s0, n)
 
         def add_direct(ring, s0, n, z_woven):
-            taken = ring[:].rearrange("p (t s) -> p t s", t=PACK)
+            taken = ring.rearrange("p (t s) -> p t s", t=PACK)
             nc.vector.tensor_tensor(woven(z_woven), planar(taken), planar(h_late[:, :, s0 - HALF : s0 - HALF + n]), ADD)
 
-        ring = keep.tile([P, PACK * QUARTER], F32, name="ring0", tag="ring", align_bytes=64)
+        ring = w2_late[:, H - BLOCK : H - BLOCK + PACK * QUARTER]
         z_first = ring[:, HALF:].bitcast(BF16)
         pair_tiles = [keep.tile([P, H], BF16, name="pair%d" % b) for b in range(3)]
         pairs = [pair_tiles[b][:] for b in (0, 1, 2, 1)]
@@ -268,13 +288,12 @@ def tile_picked_treeup_relu_lo_kernel(tc, xT, w1, w2, share, offs, par, out_0, o
         add_direct(ring, HALF, QUARTER, z_third[:])
         second_layer(HALF, QUARTER, z_third[:])
         for s0 in (S - QUARTER, S - BLOCK):
-            ring = keep.tile([P, PACK * BLOCK], F32, name="ring%d" % s0, tag="ring", align_bytes=64)
             z_woven = keep.tile([P, PACK * BLOCK], BF16, name="z_woven%d" % s0, tag="z_woven%d" % s0, align_bytes=64)
-            take_all(ring, s0, BLOCK)
-            add_direct(ring, s0, BLOCK, z_woven[:])
+            take_all(ring[:, : PACK * BLOCK], s0, BLOCK)
+            add_direct(ring[:, : PACK * BLOCK], s0, BLOCK, z_woven[:])
             second_layer(s0, BLOCK, z_woven[:])
             weave_waiting()
-        y_scales = keep.tile([P, S], U8, name="y_scales", tag="ring", align_bytes=64)
+        y_scales = keep.tile([P, S], U8, name="y_scales", tag="z_woven%d" % (S - BLOCK), align_bytes=64)
         hand_on(0, HALF)
         store_words(0, HALF)
         hand_on(HALF, QUARTER)

@@ -24,7 +24,6 @@ LIST_COL = 16
 HALF = 512
 QUARTER = 256
 BLOCK = 128
-BANKS = 8
 FIRST_SPLIT = 640
 LAST_SPLIT = 384
 
@@ -49,10 +48,8 @@ def tile_picked_treeup_relu_lo_kernel(tc, xT, w1, w2, share, offs, par, out_0, o
 
         offs_sb = keep.tile([P, S // LIST_COL], U16, name="offs_sb")
         par_sb = keep.tile([P, S // LIST_COL], U16, name="par_sb")
-        w1_raw = [keep.tile([P, PACK, QUARTER], F32, name="w1_raw%d" % u) for u in range(2)]
-        w2_early = keep.tile([P, PACK, BLOCK], F32, name="w2_early")
-        w2_late = keep.tile([P, PACK * (H - BLOCK)], F32, name="w2_late", align_bytes=64)
-        w2_rest = w2_late[:].rearrange("p (j c) -> p j c", j=PACK)
+        w1_raw = keep.tile([P, PACK, H], F32, name="w1_raw")
+        w2_early = keep.tile([P, PACK, QUARTER], F32, name="w2_early")
         share_sb = keep.tile([P, S], F32, name="share_sb")
 
         x_view = xT.rearrange("(p u e) s -> u p e s", u=2, e=2)
@@ -61,14 +58,11 @@ def tile_picked_treeup_relu_lo_kernel(tc, xT, w1, w2, share, offs, par, out_0, o
         nc.sync.dma_start(offs_sb[:], offs)
         for k, (u, c0, n) in enumerate(x_pieces):
             nc.sync.dma_start(x_raw[k][:], x_view[u][:, :, c0 : c0 + n])
-        w1_view = w1.rearrange("(p j) c -> p j c", j=PACK)
-        for u in range(2):
-            nc.sync.dma_start(w1_raw[u][:], w1_view[:, :, u * QUARTER : (u + 1) * QUARTER])
-        w2_view = w2.rearrange("(p j) c -> p j c", j=PACK)
-        nc.sync.dma_start(w2_early[:], w2_view[:, :, :BLOCK])
+        nc.sync.dma_start(w1_raw[:], w1.rearrange("(p j) c -> p j c", j=PACK))
         nc.sync.dma_start(par_sb[:], par)
         nc.sync.dma_start(share_sb[:], share)
-        nc.sync.dma_start(w2_rest, w2_view[:, :, BLOCK:])
+        w2_view = w2.rearrange("(p j) c -> p j c", j=PACK)
+        nc.sync.dma_start(w2_early[:], w2_view[:, :, QUARTER:])
 
         x_pairs = [keep.tile([P, 2 * T], BF16, name="x_pairs%d" % u, align_bytes=64) for u in range(2)]
 
@@ -106,36 +100,34 @@ def tile_picked_treeup_relu_lo_kernel(tc, xT, w1, w2, share, offs, par, out_0, o
         pick(1)
         for lo in (0, QUARTER):
             weave_words(nc.scalar.copy, U32, 0, lo, QUARTER)
-        weave_words(nc.vector.tensor_copy, I32, 1, 0, QUARTER)
+        for q in (1, 2):
+            weave_words(nc.scalar.copy, U32, q, 0, QUARTER)
 
         def deal(engine_copy, raw, dealt, t0, nt, m0=0):
             columns = raw.rearrange("p j (m t) -> p m j t", t=PACK)[:, :, :, t0 : t0 + nt]
             engine_copy(dealt.rearrange("p (t m j) -> p m j t", t=nt, j=PACK)[:, m0 : m0 + columns.shape[1]], columns)
 
-        w1_first = keep.tile([P, 2 * P * PACK], BF16, name="w1_first", tag="w1_dealt0", align_bytes=64)
-        w1_dealt = [w1_first[:], x_woven[1]]
-        w1_codes = [keep.tile([P, 2 * P], U32, name="w1_codes%d" % u, tag="w1_codes%d" % u, align_bytes=64) for u in range(2)]
+        w1_dealt = [keep.tile([P, 2 * P * PACK], BF16, name="w1_dealt%d" % u, tag="w1_dealt%d" % u, align_bytes=64) for u in range(2)]
+        w1_codes = [keep.tile([P, 2 * P], U32, name="w1_codes%d" % u, align_bytes=64) for u in range(2)]
         w1_scales = [keep.tile([P, 2 * P], U8, name="w1_scales%d" % u, align_bytes=64) for u in range(2)]
         x_codes = keep.tile([P, S], U32, name="x_codes", align_bytes=64)
-        x_scales = [keep.tile([P, HALF], U8, name="x_scales0", align_bytes=64)]
-        for u in range(2):
-            deal(nc.scalar.copy, w1_raw[u][:], w1_dealt[0], 0, 2, u * QUARTER // PACK)
-        weave_words(nc.scalar.copy, U32, 2, 0, QUARTER)
+        x_scales = [keep.tile([P, HALF], U8, name="x_scales%d" % u, align_bytes=64) for u in range(2)]
+        deal(nc.vector.tensor_copy, w1_raw[:], w1_dealt[0][:], 0, 2)
+        deal(nc.scalar.copy, w1_raw[:], w1_dealt[1][:], 2, 2)
         nc.vector.quantize_mx(out=x_codes[:, :HALF].bitcast(FP8X4), scales=x_scales[0][:], in_=x_woven[0])
-        nc.vector.quantize_mx(out=w1_codes[0][:].bitcast(FP8X4), scales=w1_scales[0][:], in_=w1_dealt[0])
-        x_scales.append(keep.tile([P, HALF], U8, name="x_scales1", tag="w1_dealt0", align_bytes=64))
+        nc.vector.quantize_mx(out=w1_codes[0][:].bitcast(FP8X4), scales=w1_scales[0][:], in_=w1_dealt[0][:])
         for q in (1, 2):
             s0, n = node_parts[q]
             nc.vector.quantize_mx(out=x_codes[:, s0 : s0 + n].bitcast(FP8X4), scales=x_scales[1][:, s0 - HALF : s0 - HALF + n], in_=x_woven[q])
-        for u in range(2):
-            deal(nc.vector.tensor_copy, w1_raw[u][:], w1_dealt[1], 2, 2, u * QUARTER // PACK)
-        nc.vector.quantize_mx(out=w1_codes[1][:].bitcast(FP8X4), scales=w1_scales[1][:], in_=w1_dealt[1])
+        nc.vector.quantize_mx(out=w1_codes[1][:].bitcast(FP8X4), scales=w1_scales[1][:], in_=w1_dealt[1][:])
 
         identity = keep.tile([P, P], F32, name="identity")
         make_identity(nc, identity[:])
 
         w2_dealt = keep.tile([P, H * PACK], BF16, name="w2_dealt", align_bytes=64)
-        deal(nc.scalar.copy, w2_early[:], w2_dealt[:], 0, PACK)
+        deal(nc.vector.tensor_copy, w2_early[:], w2_dealt[:], 0, PACK, QUARTER // PACK)
+        w2_late = keep.tile([P, PACK, QUARTER], F32, name="w2_late", tag="w1_dealt0", align_bytes=64)
+        nc.sync.dma_start(w2_late[:], w2_view[:, :, :QUARTER])
         w2_codes = keep.tile([P, H], U32, name="w2_codes", align_bytes=64)
         w2_scales = keep.tile([P, H], U8, name="w2_scales", align_bytes=64)
 
@@ -162,8 +154,7 @@ def tile_picked_treeup_relu_lo_kernel(tc, xT, w1, w2, share, offs, par, out_0, o
                 )
                 nc.scalar.activation(h_rows[t][:, cols], bank[:], RELU)
             nc.sync.dma_start(h_late[:, t, :], h_rows[t][:, HALF:])
-        deal(nc.scalar.copy, w2_rest[:, :, :QUARTER], w2_dealt[:], 0, PACK, BLOCK // PACK)
-        deal(nc.scalar.copy, w2_rest[:, :, QUARTER:], w2_dealt[:], 0, PACK, (BLOCK + QUARTER) // PACK)
+        deal(nc.scalar.copy, w2_late[:], w2_dealt[:], 0, PACK)
 
         def take(out, t, s0, n):
             nc.vector.tensor_tensor(out, h_rows[t][:].indirect(entries(par_sb, s0, n)), share_sb[:, s0 : s0 + n], MULT)
@@ -185,7 +176,7 @@ def tile_picked_treeup_relu_lo_kernel(tc, xT, w1, w2, share, offs, par, out_0, o
             take_and_turn(narrow[:, t - 2, :], t, 0, QUARTER)
         taken_last = keep.tile([P, QUARTER], F32, name="taken_last")
         take_and_turn(taken_last[:], 3, QUARTER, QUARTER)
-        take_and_turn(w2_late[:, :QUARTER], 2, QUARTER, QUARTER)
+        take_and_turn(w2_late[:, PACK - 1, :], 2, QUARTER, QUARTER)
         nc.vector.quantize_mx(out=w2_codes[:].bitcast(FP8X4), scales=w2_scales[:], in_=w2_dealt[:])
 
         def round_block(b, pair, back):
@@ -206,7 +197,6 @@ def tile_picked_treeup_relu_lo_kernel(tc, xT, w1, w2, share, offs, par, out_0, o
         y_view = out_0.rearrange("(p t) s -> p t s", t=PACK)
         words_view = out_1[0].rearrange("p c r -> p (c r)").bitcast(I32)
         y_woven = keep.tile([P, PACK * S], BF16, name="y_woven", align_bytes=64)
-        last_rows = []
         unwoven = []
 
         def product(bank, t, z_codes, z_scales):
@@ -221,11 +211,10 @@ def tile_picked_treeup_relu_lo_kernel(tc, xT, w1, w2, share, offs, par, out_0, o
                 stop=True,
             )
 
-        def second_layer(s0, n, z_woven):
+        def second_layer(s0, n, z_woven, y_rows):
             z_codes = keep.tile([P, n], U32, name="z_codes%d" % s0, align_bytes=64)
             z_scales = keep.tile([P, n], U8, name="z_scales%d" % s0, align_bytes=64)
             nc.vector.quantize_mx(out=z_codes[:].bitcast(FP8X4), scales=z_scales[:], in_=z_woven)
-            y_rows = keep.tile([P, PACK, n], F32, name="y_rows%d" % s0)
             for b0 in range(0, n, BLOCK):
                 block = slice(b0, b0 + BLOCK)
                 y_block = y_woven[:, PACK * (s0 + b0) : PACK * (s0 + b0 + BLOCK)]
@@ -235,20 +224,17 @@ def tile_picked_treeup_relu_lo_kernel(tc, xT, w1, w2, share, offs, par, out_0, o
                         for e in range(2):
                             product(bank[:, e, :], 2 * u + e, z_codes[:, block], z_scales[:, block])
                         nc.scalar.copy(y_rows[:, 2 * u : 2 * u + 2, :], bank[:])
-                    last_rows.append(y_rows)
                     continue
                 bank = next_bank([P, PACK, BLOCK])
                 for t in range(PACK):
                     product(bank[:, t, :], t, z_codes[:, block], z_scales[:, block])
                 nc.scalar.copy(y_rows[:, :, block], bank[:])
                 unwoven.append((y_block, bank))
-            queue = nc.scalar if s0 + n == S else nc.sync
-            queue.dma_start(y_view[:, :, s0 : s0 + n], y_rows[:])
 
-        def weave_waiting():
-            for y_block, bank in unwoven:
+        def weave_waiting(count):
+            for b in range(count):
+                y_block, bank = unwoven.pop(0)
                 nc.scalar.copy(y_block.rearrange("p (s t) -> p s t", t=PACK), bank[:].rearrange("p t s -> p s t"))
-            unwoven.clear()
 
         def hand_on(s0, n):
             cols = slice(s0, s0 + n)
@@ -259,49 +245,56 @@ def tile_picked_treeup_relu_lo_kernel(tc, xT, w1, w2, share, offs, par, out_0, o
 
         def take_all(ring, s0, n):
             for t in range(PACK):
-                take(ring[:, t * n : (t + 1) * n], t, s0, n)
+                take(ring[:, t, :], t, s0, n)
 
         def add_direct(ring, s0, n, z_woven):
-            taken = ring.rearrange("p (t s) -> p t s", t=PACK)
-            nc.vector.tensor_tensor(woven(z_woven), planar(taken), planar(h_late[:, :, s0 - HALF : s0 - HALF + n]), ADD)
+            nc.vector.tensor_tensor(woven(z_woven), planar(ring), planar(h_late[:, :, s0 - HALF : s0 - HALF + n]), ADD)
 
-        ring = w2_late[:, H - BLOCK : H - BLOCK + PACK * QUARTER]
-        z_first = ring[:, HALF:].bitcast(BF16)
-        pair_tiles = [keep.tile([P, H], BF16, name="pair%d" % b) for b in range(3)]
+        y_tiles = [keep.tile([P, PACK, n], F32, name="y_rows%d" % c) for c, n in enumerate((QUARTER, QUARTER, QUARTER, BLOCK, BLOCK))]
+        z_first = keep.tile([P, PACK * QUARTER], BF16, name="z_first", align_bytes=64)
+        z_second = keep.tile([P, PACK * QUARTER], BF16, name="z_second", align_bytes=64)
+        pair_tiles = [keep.tile([P, H], BF16, name="pair%d" % b, tag="pair%d" % b) for b in range(3)]
         pairs = [pair_tiles[b][:] for b in (0, 1, 2, 1)]
-        z_second = keep.tile([P, PACK * QUARTER], BF16, name="z_second", tag="z", align_bytes=64)
         back_first = next_bank([P, 2, 2, BLOCK])
         backs = [next_bank([P, 1, 2, BLOCK]) for b in range(2)]
         round_block(0, pairs[0], back_first[:, 0])
         round_block(1, pairs[1], back_first[:, 1])
         round_block(2, pairs[2], backs[0][:, 0])
-        weave_back(back_first[:], z_first)
+        weave_back(back_first[:], z_first[:])
         round_block(3, pairs[3], backs[1][:, 0])
         for b in range(2):
             weave_back(backs[b][:], z_second[:, b * H : (b + 1) * H])
-        second_layer(0, QUARTER, z_first)
-        weave_waiting()
-        take_all(ring, HALF, QUARTER)
-        second_layer(QUARTER, QUARTER, z_second[:])
-        weave_waiting()
-        z_third = keep.tile([P, PACK * QUARTER], BF16, name="z_third", tag="z", align_bytes=64)
-        add_direct(ring, HALF, QUARTER, z_third[:])
-        second_layer(HALF, QUARTER, z_third[:])
-        for s0 in (S - QUARTER, S - BLOCK):
-            z_woven = keep.tile([P, PACK * BLOCK], BF16, name="z_woven%d" % s0, tag="z_woven%d" % s0, align_bytes=64)
-            take_all(ring[:, : PACK * BLOCK], s0, BLOCK)
-            add_direct(ring[:, : PACK * BLOCK], s0, BLOCK, z_woven[:])
-            second_layer(s0, BLOCK, z_woven[:])
-            weave_waiting()
-        y_scales = keep.tile([P, S], U8, name="y_scales", tag="z_woven%d" % (S - BLOCK), align_bytes=64)
-        hand_on(0, HALF)
-        store_words(0, HALF)
+        for c, z_turned in enumerate((z_first, z_second)):
+            second_layer(c * QUARTER, QUARTER, z_turned[:], y_tiles[c][:])
+            nc.sync.dma_start(y_view[:, :, c * QUARTER : (c + 1) * QUARTER], y_tiles[c][:])
+            weave_waiting(2)
+        ring_odd = keep.tile([P, PACK, BLOCK], F32, name="ring_odd", tag="pair1")
+        rings = [w2_late[:, :, :BLOCK], ring_odd[:]]
+        z_late = keep.tile([P, PACK * 3 * BLOCK], BF16, name="z_late", align_bytes=64)
+        for b in range(HALF // BLOCK):
+            s0 = HALF + b * BLOCK
+            z_woven = z_first[:, :H] if b == 0 else z_late[:, (b - 1) * H : b * H]
+            take_all(rings[b % 2], s0, BLOCK)
+            add_direct(rings[b % 2], s0, BLOCK, z_woven)
+            if b < 2:
+                second_layer(s0, BLOCK, z_woven, y_tiles[2][:, :, b * BLOCK : (b + 1) * BLOCK])
+            else:
+                second_layer(s0, BLOCK, z_woven, y_tiles[b + 1][:])
+            if b == 1:
+                nc.sync.dma_start(y_view[:, :, HALF : HALF + QUARTER], y_tiles[2][:])
+                weave_waiting(2)
+            if b >= 2:
+                nc.scalar.dma_start(y_view[:, :, s0 : s0 + BLOCK], y_tiles[b + 1][:])
+        y_scales = keep.tile([P, S], U8, name="y_scales", align_bytes=64)
+        hand_on(0, QUARTER)
+        hand_on(QUARTER, QUARTER)
         hand_on(HALF, QUARTER)
+        store_words(0, S - QUARTER)
+        nc.vector.tensor_copy(woven(y_woven[:, PACK * (S - QUARTER) : PACK * (S - BLOCK)]), planar(y_tiles[-2][:]))
         hand_on(S - QUARTER, BLOCK)
-        store_words(HALF, QUARTER + BLOCK)
-        nc.vector.tensor_copy(woven(y_woven[:, PACK * (S - BLOCK) :]), planar(last_rows[0][:]))
+        nc.vector.tensor_copy(woven(y_woven[:, PACK * (S - BLOCK) :]), planar(y_tiles[-1][:]))
         hand_on(S - BLOCK, BLOCK)
-        store_words(S - BLOCK, BLOCK)
+        store_words(S - QUARTER, QUARTER)
 
         scales_view = out_2[0].bitcast(I32)
         for q in range(4):

@@ -24,8 +24,6 @@ LIST_COL = 16
 HALF = 512
 QUARTER = 256
 BLOCK = 128
-FIRST_SPLIT = 640
-LAST_SPLIT = 384
 
 
 def entries(list_tile, start, count):
@@ -52,56 +50,27 @@ def tile_picked_treeup_relu_lo_kernel(tc, xT, w1, w2, share, offs, par, out_0, o
         w2_early = keep.tile([P, PACK, QUARTER], F32, name="w2_early")
         share_sb = keep.tile([P, S], F32, name="share_sb")
 
-        x_view = xT.rearrange("(p u e) s -> u p e s", u=2, e=2)
-        x_pieces = [(0, 0, 2 * HALF), (0, 2 * HALF, 2 * HALF), (1, 0, 2 * HALF), (1, 2 * HALF, HALF), (1, 3 * HALF, HALF)]
-        x_raw = [keep.tile([P, 2, n], F32, name="x_raw%d" % k) for k, (u, c0, n) in enumerate(x_pieces)]
+        x_rows = [keep.tile([P, T], F32, name="x_rows%d" % j) for j in range(PACK)]
+        x_view = xT.rearrange("(p j) s -> j p s", j=PACK)
         nc.sync.dma_start(offs_sb[:], offs)
-        for k, (u, c0, n) in enumerate(x_pieces):
-            nc.sync.dma_start(x_raw[k][:], x_view[u][:, :, c0 : c0 + n])
+        for j in range(PACK):
+            nc.sync.dma_start(x_rows[j][:], x_view[j])
         nc.sync.dma_start(w1_raw[:], w1.rearrange("(p j) c -> p j c", j=PACK))
         nc.sync.dma_start(par_sb[:], par)
         nc.sync.dma_start(share_sb[:], share)
         w2_view = w2.rearrange("(p j) c -> p j c", j=PACK)
         nc.sync.dma_start(w2_early[:], w2_view[:, :, QUARTER:])
 
-        x_pairs = [keep.tile([P, 2 * T], BF16, name="x_pairs%d" % u, align_bytes=64) for u in range(2)]
-
-        def pair_up(copy, k, lo, hi):
-            u, c0, n = x_pieces[k]
-            copy(
-                x_pairs[u][:, 2 * (c0 + lo) : 2 * (c0 + hi)].rearrange("p (c i e) -> p c e i", i=4, e=2),
-                x_raw[k][:, :, lo:hi].rearrange("p e (c i) -> p c e i", i=4),
-            )
-
-        node_parts = [(0, HALF), (HALF, QUARTER), (HALF + QUARTER, QUARTER)]
-        x_woven = [keep.tile([P, PACK * n], BF16, name="x_woven%d" % q, align_bytes=64)[:] for q, (s0, n) in enumerate(node_parts)]
-
-        picked = [keep.tile([P, 2, QUARTER], U32, name="picked%d" % r) for r in range(S // QUARTER)]
-
-        def pick(u):
-            for r in range(S // QUARTER):
-                nc.vector.tensor_copy(picked[r][:, u, :], x_pairs[u][:].bitcast(U32).indirect(entries(offs_sb, r * QUARTER, QUARTER)))
-
-        def weave_words(copy, dtype, q, lo, n):
-            s0 = node_parts[q][0] + lo
-            copy(
-                x_woven[q].bitcast(dtype)[:, 2 * lo : 2 * (lo + n)].rearrange("p (c i u) -> p c u i", i=4, u=2),
-                picked[s0 // QUARTER][:].bitcast(dtype).rearrange("p u (c i) -> p c u i", i=4),
-            )
-
-        pair_up(lambda out, in_: nc.scalar.activation(out, in_, COPY), 0, 0, 2 * HALF)
-        pair_up(nc.vector.tensor_copy, 1, 0, FIRST_SPLIT)
-        pair_up(nc.scalar.copy, 1, FIRST_SPLIT, 2 * HALF)
-        pick(0)
-        pair_up(nc.scalar.copy, 2, 0, 2 * HALF)
-        pair_up(nc.vector.tensor_copy, 3, 0, HALF)
-        pair_up(nc.vector.tensor_copy, 4, 0, LAST_SPLIT)
-        pair_up(nc.scalar.copy, 4, LAST_SPLIT, HALF)
-        pick(1)
-        for lo in (0, QUARTER):
-            weave_words(nc.scalar.copy, U32, 0, lo, QUARTER)
-        for q in (1, 2):
-            weave_words(nc.scalar.copy, U32, q, 0, QUARTER)
+        picked = keep.tile([P, PACK, S], BF16, name="picked", align_bytes=64)
+        x_woven = [keep.tile([P, PACK * HALF], BF16, name="x_woven%d" % u, align_bytes=64) for u in range(2)]
+        for j in range(PACK - 1):
+            nc.vector.tensor_copy(picked[:, j, :], x_rows[j][:].indirect(offs_sb[:]))
+        for s0 in range(0, S, QUARTER):
+            nc.vector.tensor_copy(picked[:, PACK - 1, s0 : s0 + QUARTER], x_rows[PACK - 1][:].indirect(entries(offs_sb, s0, QUARTER)))
+        x_copies = [lambda out, in_: nc.scalar.activation(out, in_, COPY), nc.scalar.copy, nc.scalar.copy, nc.vector.tensor_copy]
+        for q, copy in enumerate(x_copies):
+            part = x_woven[q // 2][:, PACK * QUARTER * (q % 2) : PACK * QUARTER * (q % 2 + 1)]
+            copy(woven(part), planar(picked[:, :, q * QUARTER : (q + 1) * QUARTER]))
 
         def deal(engine_copy, raw, dealt, t0, nt, m0=0):
             columns = raw.rearrange("p j (m t) -> p m j t", t=PACK)[:, :, :, t0 : t0 + nt]
@@ -114,11 +83,9 @@ def tile_picked_treeup_relu_lo_kernel(tc, xT, w1, w2, share, offs, par, out_0, o
         x_scales = [keep.tile([P, HALF], U8, name="x_scales%d" % u, align_bytes=64) for u in range(2)]
         deal(nc.vector.tensor_copy, w1_raw[:], w1_dealt[0][:], 0, 2)
         deal(nc.scalar.copy, w1_raw[:], w1_dealt[1][:], 2, 2)
-        nc.vector.quantize_mx(out=x_codes[:, :HALF].bitcast(FP8X4), scales=x_scales[0][:], in_=x_woven[0])
+        nc.vector.quantize_mx(out=x_codes[:, :HALF].bitcast(FP8X4), scales=x_scales[0][:], in_=x_woven[0][:])
         nc.vector.quantize_mx(out=w1_codes[0][:].bitcast(FP8X4), scales=w1_scales[0][:], in_=w1_dealt[0][:])
-        for q in (1, 2):
-            s0, n = node_parts[q]
-            nc.vector.quantize_mx(out=x_codes[:, s0 : s0 + n].bitcast(FP8X4), scales=x_scales[1][:, s0 - HALF : s0 - HALF + n], in_=x_woven[q])
+        nc.vector.quantize_mx(out=x_codes[:, HALF:].bitcast(FP8X4), scales=x_scales[1][:], in_=x_woven[1][:])
         nc.vector.quantize_mx(out=w1_codes[1][:].bitcast(FP8X4), scales=w1_scales[1][:], in_=w1_dealt[1][:])
 
         identity = keep.tile([P, P], F32, name="identity")
@@ -131,7 +98,7 @@ def tile_picked_treeup_relu_lo_kernel(tc, xT, w1, w2, share, offs, par, out_0, o
         w2_codes = keep.tile([P, H], U32, name="w2_codes", align_bytes=64)
         w2_scales = keep.tile([P, H], U8, name="w2_scales", align_bytes=64)
 
-        bank_turn = [0, 1, 2, 3, 1, 4, 5, 6, 7, 0] + 2 * [2, 3, 1, 4, 5, 6, 7, 0]
+        bank_turn = [0, 1, 0, 2, 3, 4, 5, 6] + 3 * [7, 1, 2, 0, 3, 4, 5, 6]
 
         def next_bank(shape):
             return psum.tile(shape, F32, name="bank", tag="bank%d" % bank_turn.pop(0))
@@ -140,7 +107,7 @@ def tile_picked_treeup_relu_lo_kernel(tc, xT, w1, w2, share, offs, par, out_0, o
         h_late = keep.tile([P, PACK, HALF], F32, name="h_late")
         for t in range(PACK):
             w_cols = slice((t % 2) * P, (t % 2 + 1) * P)
-            for s0, n in [(s0, QUARTER) for s0 in range(0, S, QUARTER)] if t == 0 else [(0, HALF), (HALF, HALF)]:
+            for s0, n in [(0, HALF), (HALF, HALF)]:
                 cols = slice(s0, s0 + n)
                 bank = next_bank([P, n])
                 nc.tensor.matmul_mx(
@@ -291,9 +258,8 @@ def tile_picked_treeup_relu_lo_kernel(tc, xT, w1, w2, share, offs, par, out_0, o
         hand_on(HALF, QUARTER)
         store_words(0, S - QUARTER)
         nc.vector.tensor_copy(woven(y_woven[:, PACK * (S - QUARTER) : PACK * (S - BLOCK)]), planar(y_tiles[-2][:]))
-        hand_on(S - QUARTER, BLOCK)
         nc.vector.tensor_copy(woven(y_woven[:, PACK * (S - BLOCK) :]), planar(y_tiles[-1][:]))
-        hand_on(S - BLOCK, BLOCK)
+        hand_on(S - QUARTER, QUARTER)
         store_words(S - QUARTER, QUARTER)
 
         scales_view = out_2[0].bitcast(I32)

@@ -19,11 +19,13 @@ COPY = mybir.ActivationFunctionType.Copy
 RELU = mybir.ActivationFunctionType.Relu
 
 P = 128
-PACK = 4
+SLOTS = 4
 LIST_COL = 16
-HALF = 512
-QUARTER = 256
+HALF = S // 2
+QUARTER = S // 4
 BLOCK = 128
+BANKS = 8
+LAST = S - BLOCK
 
 
 def entries(list_tile, start, count):
@@ -31,11 +33,15 @@ def entries(list_tile, start, count):
 
 
 def woven(ap):
-    return ap.rearrange("p (c i t) -> p c t i", i=4, t=PACK)
+    return ap.rearrange("p (c i t) -> p c t i", i=4, t=SLOTS)
 
 
 def planar(ap):
     return ap.rearrange("p t (c i) -> p c t i", i=4)
+
+
+def nodes(woven_tile, start, count):
+    return woven_tile[:, SLOTS * start : SLOTS * (start + count)]
 
 
 def tile_picked_treeup_relu_lo_kernel(tc, xT, w1, w2, share, offs, par, out_0, out_1, out_2):
@@ -44,222 +50,211 @@ def tile_picked_treeup_relu_lo_kernel(tc, xT, w1, w2, share, offs, par, out_0, o
         keep = ctx.enter_context(tc.tile_pool(name="keep", bufs=1))
         psum = ctx.enter_context(tc.psum_pool(name="psum", bufs=1))
 
+        def quantise(codes, scales, values):
+            nc.vector.quantize_mx(out=codes.bitcast(FP8X4), scales=scales, in_=values)
+
+        def product(out, w_codes, w_scales, codes, scales):
+            nc.tensor.matmul_mx(
+                out=out, lhsT=w_codes.bitcast(FP8X4), lhsT_scale=w_scales, rhs=codes.bitcast(FP8X4), rhs_scale=scales, start=True, stop=True
+            )
+
+        def deal(copy, raw, dealt, first_slot):
+            columns = raw[:].rearrange("p j (m t) -> p m j t", t=SLOTS)[:, :, :, first_slot : first_slot + 2]
+            copy(dealt[:].rearrange("p (t m j) -> p m j t", t=2, j=SLOTS), columns)
+
+        banks_taken = []
+
+        def next_bank(shape):
+            banks_taken.append(shape)
+            return psum.tile(shape, F32, name="bank", tag="bank%d" % (len(banks_taken) % BANKS))
+
         offs_sb = keep.tile([P, S // LIST_COL], U16, name="offs_sb")
         par_sb = keep.tile([P, S // LIST_COL], U16, name="par_sb")
-        w1_raw = keep.tile([P, PACK, H], F32, name="w1_raw")
-        w2_early = keep.tile([P, PACK, QUARTER], F32, name="w2_early")
+        x_rows = [keep.tile([P, T], F32, name="x_rows%d" % t) for t in range(SLOTS)]
+        w1_raw = keep.tile([P, SLOTS, H], F32, name="w1_raw")
+        w2_raw = keep.tile([P, SLOTS, H], F32, name="w2_raw")
         share_sb = keep.tile([P, S], F32, name="share_sb")
-
-        x_rows = [keep.tile([P, T], F32, name="x_rows%d" % j) for j in range(PACK)]
-        x_view = xT.rearrange("(p j) s -> j p s", j=PACK)
+        x_view = xT.rearrange("(p t) s -> t p s", t=SLOTS)
+        nc.sync.dma_start(x_rows[0][:], x_view[0])
         nc.sync.dma_start(offs_sb[:], offs)
-        for j in range(PACK):
-            nc.sync.dma_start(x_rows[j][:], x_view[j])
-        nc.sync.dma_start(w1_raw[:], w1.rearrange("(p j) c -> p j c", j=PACK))
+        for t in range(1, SLOTS):
+            nc.sync.dma_start(x_rows[t][:], x_view[t])
+        nc.sync.dma_start(w1_raw[:], w1.rearrange("(p j) c -> p j c", j=SLOTS))
+        nc.sync.dma_start(w2_raw[:], w2.rearrange("(p j) c -> p j c", j=SLOTS))
         nc.sync.dma_start(par_sb[:], par)
         nc.sync.dma_start(share_sb[:], share)
-        w2_view = w2.rearrange("(p j) c -> p j c", j=PACK)
-        nc.sync.dma_start(w2_early[:], w2_view[:, :, QUARTER:])
 
-        picked = keep.tile([P, PACK, S], BF16, name="picked", align_bytes=64)
-        x_woven = [keep.tile([P, PACK * HALF], BF16, name="x_woven%d" % u, align_bytes=64) for u in range(2)]
-        for j in range(PACK - 1):
-            nc.vector.tensor_copy(picked[:, j, :], x_rows[j][:].indirect(offs_sb[:]))
+        picked = keep.tile([P, SLOTS, S], BF16, name="picked", align_bytes=64)
+        x_rounded = keep.tile([P, T], BF16, name="x_rounded")
+        nc.scalar.activation(x_rounded[:], x_rows[1][:], COPY)
+        nc.scalar.activation(picked[:, 1, S - QUARTER :], x_rounded[:].indirect(entries(offs_sb, S - QUARTER, QUARTER)), COPY)
+        for t, count in enumerate((S, S - QUARTER, S)):
+            nc.vector.tensor_copy(picked[:, t, :count], x_rows[t][:].indirect(entries(offs_sb, 0, count)))
         for s0 in range(0, S, QUARTER):
-            nc.vector.tensor_copy(picked[:, PACK - 1, s0 : s0 + QUARTER], x_rows[PACK - 1][:].indirect(entries(offs_sb, s0, QUARTER)))
-        x_copies = [lambda out, in_: nc.scalar.activation(out, in_, COPY), nc.scalar.copy, nc.scalar.copy, nc.vector.tensor_copy]
-        for q, copy in enumerate(x_copies):
-            part = x_woven[q // 2][:, PACK * QUARTER * (q % 2) : PACK * QUARTER * (q % 2 + 1)]
-            copy(woven(part), planar(picked[:, :, q * QUARTER : (q + 1) * QUARTER]))
+            nc.vector.tensor_copy(picked[:, SLOTS - 1, s0 : s0 + QUARTER], x_rows[SLOTS - 1][:].indirect(entries(offs_sb, s0, QUARTER)))
 
-        def deal(engine_copy, raw, dealt, t0, nt, m0=0):
-            columns = raw.rearrange("p j (m t) -> p m j t", t=PACK)[:, :, :, t0 : t0 + nt]
-            engine_copy(dealt.rearrange("p (t m j) -> p m j t", t=nt, j=PACK)[:, m0 : m0 + columns.shape[1]], columns)
+        x_woven = [keep.tile([P, SLOTS * HALF], BF16, name="x_woven%d" % u, align_bytes=64) for u in range(2)]
+        for q, copy in enumerate((nc.scalar.copy, nc.scalar.copy, nc.vector.tensor_copy, nc.scalar.copy)):
+            copy(woven(nodes(x_woven[q // 2], q % 2 * QUARTER, QUARTER)), planar(picked[:, :, q * QUARTER : (q + 1) * QUARTER]))
 
-        w1_dealt = [keep.tile([P, 2 * P * PACK], BF16, name="w1_dealt%d" % u, tag="w1_dealt%d" % u, align_bytes=64) for u in range(2)]
-        w1_codes = [keep.tile([P, 2 * P], U32, name="w1_codes%d" % u, align_bytes=64) for u in range(2)]
+        w1_dealt = [keep.tile([P, 2 * P * SLOTS], BF16, name="w1_dealt%d" % u, align_bytes=64) for u in range(2)]
+        w1_codes = [keep.tile([P, 2 * P], U32, name="w1_codes%d" % u, tag="w1_codes%d" % u, align_bytes=64) for u in range(2)]
         w1_scales = [keep.tile([P, 2 * P], U8, name="w1_scales%d" % u, align_bytes=64) for u in range(2)]
         x_codes = keep.tile([P, S], U32, name="x_codes", align_bytes=64)
         x_scales = [keep.tile([P, HALF], U8, name="x_scales%d" % u, align_bytes=64) for u in range(2)]
-        deal(nc.vector.tensor_copy, w1_raw[:], w1_dealt[0][:], 0, 2)
-        deal(nc.scalar.copy, w1_raw[:], w1_dealt[1][:], 2, 2)
-        nc.vector.quantize_mx(out=x_codes[:, :HALF].bitcast(FP8X4), scales=x_scales[0][:], in_=x_woven[0][:])
-        nc.vector.quantize_mx(out=w1_codes[0][:].bitcast(FP8X4), scales=w1_scales[0][:], in_=w1_dealt[0][:])
-        nc.vector.quantize_mx(out=x_codes[:, HALF:].bitcast(FP8X4), scales=x_scales[1][:], in_=x_woven[1][:])
-        nc.vector.quantize_mx(out=w1_codes[1][:].bitcast(FP8X4), scales=w1_scales[1][:], in_=w1_dealt[1][:])
+        deal(nc.vector.tensor_copy, w1_raw, w1_dealt[0], 0)
+        deal(nc.scalar.copy, w1_raw, w1_dealt[1], 2)
+        for u in range(2):
+            quantise(x_codes[:, u * HALF : (u + 1) * HALF], x_scales[u][:], x_woven[u][:])
+            quantise(w1_codes[u][:], w1_scales[u][:], w1_dealt[u][:])
 
         identity = keep.tile([P, P], F32, name="identity")
         make_identity(nc, identity[:])
 
-        w2_dealt = keep.tile([P, H * PACK], BF16, name="w2_dealt", align_bytes=64)
-        deal(nc.vector.tensor_copy, w2_early[:], w2_dealt[:], 0, PACK, QUARTER // PACK)
-        w2_late = keep.tile([P, PACK, QUARTER], F32, name="w2_late", tag="w1_dealt0", align_bytes=64)
-        nc.sync.dma_start(w2_late[:], w2_view[:, :, :QUARTER])
         w2_codes = keep.tile([P, H], U32, name="w2_codes", align_bytes=64)
         w2_scales = keep.tile([P, H], U8, name="w2_scales", align_bytes=64)
+        w2_first = keep.tile([P, 2 * P * SLOTS], BF16, name="w2_first", align_bytes=64)
+        deal(nc.vector.tensor_copy, w2_raw, w2_first, 0)
+        quantise(w2_codes[:, : 2 * P], w2_scales[:, : 2 * P], w2_first[:])
 
-        bank_turn = [0, 1, 0, 2, 3, 4, 5, 6] + 3 * [7, 1, 2, 0, 3, 4, 5, 6]
-
-        def next_bank(shape):
-            return psum.tile(shape, F32, name="bank", tag="bank%d" % bank_turn.pop(0))
-
-        h_rows = [keep.tile([P, S], F32, name="h_rows%d" % t) for t in range(PACK)]
-        h_late = keep.tile([P, PACK, HALF], F32, name="h_late")
-        for t in range(PACK):
-            w_cols = slice((t % 2) * P, (t % 2 + 1) * P)
-            for s0, n in [(0, HALF), (HALF, HALF)]:
-                cols = slice(s0, s0 + n)
-                bank = next_bank([P, n])
-                nc.tensor.matmul_mx(
-                    out=bank[:],
-                    lhsT=w1_codes[t // 2][:, w_cols].bitcast(FP8X4),
-                    lhsT_scale=w1_scales[t // 2][:, w_cols],
-                    rhs=x_codes[:, cols].bitcast(FP8X4),
-                    rhs_scale=x_scales[s0 // HALF][:, s0 % HALF : s0 % HALF + n],
-                    start=True,
-                    stop=True,
-                )
+        h_rows = [keep.tile([P, S], F32, name="h_rows%d" % t) for t in range(SLOTS)]
+        h_late = keep.tile([P, SLOTS, HALF], F32, name="h_late")
+        for t in range(SLOTS):
+            w_cols = slice(t % 2 * P, (t % 2 + 1) * P)
+            for u in range(2):
+                cols = slice(u * HALF, (u + 1) * HALF)
+                bank = next_bank([P, HALF])
+                product(bank[:], w1_codes[t // 2][:, w_cols], w1_scales[t // 2][:, w_cols], x_codes[:, cols], x_scales[u][:])
                 nc.scalar.activation(h_rows[t][:, cols], bank[:], RELU)
             nc.sync.dma_start(h_late[:, t, :], h_rows[t][:, HALF:])
-        deal(nc.scalar.copy, w2_late[:], w2_dealt[:], 0, PACK)
 
-        def take(out, t, s0, n):
-            nc.vector.tensor_tensor(out, h_rows[t][:].indirect(entries(par_sb, s0, n)), share_sb[:, s0 : s0 + n], MULT)
+        w2_second = keep.tile([P, 2 * P * SLOTS], BF16, name="w2_second", tag="w1_codes1", align_bytes=64)
+        deal(nc.scalar.copy, w2_raw, w2_second, 2)
 
-        sum_banks = [next_bank([P, PACK, P]) for b in range(HALF // BLOCK)]
+        def take(out, t, s0, count):
+            nc.vector.tensor_tensor(out, h_rows[t][:].indirect(entries(par_sb, s0, count)), share_sb[:, s0 : s0 + count], MULT)
 
-        def take_and_turn(taken, t, s0, n):
-            take(taken, t, s0, n)
-            for b0 in range(0, n, BLOCK):
-                bank = sum_banks[(s0 + b0) // BLOCK]
-                nc.tensor.matmul(bank[:, t, :], h_rows[t][:, s0 + b0 : s0 + b0 + BLOCK], identity[:], start=True, stop=False, is_transpose=True)
-                nc.tensor.matmul(bank[:, t, :], taken[:, b0 : b0 + BLOCK], identity[:], start=False, stop=True, is_transpose=True)
+        sums = [next_bank([P, SLOTS, P]) for b in range(HALF // BLOCK)]
+
+        def take_and_add(taken, t, s0, count):
+            take(taken, t, s0, count)
+            for b0 in range(0, count, BLOCK):
+                place = sums[(s0 + b0) // BLOCK][:, t, :]
+                own = h_rows[t][:, s0 + b0 : s0 + b0 + BLOCK]
+                nc.tensor.matmul(place, own, identity[:], start=True, stop=False, is_transpose=True)
+                nc.tensor.matmul(place, taken[:, b0 : b0 + BLOCK], identity[:], start=False, stop=True, is_transpose=True)
 
         for t in range(2):
             wide = keep.tile([P, HALF], F32, name="taken_wide%d" % t)
-            take_and_turn(wide[:], t, 0, HALF)
-        narrow = keep.tile([P, 2, QUARTER], F32, name="taken_narrow")
-        for t in range(2, PACK):
-            take_and_turn(narrow[:, t - 2, :], t, 0, QUARTER)
-        taken_last = keep.tile([P, QUARTER], F32, name="taken_last")
-        take_and_turn(taken_last[:], 3, QUARTER, QUARTER)
-        take_and_turn(w2_late[:, PACK - 1, :], 2, QUARTER, QUARTER)
-        nc.vector.quantize_mx(out=w2_codes[:].bitcast(FP8X4), scales=w2_scales[:], in_=w2_dealt[:])
+            take_and_add(wide[:], t, 0, HALF)
+        for t, s0 in ((2, 0), (3, 0), (3, QUARTER)):
+            narrow = keep.tile([P, QUARTER], F32, name="taken_narrow%d_%d" % (t, s0))
+            take_and_add(narrow[:], t, s0, QUARTER)
+        take_and_add(w2_raw[:, 0, :QUARTER], 2, QUARTER, QUARTER)
+        quantise(w2_codes[:, 2 * P :], w2_scales[:, 2 * P :], w2_second[:])
 
-        def round_block(b, pair, back):
-            nc.scalar.copy(
-                pair.rearrange("s (u p e) -> s u p e", u=2, e=2),
-                sum_banks[b][:].rearrange("s (u e) p -> s u p e", e=2),
-            )
+        def round_and_turn(b, pair, back):
+            nc.scalar.copy(pair[:].rearrange("s (u p e) -> s u p e", u=2, e=2), sums[b][:].rearrange("s (u e) p -> s u p e", e=2))
             for u in range(2):
-                nc.tensor.transpose(back[:, u, :], pair.bitcast(F32)[:, u * P : (u + 1) * P], identity[:])
+                nc.tensor.transpose(back[:, u, :], pair[:].bitcast(F32)[:, u * P : (u + 1) * P], identity[:])
 
-        def weave_back(back, z_woven):
-            nc.scalar.copy(
-                z_woven.bitcast(F32).rearrange("p (b s u) -> p b s u", s=BLOCK, u=2),
-                back.rearrange("p b u s -> p b s u"),
-            )
+        def weave_words(back, z_part):
+            nc.scalar.copy(z_part.bitcast(F32).rearrange("p (b s u) -> p b s u", s=BLOCK, u=2), back[:].rearrange("p b u s -> p b s u"))
 
-        y_codes = keep.tile([P, S], U32, name="y_codes", align_bytes=64)
-        y_view = out_0.rearrange("(p t) s -> p t s", t=PACK)
-        words_view = out_1[0].rearrange("p c r -> p (c r)").bitcast(I32)
-        y_woven = keep.tile([P, PACK * S], BF16, name="y_woven", align_bytes=64)
-        unwoven = []
-
-        def product(bank, t, z_codes, z_scales):
-            w_cols = slice(t * P, (t + 1) * P)
-            nc.tensor.matmul_mx(
-                out=bank,
-                lhsT=w2_codes[:, w_cols].bitcast(FP8X4),
-                lhsT_scale=w2_scales[:, w_cols],
-                rhs=z_codes.bitcast(FP8X4),
-                rhs_scale=z_scales,
-                start=True,
-                stop=True,
-            )
-
-        def second_layer(s0, n, z_woven, y_rows):
-            z_codes = keep.tile([P, n], U32, name="z_codes%d" % s0, align_bytes=64)
-            z_scales = keep.tile([P, n], U8, name="z_scales%d" % s0, align_bytes=64)
-            nc.vector.quantize_mx(out=z_codes[:].bitcast(FP8X4), scales=z_scales[:], in_=z_woven)
-            for b0 in range(0, n, BLOCK):
-                block = slice(b0, b0 + BLOCK)
-                y_block = y_woven[:, PACK * (s0 + b0) : PACK * (s0 + b0 + BLOCK)]
-                if s0 + b0 == S - BLOCK:
-                    for u in range(2):
-                        bank = next_bank([P, 2, BLOCK])
-                        for e in range(2):
-                            product(bank[:, e, :], 2 * u + e, z_codes[:, block], z_scales[:, block])
-                        nc.scalar.copy(y_rows[:, 2 * u : 2 * u + 2, :], bank[:])
-                    continue
-                bank = next_bank([P, PACK, BLOCK])
-                for t in range(PACK):
-                    product(bank[:, t, :], t, z_codes[:, block], z_scales[:, block])
-                nc.scalar.copy(y_rows[:, :, block], bank[:])
-                unwoven.append((y_block, bank))
-
-        def weave_waiting(count):
-            for b in range(count):
-                y_block, bank = unwoven.pop(0)
-                nc.scalar.copy(y_block.rearrange("p (s t) -> p s t", t=PACK), bank[:].rearrange("p t s -> p s t"))
-
-        def hand_on(s0, n):
-            cols = slice(s0, s0 + n)
-            nc.vector.quantize_mx(out=y_codes[:, cols].bitcast(FP8X4), scales=y_scales[:, cols], in_=y_woven[:, PACK * s0 : PACK * (s0 + n)])
-
-        def store_words(s0, n):
-            nc.sync.dma_start(words_view[:, s0 : s0 + n], y_codes[:, s0 : s0 + n].bitcast(I32))
-
-        def take_all(ring, s0, n):
-            for t in range(PACK):
-                take(ring[:, t, :], t, s0, n)
-
-        def add_direct(ring, s0, n, z_woven):
-            nc.vector.tensor_tensor(woven(z_woven), planar(ring), planar(h_late[:, :, s0 - HALF : s0 - HALF + n]), ADD)
-
-        y_tiles = [keep.tile([P, PACK, n], F32, name="y_rows%d" % c) for c, n in enumerate((QUARTER, QUARTER, QUARTER, BLOCK, BLOCK))]
-        z_first = keep.tile([P, PACK * QUARTER], BF16, name="z_first", align_bytes=64)
-        z_second = keep.tile([P, PACK * QUARTER], BF16, name="z_second", align_bytes=64)
-        pair_tiles = [keep.tile([P, H], BF16, name="pair%d" % b, tag="pair%d" % b) for b in range(3)]
-        pairs = [pair_tiles[b][:] for b in (0, 1, 2, 1)]
+        z_turned = [keep.tile([P, SLOTS * QUARTER], BF16, name="z_turned%d" % c, align_bytes=64) for c in range(2)]
+        pairs = [keep.tile([P, H], BF16, name="pair%d" % b, tag="pair%d" % b) for b in range(3)]
         back_first = next_bank([P, 2, 2, BLOCK])
         backs = [next_bank([P, 1, 2, BLOCK]) for b in range(2)]
-        round_block(0, pairs[0], back_first[:, 0])
-        round_block(1, pairs[1], back_first[:, 1])
-        round_block(2, pairs[2], backs[0][:, 0])
-        weave_back(back_first[:], z_first[:])
-        round_block(3, pairs[3], backs[1][:, 0])
+        round_and_turn(0, pairs[0], back_first[:, 0])
+        round_and_turn(1, pairs[1], back_first[:, 1])
+        round_and_turn(2, pairs[2], backs[0][:, 0])
+        weave_words(back_first, z_turned[0][:])
+        round_and_turn(3, pairs[1], backs[1][:, 0])
         for b in range(2):
-            weave_back(backs[b][:], z_second[:, b * H : (b + 1) * H])
-        for c, z_turned in enumerate((z_first, z_second)):
-            second_layer(c * QUARTER, QUARTER, z_turned[:], y_tiles[c][:])
-            nc.sync.dma_start(y_view[:, :, c * QUARTER : (c + 1) * QUARTER], y_tiles[c][:])
-            weave_waiting(2)
-        ring_odd = keep.tile([P, PACK, BLOCK], F32, name="ring_odd", tag="pair1")
-        rings = [w2_late[:, :, :BLOCK], ring_odd[:]]
-        z_late = keep.tile([P, PACK * 3 * BLOCK], BF16, name="z_late", align_bytes=64)
-        for b in range(HALF // BLOCK):
-            s0 = HALF + b * BLOCK
-            z_woven = z_first[:, :H] if b == 0 else z_late[:, (b - 1) * H : b * H]
-            take_all(rings[b % 2], s0, BLOCK)
-            add_direct(rings[b % 2], s0, BLOCK, z_woven)
-            if b < 2:
-                second_layer(s0, BLOCK, z_woven, y_tiles[2][:, :, b * BLOCK : (b + 1) * BLOCK])
-            else:
-                second_layer(s0, BLOCK, z_woven, y_tiles[b + 1][:])
-            if b == 1:
-                nc.sync.dma_start(y_view[:, :, HALF : HALF + QUARTER], y_tiles[2][:])
-                weave_waiting(2)
-            if b >= 2:
-                nc.scalar.dma_start(y_view[:, :, s0 : s0 + BLOCK], y_tiles[b + 1][:])
+            weave_words(backs[b], nodes(z_turned[1], b * BLOCK, BLOCK))
+
+        y_view = out_0.rearrange("(p t) s -> p t s", t=SLOTS)
+        words_view = out_1[0].rearrange("p c r -> p (c r)").bitcast(I32)
+        y_woven = keep.tile([P, SLOTS * S], BF16, name="y_woven", align_bytes=64)
+        y_codes = keep.tile([P, S], U32, name="y_codes", align_bytes=64)
         y_scales = keep.tile([P, S], U8, name="y_scales", align_bytes=64)
-        hand_on(0, QUARTER)
-        hand_on(QUARTER, QUARTER)
-        hand_on(HALF, QUARTER)
+        y_banks = {}
+
+        def quantise_z(s0, count, z_part):
+            z_codes = keep.tile([P, count], U32, name="z_codes%d" % s0, align_bytes=64)
+            z_scales = keep.tile([P, count], U8, name="z_scales%d" % s0, align_bytes=64)
+            quantise(z_codes[:], z_scales[:], z_part)
+            return z_codes, z_scales
+
+        def multiply(z_codes, z_scales, y_part, first_slot):
+            bank = next_bank([P, y_part.shape[1], BLOCK])
+            for e in range(y_part.shape[1]):
+                w_cols = slice((first_slot + e) * P, (first_slot + e + 1) * P)
+                product(bank[:, e, :], w2_codes[:, w_cols], w2_scales[:, w_cols], z_codes, z_scales)
+            nc.scalar.copy(y_part, bank[:])
+            return bank
+
+        def weave_banks(*starts):
+            for s0 in starts:
+                nc.scalar.copy(nodes(y_woven, s0, BLOCK).rearrange("p (s t) -> p s t", t=SLOTS), y_banks[s0][:].rearrange("p t s -> p s t"))
+
+        def store_rows(queue, s0, y_rows):
+            queue.dma_start(y_view[:, :, s0 : s0 + y_rows.shape[2]], y_rows[:])
+
+        def weave_rows(s0, y_rows):
+            nc.vector.tensor_copy(woven(nodes(y_woven, s0, BLOCK)), planar(y_rows[:]))
+
+        def quantise_y(s0, count):
+            quantise(y_codes[:, s0 : s0 + count], y_scales[:, s0 : s0 + count], nodes(y_woven, s0, count))
+
+        def store_words(s0, count):
+            nc.sync.dma_start(words_view[:, s0 : s0 + count], y_codes[:, s0 : s0 + count].bitcast(I32))
+
+        for c in range(2):
+            s0 = c * QUARTER
+            z_codes, z_scales = quantise_z(s0, QUARTER, z_turned[c][:])
+            y_rows = keep.tile([P, SLOTS, QUARTER], F32, name="y_rows%d" % s0)
+            for b0 in (0, BLOCK):
+                block = slice(b0, b0 + BLOCK)
+                y_banks[s0 + b0] = multiply(z_codes[:, block], z_scales[:, block], y_rows[:, :, block], 0)
+            store_rows(nc.sync, s0, y_rows)
+            weave_banks(s0, s0 + BLOCK)
+
+        taken_odd = keep.tile([P, SLOTS, BLOCK], F32, name="taken_odd", tag="pair1")
+        places = [w2_raw[:, :, QUARTER : QUARTER + BLOCK], taken_odd[:]]
+        z_added = keep.tile([P, SLOTS * (HALF - BLOCK)], BF16, name="z_added", align_bytes=64)
+
+        def add_block(b):
+            s0 = HALF + b * BLOCK
+            z_part = nodes(z_turned[0], 0, BLOCK) if b == 0 else nodes(z_added, (b - 1) * BLOCK, BLOCK)
+            for t in range(SLOTS):
+                take(places[b % 2][:, t, :], t, s0, BLOCK)
+            nc.vector.tensor_tensor(woven(z_part), planar(places[b % 2]), planar(h_late[:, :, b * BLOCK : (b + 1) * BLOCK]), ADD)
+            z_codes, z_scales = quantise_z(s0, BLOCK, z_part)
+            return z_codes[:], z_scales[:]
+
+        y_third = keep.tile([P, SLOTS, QUARTER], F32, name="y_third")
+        for b in range(2):
+            y_banks[HALF + b * BLOCK] = multiply(*add_block(b), y_third[:, :, b * BLOCK : (b + 1) * BLOCK], 0)
+        store_rows(nc.sync, HALF, y_third)
+        weave_banks(HALF)
+        y_before_last = keep.tile([P, SLOTS, BLOCK], F32, name="y_before_last")
+        multiply(*add_block(2), y_before_last[:], 0)
+        store_rows(nc.sync, LAST - BLOCK, y_before_last)
+        weave_banks(HALF + BLOCK)
+
+        y_last = keep.tile([P, SLOTS, BLOCK], F32, name="y_last")
+        z_codes, z_scales = add_block(3)
+        for first_slot in (0, 2):
+            multiply(z_codes, z_scales, y_last[:, first_slot : first_slot + 2, :], first_slot)
+        store_rows(nc.scalar, LAST, y_last)
+
+        for s0 in range(0, S - QUARTER, QUARTER):
+            quantise_y(s0, QUARTER)
         store_words(0, S - QUARTER)
-        nc.vector.tensor_copy(woven(y_woven[:, PACK * (S - QUARTER) : PACK * (S - BLOCK)]), planar(y_tiles[-2][:]))
-        nc.vector.tensor_copy(woven(y_woven[:, PACK * (S - BLOCK) :]), planar(y_tiles[-1][:]))
-        hand_on(S - QUARTER, QUARTER)
+        weave_rows(LAST - BLOCK, y_before_last)
+        weave_rows(LAST, y_last)
+        quantise_y(S - QUARTER, QUARTER)
         store_words(S - QUARTER, QUARTER)
 
         scales_view = out_2[0].bitcast(I32)

@@ -58,9 +58,19 @@ def tile_picked_treeup_relu_lo_kernel(tc, xT, w1, w2, share, offs, par, out_0, o
                 out=out, lhsT=w_codes.bitcast(FP8X4), lhsT_scale=w_scales, rhs=codes.bitcast(FP8X4), rhs_scale=scales, start=True, stop=True
             )
 
-        def deal(copy, raw, dealt, first_slot):
-            columns = raw[:].rearrange("p j (m t) -> p m j t", t=SLOTS)[:, :, :, first_slot : first_slot + 2]
-            copy(dealt[:].rearrange("p (t m j) -> p m j t", t=2, j=SLOTS), columns)
+        def deal_w1(copy, dealt, first_slot):
+            columns = w1_raw[:].rearrange("p j (g t h r) -> p t g h j r", t=SLOTS, h=2, r=4)
+            for e in range(2):
+                copy(nodes(dealt, e * P, P).rearrange("p (g h r j) -> p g h j r", h=2, r=4, j=SLOTS), columns[:, first_slot + e])
+
+        def deal_w2(copy, dealt, half):
+            columns = w2_raw[:, :, half * H // 2 : (half + 1) * H // 2].rearrange("p j (m t) -> p m j t", t=SLOTS)
+            copy(dealt[:].rearrange("p (t m j) -> p m j t", t=SLOTS, j=SLOTS), columns)
+
+        def quantise_w2(dealt, half):
+            for t in range(SLOTS):
+                cols = slice(t * P + half * P // 2, t * P + (half + 1) * P // 2)
+                quantise(w2_codes[:, cols], w2_scales[:, cols], nodes(dealt, t * P // 2, P // 2))
 
         banks_taken = []
 
@@ -80,7 +90,9 @@ def tile_picked_treeup_relu_lo_kernel(tc, xT, w1, w2, share, offs, par, out_0, o
         for t in range(1, SLOTS):
             nc.sync.dma_start(x_rows[t][:], x_view[t])
         nc.sync.dma_start(w1_raw[:], w1.rearrange("(p j) c -> p j c", j=SLOTS))
-        nc.sync.dma_start(w2_raw[:], w2.rearrange("(p j) c -> p j c", j=SLOTS))
+        w2_view = w2.rearrange("(g t r) c -> t g r c", t=SLOTS, r=8)
+        for t in range(SLOTS):
+            nc.sync.dma_start(w2_raw[:, t, :], w2_view[t])
         nc.sync.dma_start(par_sb[:], par)
         nc.sync.dma_start(share_sb[:], share)
 
@@ -102,8 +114,8 @@ def tile_picked_treeup_relu_lo_kernel(tc, xT, w1, w2, share, offs, par, out_0, o
         w1_scales = [keep.tile([P, 2 * P], U8, name="w1_scales%d" % u, align_bytes=64) for u in range(2)]
         x_codes = keep.tile([P, S], U32, name="x_codes", align_bytes=64)
         x_scales = [keep.tile([P, HALF], U8, name="x_scales%d" % u, align_bytes=64) for u in range(2)]
-        deal(nc.vector.tensor_copy, w1_raw, w1_dealt[0], 0)
-        deal(nc.scalar.copy, w1_raw, w1_dealt[1], 2)
+        deal_w1(nc.vector.tensor_copy, w1_dealt[0], 0)
+        deal_w1(nc.scalar.copy, w1_dealt[1], 2)
         for u in range(2):
             quantise(x_codes[:, u * HALF : (u + 1) * HALF], x_scales[u][:], x_woven[u][:])
             quantise(w1_codes[u][:], w1_scales[u][:], w1_dealt[u][:])
@@ -114,8 +126,8 @@ def tile_picked_treeup_relu_lo_kernel(tc, xT, w1, w2, share, offs, par, out_0, o
         w2_codes = keep.tile([P, H], U32, name="w2_codes", align_bytes=64)
         w2_scales = keep.tile([P, H], U8, name="w2_scales", align_bytes=64)
         w2_first = keep.tile([P, 2 * P * SLOTS], BF16, name="w2_first", align_bytes=64)
-        deal(nc.vector.tensor_copy, w2_raw, w2_first, 0)
-        quantise(w2_codes[:, : 2 * P], w2_scales[:, : 2 * P], w2_first[:])
+        deal_w2(nc.vector.tensor_copy, w2_first, 1)
+        quantise_w2(w2_first, 1)
 
         h_rows = [keep.tile([P, S], F32, name="h_rows%d" % t) for t in range(SLOTS)]
         h_late = keep.tile([P, SLOTS, HALF], F32, name="h_late")
@@ -129,7 +141,7 @@ def tile_picked_treeup_relu_lo_kernel(tc, xT, w1, w2, share, offs, par, out_0, o
             nc.sync.dma_start(h_late[:, t, :], h_rows[t][:, HALF:])
 
         w2_second = keep.tile([P, 2 * P * SLOTS], BF16, name="w2_second", tag="w1_codes1", align_bytes=64)
-        deal(nc.scalar.copy, w2_raw, w2_second, 2)
+        deal_w2(nc.scalar.copy, w2_second, 0)
 
         def take(out, t, s0, count):
             nc.vector.tensor_tensor(out, h_rows[t][:].indirect(entries(par_sb, s0, count)), share_sb[:, s0 : s0 + count], MULT)
@@ -150,8 +162,8 @@ def tile_picked_treeup_relu_lo_kernel(tc, xT, w1, w2, share, offs, par, out_0, o
         for t, s0 in ((2, 0), (3, 0), (3, QUARTER)):
             narrow = keep.tile([P, QUARTER], F32, name="taken_narrow%d_%d" % (t, s0))
             take_and_add(narrow[:], t, s0, QUARTER)
-        take_and_add(w2_raw[:, 0, :QUARTER], 2, QUARTER, QUARTER)
-        quantise(w2_codes[:, 2 * P :], w2_scales[:, 2 * P :], w2_second[:])
+        take_and_add(w2_raw[:, SLOTS - 1, :QUARTER], 2, QUARTER, QUARTER)
+        quantise_w2(w2_second, 0)
 
         def round_and_turn(b, pair, back):
             nc.scalar.copy(pair[:].rearrange("s (u p e) -> s u p e", u=2, e=2), sums[b][:].rearrange("s (u e) p -> s u p e", e=2))
@@ -221,7 +233,7 @@ def tile_picked_treeup_relu_lo_kernel(tc, xT, w1, w2, share, offs, par, out_0, o
             weave_banks(s0, s0 + BLOCK)
 
         taken_odd = keep.tile([P, SLOTS, BLOCK], F32, name="taken_odd", tag="pair1")
-        places = [w2_raw[:, :, QUARTER : QUARTER + BLOCK], taken_odd[:]]
+        places = [w2_raw[:, :, :BLOCK], taken_odd[:]]
         z_added = keep.tile([P, SLOTS * (HALF - BLOCK)], BF16, name="z_added", align_bytes=64)
 
         def add_block(b):

@@ -58,19 +58,13 @@ def tile_picked_treeup_relu_lo_kernel(tc, xT, w1, w2, share, offs, par, out_0, o
                 out=out, lhsT=w_codes.bitcast(FP8X4), lhsT_scale=w_scales, rhs=codes.bitcast(FP8X4), rhs_scale=scales, start=True, stop=True
             )
 
-        def deal_w1(copy, dealt, first_slot):
-            columns = w1_raw[:].rearrange("p j (g t h r) -> p t g h j r", t=SLOTS, h=2, r=4)
-            for e in range(2):
-                copy(nodes(dealt, e * P, P).rearrange("p (g h r j) -> p g h j r", h=2, r=4, j=SLOTS), columns[:, first_slot + e])
-
         def deal_w2(copy, dealt, half):
-            columns = w2_raw[:, :, half * H // 2 : (half + 1) * H // 2].rearrange("p j (m t) -> p m j t", t=SLOTS)
-            copy(dealt[:].rearrange("p (t m j) -> p m j t", t=SLOTS, j=SLOTS), columns)
+            columns = w2_raw[:].rearrange("p j (m u e) -> p u m j e", u=2, e=2)
+            copy(dealt[:].rearrange("p (e m j) -> p m j e", e=2, j=SLOTS), columns[:, half])
 
         def quantise_w2(dealt, half):
-            for t in range(SLOTS):
-                cols = slice(t * P + half * P // 2, t * P + (half + 1) * P // 2)
-                quantise(w2_codes[:, cols], w2_scales[:, cols], nodes(dealt, t * P // 2, P // 2))
+            cols = slice(half * H // 2, (half + 1) * H // 2)
+            quantise(w2_codes[:, cols], w2_scales[:, cols], dealt[:])
 
         banks_taken = []
 
@@ -87,6 +81,8 @@ def tile_picked_treeup_relu_lo_kernel(tc, xT, w1, w2, share, offs, par, out_0, o
         x_view = xT.rearrange("(p t) s -> t p s", t=SLOTS)
         nc.sync.dma_start(x_rows[0][:], x_view[0])
         nc.sync.dma_start(offs_sb[:], offs)
+        share_cols = keep.tile([P, S // P], F32, name="share_cols")
+        nc.sync.dma_start(share_cols[:], share[0].rearrange("(p b) -> p b", p=P))
         for t in range(1, SLOTS):
             nc.sync.dma_start(x_rows[t][:], x_view[t])
         nc.sync.dma_start(w1_raw[:], w1.rearrange("(p j) c -> p j c", j=SLOTS))
@@ -94,7 +90,16 @@ def tile_picked_treeup_relu_lo_kernel(tc, xT, w1, w2, share, offs, par, out_0, o
         for t in range(SLOTS):
             nc.sync.dma_start(w2_raw[:, t, :], w2_view[t])
         nc.sync.dma_start(par_sb[:], par)
-        nc.sync.dma_start(share_sb[:], share)
+
+        identity = keep.tile([P, P], F32, name="identity")
+        make_identity(nc, identity[:])
+        share_view = share_sb[:].rearrange("p (n u b) -> p u n b", u=2, b=4)
+        for u in range(2):
+            spread = next_bank([P, 4, P])
+            for b in range(4):
+                column = share_cols[:, 4 * u + b : 4 * u + b + 1]
+                nc.tensor.transpose(spread[:, b, :], column.to_broadcast([P, P]), identity[:])
+            nc.scalar.copy(share_view[:, u], spread[:].rearrange("p b n -> p n b"))
 
         picked = keep.tile([P, SLOTS, S], BF16, name="picked", align_bytes=64)
         x_rounded = keep.tile([P, T], BF16, name="x_rounded")
@@ -105,42 +110,53 @@ def tile_picked_treeup_relu_lo_kernel(tc, xT, w1, w2, share, offs, par, out_0, o
         for s0 in range(0, S, QUARTER):
             nc.vector.tensor_copy(picked[:, SLOTS - 1, s0 : s0 + QUARTER], x_rows[SLOTS - 1][:].indirect(entries(offs_sb, s0, QUARTER)))
 
-        x_woven = [keep.tile([P, SLOTS * HALF], BF16, name="x_woven%d" % u, align_bytes=64) for u in range(2)]
-        for q, copy in enumerate((nc.scalar.copy, nc.scalar.copy, nc.vector.tensor_copy, nc.scalar.copy)):
+        def aligned(shape, dtype, name, on=None):
+            return keep.tile(shape, dtype, name=name, tag=on or name, align_bytes=64)
+
+        x_woven = [aligned([P, SLOTS * HALF], BF16, "x_woven%d" % u) for u in range(2)]
+        for q, copy in enumerate((nc.scalar.copy, nc.scalar.copy, nc.vector.tensor_copy, nc.vector.tensor_copy)):
             copy(woven(nodes(x_woven[q // 2], q % 2 * QUARTER, QUARTER)), planar(picked[:, :, q * QUARTER : (q + 1) * QUARTER]))
 
-        w1_dealt = [keep.tile([P, 2 * P * SLOTS], BF16, name="w1_dealt%d" % u, align_bytes=64) for u in range(2)]
-        w1_codes = [keep.tile([P, 2 * P], U32, name="w1_codes%d" % u, tag="w1_codes%d" % u, align_bytes=64) for u in range(2)]
-        w1_scales = [keep.tile([P, 2 * P], U8, name="w1_scales%d" % u, align_bytes=64) for u in range(2)]
-        x_codes = keep.tile([P, S], U32, name="x_codes", align_bytes=64)
-        x_scales = [keep.tile([P, HALF], U8, name="x_scales%d" % u, align_bytes=64) for u in range(2)]
-        deal_w1(nc.vector.tensor_copy, w1_dealt[0], 0)
-        deal_w1(nc.scalar.copy, w1_dealt[1], 2)
-        for u in range(2):
-            quantise(x_codes[:, u * HALF : (u + 1) * HALF], x_scales[u][:], x_woven[u][:])
-            quantise(w1_codes[u][:], w1_scales[u][:], w1_dealt[u][:])
+        w1_columns = w1_raw[:].rearrange("p j (g t h r) -> p t g h j r", t=SLOTS, h=2, r=4)
+        w1_codes = aligned([P, H], U32, "w1_codes")
+        w1_scales = aligned([P, H], U8, "w1_scales")
+        w1_dealt = [aligned([P, SLOTS * P * n], BF16, "w1_dealt%d" % t) for t, n in enumerate((1, 1, 2))]
+        for t in range(SLOTS):
+            dealt = nodes(w1_dealt[min(t, 2)], max(t - 2, 0) * P, P)
+            nc.scalar.copy(dealt.rearrange("p (g h r j) -> p g h j r", h=2, r=4, j=SLOTS), w1_columns[:, t])
 
-        identity = keep.tile([P, P], F32, name="identity")
-        make_identity(nc, identity[:])
+        def quantise_w1(t, slots):
+            cols = slice(t * P, (t + slots) * P)
+            quantise(w1_codes[:, cols], w1_scales[:, cols], w1_dealt[t][:])
 
-        w2_codes = keep.tile([P, H], U32, name="w2_codes", align_bytes=64)
-        w2_scales = keep.tile([P, H], U8, name="w2_scales", align_bytes=64)
-        w2_first = keep.tile([P, 2 * P * SLOTS], BF16, name="w2_first", align_bytes=64)
+        x_codes = [aligned([P, HALF], U32, "x_codes0")]
+        x_scales = [aligned([P, HALF], U8, "x_scales0")]
+        quantise(x_codes[0][:], x_scales[0][:], x_woven[0][:])
+        quantise_w1(0, 1)
+        x_codes.append(aligned([P, HALF], U32, "x_codes1", on="x_woven0"))
+        x_scales.append(aligned([P, HALF], U8, "x_scales1", on="w1_dealt0"))
+        quantise(x_codes[1][:], x_scales[1][:], x_woven[1][:])
+        quantise_w1(1, 1)
+        quantise_w1(2, 2)
+
+        w2_codes = aligned([P, H], U32, "w2_codes")
+        w2_scales = aligned([P, H], U8, "w2_scales")
+        w2_first = aligned([P, 2 * P * SLOTS], BF16, "w2_first")
         deal_w2(nc.vector.tensor_copy, w2_first, 1)
         quantise_w2(w2_first, 1)
 
         h_rows = [keep.tile([P, S], F32, name="h_rows%d" % t) for t in range(SLOTS)]
         h_late = keep.tile([P, SLOTS, HALF], F32, name="h_late")
         for t in range(SLOTS):
-            w_cols = slice(t % 2 * P, (t % 2 + 1) * P)
+            w_cols = slice(t * P, (t + 1) * P)
             for u in range(2):
                 cols = slice(u * HALF, (u + 1) * HALF)
                 bank = next_bank([P, HALF])
-                product(bank[:], w1_codes[t // 2][:, w_cols], w1_scales[t // 2][:, w_cols], x_codes[:, cols], x_scales[u][:])
+                product(bank[:], w1_codes[:, w_cols], w1_scales[:, w_cols], x_codes[u][:], x_scales[u][:])
                 nc.scalar.activation(h_rows[t][:, cols], bank[:], RELU)
             nc.sync.dma_start(h_late[:, t, :], h_rows[t][:, HALF:])
 
-        w2_second = keep.tile([P, 2 * P * SLOTS], BF16, name="w2_second", tag="w1_codes1", align_bytes=64)
+        w2_second = keep.tile([P, 2 * P * SLOTS], BF16, name="w2_second", tag="w1_codes", align_bytes=64)
         deal_w2(nc.scalar.copy, w2_second, 0)
 
         def take(out, t, s0, count):

@@ -134,7 +134,7 @@ def tile_picked_treeup_relu_lo_kernel(tc, xT, w1, w2, share, offs, par, out_0, o
         quantise(x_codes[0][:], x_scales[0][:], x_woven[0][:])
         quantise_w1(0, 1)
         x_codes.append(aligned([P, HALF], U32, "x_codes1", on="x_woven0"))
-        x_scales.append(aligned([P, HALF], U8, "x_scales1", on="w1_dealt0"))
+        x_scales.append(aligned([P, HALF], U8, "x_scales1"))
         quantise(x_codes[1][:], x_scales[1][:], x_woven[1][:])
         quantise_w1(1, 1)
         quantise_w1(2, 2)
@@ -178,8 +178,7 @@ def tile_picked_treeup_relu_lo_kernel(tc, xT, w1, w2, share, offs, par, out_0, o
         for t, s0 in ((2, 0), (3, 0), (3, QUARTER)):
             narrow = keep.tile([P, QUARTER], F32, name="taken_narrow%d_%d" % (t, s0))
             take_and_add(narrow[:], t, s0, QUARTER)
-        take_and_add(w2_raw[:, SLOTS - 1, :QUARTER], 2, QUARTER, QUARTER)
-        quantise_w2(w2_second, 0)
+        take_and_add(w2_raw[:, SLOTS - 1, QUARTER:], 2, QUARTER, QUARTER)
 
         def round_and_turn(b, pair, back):
             nc.scalar.copy(pair[:].rearrange("s (u p e) -> s u p e", u=2, e=2), sums[b][:].rearrange("s (u e) p -> s u p e", e=2))
@@ -187,19 +186,21 @@ def tile_picked_treeup_relu_lo_kernel(tc, xT, w1, w2, share, offs, par, out_0, o
                 nc.tensor.transpose(back[:, u, :], pair[:].bitcast(F32)[:, u * P : (u + 1) * P], identity[:])
 
         def weave_words(back, z_part):
-            nc.scalar.copy(z_part.bitcast(F32).rearrange("p (b s u) -> p b s u", s=BLOCK, u=2), back[:].rearrange("p b u s -> p b s u"))
+            nc.scalar.copy(z_part.bitcast(F32).rearrange("p (b s u) -> p b s u", s=BLOCK, u=2), back.rearrange("p b u s -> p b s u"))
 
-        z_turned = [keep.tile([P, SLOTS * QUARTER], BF16, name="z_turned%d" % c, align_bytes=64) for c in range(2)]
-        pairs = [keep.tile([P, H], BF16, name="pair%d" % b, tag="pair%d" % b) for b in range(3)]
+        z_first = [aligned([P, SLOTS * BLOCK], BF16, "z_first%d" % b) for b in range(2)]
+        z_second = aligned([P, SLOTS * QUARTER], BF16, "z_second")
+        pairs = [aligned([P, H], BF16, "pair%d" % b) for b in range(3)]
         back_first = next_bank([P, 2, 2, BLOCK])
         backs = [next_bank([P, 1, 2, BLOCK]) for b in range(2)]
         round_and_turn(0, pairs[0], back_first[:, 0])
         round_and_turn(1, pairs[1], back_first[:, 1])
         round_and_turn(2, pairs[2], backs[0][:, 0])
-        weave_words(back_first, z_turned[0][:])
+        for b in range(2):
+            weave_words(back_first[:, b : b + 1], z_first[b][:])
         round_and_turn(3, pairs[1], backs[1][:, 0])
         for b in range(2):
-            weave_words(backs[b], nodes(z_turned[1], b * BLOCK, BLOCK))
+            weave_words(backs[b][:], nodes(z_second, b * BLOCK, BLOCK))
 
         y_view = out_0.rearrange("(p t) s -> p t s", t=SLOTS)
         words_view = out_1[0].rearrange("p c r -> p (c r)").bitcast(I32)
@@ -208,8 +209,8 @@ def tile_picked_treeup_relu_lo_kernel(tc, xT, w1, w2, share, offs, par, out_0, o
         y_scales = keep.tile([P, S], U8, name="y_scales", align_bytes=64)
         y_banks = {}
 
-        def quantise_z(s0, count, z_part):
-            z_codes = keep.tile([P, count], U32, name="z_codes%d" % s0, align_bytes=64)
+        def quantise_z(s0, count, z_part, on=None):
+            z_codes = aligned([P, count], U32, "z_codes%d" % s0, on=on)
             z_scales = keep.tile([P, count], U8, name="z_scales%d" % s0, align_bytes=64)
             quantise(z_codes[:], z_scales[:], z_part)
             return z_codes, z_scales
@@ -238,41 +239,59 @@ def tile_picked_treeup_relu_lo_kernel(tc, xT, w1, w2, share, offs, par, out_0, o
         def store_words(s0, count):
             nc.sync.dma_start(words_view[:, s0 : s0 + count], y_codes[:, s0 : s0 + count].bitcast(I32))
 
-        for c in range(2):
-            s0 = c * QUARTER
-            z_codes, z_scales = quantise_z(s0, QUARTER, z_turned[c][:])
-            y_rows = keep.tile([P, SLOTS, QUARTER], F32, name="y_rows%d" % s0)
-            for b0 in (0, BLOCK):
-                block = slice(b0, b0 + BLOCK)
-                y_banks[s0 + b0] = multiply(z_codes[:, block], z_scales[:, block], y_rows[:, :, block], 0)
-            store_rows(nc.sync, s0, y_rows)
-            weave_banks(s0, s0 + BLOCK)
-
-        taken_odd = keep.tile([P, SLOTS, BLOCK], F32, name="taken_odd", tag="pair1")
-        places = [w2_raw[:, :, :BLOCK], taken_odd[:]]
-        z_added = keep.tile([P, SLOTS * (HALF - BLOCK)], BF16, name="z_added", align_bytes=64)
-
-        def add_block(b):
-            s0 = HALF + b * BLOCK
-            z_part = nodes(z_turned[0], 0, BLOCK) if b == 0 else nodes(z_added, (b - 1) * BLOCK, BLOCK)
+        def take_block(b, place):
             for t in range(SLOTS):
-                take(places[b % 2][:, t, :], t, s0, BLOCK)
-            nc.vector.tensor_tensor(woven(z_part), planar(places[b % 2]), planar(h_late[:, :, b * BLOCK : (b + 1) * BLOCK]), ADD)
-            z_codes, z_scales = quantise_z(s0, BLOCK, z_part)
+                take(place[:, t, :], t, HALF + b * BLOCK, BLOCK)
+            return place
+
+        def add_block(b, place):
+            z_block = aligned([P, SLOTS * BLOCK], BF16, "z_added%d" % b)
+            nc.vector.tensor_tensor(woven(z_block[:]), planar(place), planar(h_late[:, :, b * BLOCK : (b + 1) * BLOCK]), ADD)
+            return z_block
+
+        def codes_of(s0, z_block, on=None):
+            z_codes, z_scales = quantise_z(s0, BLOCK, z_block[:], on)
             return z_codes[:], z_scales[:]
 
-        y_third = keep.tile([P, SLOTS, QUARTER], F32, name="y_third")
+        def place_on(name, b):
+            return aligned([P, SLOTS, BLOCK], F32, "place%d" % b, on=name)[:]
+
+        def rows(tile, e):
+            return tile[:, :, e * BLOCK : (e + 1) * BLOCK]
+
+        y_rows = [keep.tile([P, SLOTS, QUARTER], F32, name="y_rows%d" % c) for c in range(3)]
+        place = take_block(0, w2_raw[:, :, :BLOCK])
+        quantise_w2(w2_second, 0)
+        z_fifth = add_block(0, place)
         for b in range(2):
-            y_banks[HALF + b * BLOCK] = multiply(*add_block(b), y_third[:, :, b * BLOCK : (b + 1) * BLOCK], 0)
-        store_rows(nc.sync, HALF, y_third)
+            y_banks[b * BLOCK] = multiply(*codes_of(b * BLOCK, z_first[b]), rows(y_rows[0], b), 0)
+        store_rows(nc.sync, 0, y_rows[0])
+        weave_banks(0, BLOCK)
+
+        place = take_block(1, place_on("z_first0", 1))
+        fifth = codes_of(HALF, z_fifth, "z_first1")
+        z_sixth = add_block(1, place)
+        z_codes, z_scales = quantise_z(QUARTER, QUARTER, z_second[:])
+        for b in range(2):
+            block = slice(b * BLOCK, (b + 1) * BLOCK)
+            y_banks[QUARTER + b * BLOCK] = multiply(z_codes[:, block], z_scales[:, block], rows(y_rows[1], b), 0)
+        store_rows(nc.sync, QUARTER, y_rows[1])
+        weave_banks(QUARTER, QUARTER + BLOCK)
+
+        y_banks[HALF] = multiply(*fifth, rows(y_rows[2], 0), 0)
+        y_banks[HALF + BLOCK] = multiply(*codes_of(HALF + BLOCK, z_sixth), rows(y_rows[2], 1), 0)
+        store_rows(nc.sync, HALF, y_rows[2])
         weave_banks(HALF)
+
+        z_seventh = add_block(2, take_block(2, place_on("z_second", 2)))
+        place = take_block(3, place_on("z_added1", 3))
         y_before_last = keep.tile([P, SLOTS, BLOCK], F32, name="y_before_last")
-        multiply(*add_block(2), y_before_last[:], 0)
+        multiply(*codes_of(LAST - BLOCK, z_seventh), y_before_last[:], 0)
         store_rows(nc.sync, LAST - BLOCK, y_before_last)
         weave_banks(HALF + BLOCK)
 
         y_last = keep.tile([P, SLOTS, BLOCK], F32, name="y_last")
-        z_codes, z_scales = add_block(3)
+        z_codes, z_scales = codes_of(LAST, add_block(3, place))
         for first_slot in (0, 2):
             multiply(z_codes, z_scales, y_last[:, first_slot : first_slot + 2, :], first_slot)
         store_rows(nc.scalar, LAST, y_last)

@@ -81,49 +81,57 @@ def tile_picked_treeup_relu_lo_kernel(tc, xT, w1, w2, share, offs, par, out_0, o
         x_view = xT.rearrange("(p t) s -> t p s", t=SLOTS)
         nc.sync.dma_start(x_rows[0][:], x_view[0])
         nc.sync.dma_start(offs_sb[:], offs)
-        share_cols = keep.tile([P, S // P], F32, name="share_cols")
-        nc.sync.dma_start(share_cols[:], share[0].rearrange("(p b) -> p b", p=P))
         for t in range(1, SLOTS):
             nc.sync.dma_start(x_rows[t][:], x_view[t])
         nc.sync.dma_start(w1_raw[:], w1.rearrange("(p j) c -> p j c", j=SLOTS))
+        nc.sync.dma_start(par_sb[:], par)
         w2_view = w2.rearrange("(g t r) c -> t g r c", t=SLOTS, r=8)
         for t in range(SLOTS):
             nc.sync.dma_start(w2_raw[:, t, :], w2_view[t])
-        nc.sync.dma_start(par_sb[:], par)
+        for s0 in (0, HALF):
+            nc.sync.dma_start(share_sb[:, s0 : s0 + HALF], share[:, s0 : s0 + HALF])
+
+        warm_in = keep.tile([P, 1], F32, name="warm_in")
+        warm_out = keep.tile([P, 1], F32, name="warm_out")
+        nc.vector.memset(warm_in[:], 0.0)
+        nc.scalar.activation(warm_out[:], warm_in[:], COPY)
 
         identity = keep.tile([P, P], F32, name="identity")
         make_identity(nc, identity[:])
-        share_view = share_sb[:].rearrange("p (n u b) -> p u n b", u=2, b=4)
-        for u in range(2):
-            spread = next_bank([P, 4, P])
-            for b in range(4):
-                column = share_cols[:, 4 * u + b : 4 * u + b + 1]
-                nc.tensor.transpose(spread[:, b, :], column.to_broadcast([P, P]), identity[:])
-            nc.scalar.copy(share_view[:, u], spread[:].rearrange("p b n -> p n b"))
-
-        picked = keep.tile([P, SLOTS, S], BF16, name="picked", align_bytes=64)
-        x_rounded = keep.tile([P, T], BF16, name="x_rounded")
-        nc.scalar.activation(x_rounded[:], x_rows[1][:], COPY)
-        nc.scalar.activation(picked[:, 1, S - QUARTER :], x_rounded[:].indirect(entries(offs_sb, S - QUARTER, QUARTER)), COPY)
-        for t, count in enumerate((S, S - QUARTER, S)):
-            nc.vector.tensor_copy(picked[:, t, :count], x_rows[t][:].indirect(entries(offs_sb, 0, count)))
-        for s0 in range(0, S, QUARTER):
-            nc.vector.tensor_copy(picked[:, SLOTS - 1, s0 : s0 + QUARTER], x_rows[SLOTS - 1][:].indirect(entries(offs_sb, s0, QUARTER)))
 
         def aligned(shape, dtype, name, on=None):
             return keep.tile(shape, dtype, name=name, tag=on or name, align_bytes=64)
 
+        picked = aligned([P, SLOTS, S - QUARTER], BF16, "picked")
         x_woven = [aligned([P, SLOTS * HALF], BF16, "x_woven%d" % u) for u in range(2)]
-        for q, copy in enumerate((nc.scalar.copy, nc.scalar.copy, nc.vector.tensor_copy, nc.vector.tensor_copy)):
-            copy(woven(nodes(x_woven[q // 2], q % 2 * QUARTER, QUARTER)), planar(picked[:, :, q * QUARTER : (q + 1) * QUARTER]))
+
+        def places(t, s0, count):
+            return nodes(x_woven[s0 // HALF], s0 % HALF, count).rearrange("p (s t) -> p t s", t=SLOTS)[:, t, :]
+
+        for t in range(SLOTS):
+            if t < SLOTS - 1:
+                direct = HALF - BLOCK
+                pieces = ((HALF, QUARTER), (S - QUARTER, QUARTER), (direct, BLOCK))
+            else:
+                direct = QUARTER
+                pieces = ((QUARTER, QUARTER), (HALF, QUARTER), (S - QUARTER, QUARTER))
+            nc.vector.tensor_copy(places(t, 0, direct), x_rows[t][:].indirect(entries(offs_sb, 0, direct)))
+            for s0, count in pieces:
+                piece = picked[:, t, s0 - QUARTER : s0 - QUARTER + count]
+                nc.scalar.activation(piece, x_rows[t][:].indirect(entries(offs_sb, s0, count)), COPY)
+                nc.vector.tensor_copy(places(t, s0, count), piece)
 
         w1_columns = w1_raw[:].rearrange("p j (g t h r) -> p t g h j r", t=SLOTS, h=2, r=4)
         w1_codes = aligned([P, H], U32, "w1_codes")
         w1_scales = aligned([P, H], U8, "w1_scales")
-        w1_dealt = [aligned([P, SLOTS * P * n], BF16, "w1_dealt%d" % t) for t, n in enumerate((1, 1, 2))]
-        for t in range(SLOTS):
+        w1_dealt = [aligned([P, SLOTS * P], BF16, "w1_dealt%d" % t) for t in range(2)]
+
+        def deal_w1(copy, t):
             dealt = nodes(w1_dealt[min(t, 2)], max(t - 2, 0) * P, P)
-            nc.scalar.copy(dealt.rearrange("p (g h r j) -> p g h j r", h=2, r=4, j=SLOTS), w1_columns[:, t])
+            copy(dealt.rearrange("p (g h r j) -> p g h j r", h=2, r=4, j=SLOTS), w1_columns[:, t])
+
+        deal_w1(nc.scalar.copy, 0)
+        deal_w1(nc.scalar.copy, 1)
 
         def quantise_w1(t, slots):
             cols = slice(t * P, (t + slots) * P)
@@ -133,17 +141,19 @@ def tile_picked_treeup_relu_lo_kernel(tc, xT, w1, w2, share, offs, par, out_0, o
         x_scales = [aligned([P, HALF], U8, "x_scales0")]
         quantise(x_codes[0][:], x_scales[0][:], x_woven[0][:])
         quantise_w1(0, 1)
-        x_codes.append(aligned([P, HALF], U32, "x_codes1", on="x_woven0"))
+        x_codes.append(aligned([P, HALF], U32, "x_codes1", on="w1_dealt0"))
         x_scales.append(aligned([P, HALF], U8, "x_scales1"))
         quantise(x_codes[1][:], x_scales[1][:], x_woven[1][:])
         quantise_w1(1, 1)
-        quantise_w1(2, 2)
+        w1_dealt.append(aligned([P, 2 * SLOTS * P], BF16, "w1_dealt2", on="w1_dealt1"))
+        deal_w1(nc.vector.tensor_copy, 2)
+        deal_w1(nc.vector.tensor_copy, 3)
 
         w2_codes = aligned([P, H], U32, "w2_codes")
         w2_scales = aligned([P, H], U8, "w2_scales")
+        quantise_w1(2, 2)
         w2_first = aligned([P, 2 * P * SLOTS], BF16, "w2_first")
         deal_w2(nc.vector.tensor_copy, w2_first, 1)
-        quantise_w2(w2_first, 1)
 
         h_rows = [keep.tile([P, S], F32, name="h_rows%d" % t) for t in range(SLOTS)]
         h_late = keep.tile([P, SLOTS, HALF], F32, name="h_late")
@@ -173,12 +183,12 @@ def tile_picked_treeup_relu_lo_kernel(tc, xT, w1, w2, share, offs, par, out_0, o
                 nc.tensor.matmul(place, taken[:, b0 : b0 + BLOCK], identity[:], start=False, stop=True, is_transpose=True)
 
         for t in range(2):
-            wide = keep.tile([P, HALF], F32, name="taken_wide%d" % t)
+            wide = aligned([P, HALF], F32, "taken_wide%d" % t)
             take_and_add(wide[:], t, 0, HALF)
-        for t, s0 in ((2, 0), (3, 0), (3, QUARTER)):
+        quantise_w2(w2_first, 1)
+        for t, s0 in ((2, 0), (2, QUARTER), (3, 0), (3, QUARTER)):
             narrow = keep.tile([P, QUARTER], F32, name="taken_narrow%d_%d" % (t, s0))
             take_and_add(narrow[:], t, s0, QUARTER)
-        take_and_add(w2_raw[:, SLOTS - 1, QUARTER:], 2, QUARTER, QUARTER)
 
         def round_and_turn(b, pair, back):
             nc.scalar.copy(pair[:].rearrange("s (u p e) -> s u p e", u=2, e=2), sums[b][:].rearrange("s (u e) p -> s u p e", e=2))
@@ -231,7 +241,7 @@ def tile_picked_treeup_relu_lo_kernel(tc, xT, w1, w2, share, offs, par, out_0, o
             queue.dma_start(y_view[:, :, s0 : s0 + y_rows.shape[2]], y_rows[:])
 
         def weave_rows(s0, y_rows):
-            nc.vector.tensor_copy(woven(nodes(y_woven, s0, BLOCK)), planar(y_rows[:]))
+            nc.vector.tensor_copy(woven(nodes(y_woven, s0, BLOCK)), planar(y_rows))
 
         def quantise_y(s0, count):
             quantise(y_codes[:, s0 : s0 + count], y_scales[:, s0 : s0 + count], nodes(y_woven, s0, count))
@@ -288,7 +298,6 @@ def tile_picked_treeup_relu_lo_kernel(tc, xT, w1, w2, share, offs, par, out_0, o
         y_before_last = keep.tile([P, SLOTS, BLOCK], F32, name="y_before_last")
         multiply(*codes_of(LAST - BLOCK, z_seventh), y_before_last[:], 0)
         store_rows(nc.sync, LAST - BLOCK, y_before_last)
-        weave_banks(HALF + BLOCK)
 
         y_last = keep.tile([P, SLOTS, BLOCK], F32, name="y_last")
         z_codes, z_scales = codes_of(LAST, add_block(3, place))
@@ -298,9 +307,11 @@ def tile_picked_treeup_relu_lo_kernel(tc, xT, w1, w2, share, offs, par, out_0, o
 
         for s0 in range(0, S - QUARTER, QUARTER):
             quantise_y(s0, QUARTER)
+            if s0 == QUARTER:
+                weave_rows(HALF + BLOCK, rows(y_rows[2], 1))
         store_words(0, S - QUARTER)
-        weave_rows(LAST - BLOCK, y_before_last)
-        weave_rows(LAST, y_last)
+        weave_rows(LAST - BLOCK, y_before_last[:])
+        weave_rows(LAST, y_last[:])
         quantise_y(S - QUARTER, QUARTER)
         store_words(S - QUARTER, QUARTER)
 

@@ -81,15 +81,15 @@ def tile_picked_treeup_relu_lo_kernel(tc, xT, w1, w2, share, offs, par, out_0, o
         x_view = xT.rearrange("(p t) s -> t p s", t=SLOTS)
         nc.sync.dma_start(x_rows[0][:], x_view[0])
         nc.sync.dma_start(offs_sb[:], offs)
+        share_cols = keep.tile([P, S // P], F32, name="share_cols")
+        nc.sync.dma_start(share_cols[:], share[0].rearrange("(p b) -> p b", p=P))
         for t in range(1, SLOTS):
             nc.sync.dma_start(x_rows[t][:], x_view[t])
         nc.sync.dma_start(w1_raw[:], w1.rearrange("(p j) c -> p j c", j=SLOTS))
-        nc.sync.dma_start(par_sb[:], par)
         w2_view = w2.rearrange("(g t r) c -> t g r c", t=SLOTS, r=8)
         for t in range(SLOTS):
             nc.sync.dma_start(w2_raw[:, t, :], w2_view[t])
-        for s0 in (0, HALF):
-            nc.sync.dma_start(share_sb[:, s0 : s0 + HALF], share[:, s0 : s0 + HALF])
+        nc.sync.dma_start(par_sb[:], par)
 
         warm_in = keep.tile([P, 1], F32, name="warm_in")
         warm_out = keep.tile([P, 1], F32, name="warm_out")
@@ -99,39 +99,53 @@ def tile_picked_treeup_relu_lo_kernel(tc, xT, w1, w2, share, offs, par, out_0, o
         identity = keep.tile([P, P], F32, name="identity")
         make_identity(nc, identity[:])
 
+        share_view = share_sb[:].rearrange("p (n u b) -> p u n b", u=2, b=4)
+        for u in range(2):
+            spread = next_bank([P, 4, P])
+            for b in range(4):
+                column = share_cols[:, 4 * u + b : 4 * u + b + 1]
+                nc.tensor.transpose(spread[:, b, :], column.to_broadcast([P, P]), identity[:])
+            nc.scalar.copy(share_view[:, u], spread[:].rearrange("p b n -> p n b"))
+
         def aligned(shape, dtype, name, on=None):
             return keep.tile(shape, dtype, name=name, tag=on or name, align_bytes=64)
 
-        picked = aligned([P, SLOTS, S - QUARTER], BF16, "picked")
+        picked = aligned([P, SLOTS, S], BF16, "picked")
+
+        def pick_on_vector(t, s0, count):
+            nc.vector.tensor_copy(picked[:, t, s0 : s0 + count], x_rows[t][:].indirect(entries(offs_sb, s0, count)))
+
+        def pick_on_scalar(t, s0, count):
+            nc.scalar.activation(picked[:, t, s0 : s0 + count], x_rows[t][:].indirect(entries(offs_sb, s0, count)), COPY)
+
+        for t in range(SLOTS - 1):
+            pick_on_vector(t, 0, S - QUARTER)
+            pick_on_scalar(t, S - QUARTER, QUARTER)
+        pick_on_vector(SLOTS - 1, 0, QUARTER)
+        for s0 in range(QUARTER, S, QUARTER):
+            pick_on_scalar(SLOTS - 1, s0, QUARTER)
+
         x_woven = [aligned([P, SLOTS * HALF], BF16, "x_woven%d" % u) for u in range(2)]
 
-        def places(t, s0, count):
-            return nodes(x_woven[s0 // HALF], s0 % HALF, count).rearrange("p (s t) -> p t s", t=SLOTS)[:, t, :]
+        def weave_x(copy, s0, count):
+            copy(woven(nodes(x_woven[s0 // HALF], s0 % HALF, count)), planar(picked[:, :, s0 : s0 + count]))
 
-        for t in range(SLOTS):
-            if t < SLOTS - 1:
-                direct = HALF - BLOCK
-                pieces = ((HALF, QUARTER), (S - QUARTER, QUARTER), (direct, BLOCK))
-            else:
-                direct = QUARTER
-                pieces = ((QUARTER, QUARTER), (HALF, QUARTER), (S - QUARTER, QUARTER))
-            nc.vector.tensor_copy(places(t, 0, direct), x_rows[t][:].indirect(entries(offs_sb, 0, direct)))
-            for s0, count in pieces:
-                piece = picked[:, t, s0 - QUARTER : s0 - QUARTER + count]
-                nc.scalar.activation(piece, x_rows[t][:].indirect(entries(offs_sb, s0, count)), COPY)
-                nc.vector.tensor_copy(places(t, s0, count), piece)
+        for s0 in range(0, S - QUARTER, QUARTER):
+            weave_x(nc.vector.tensor_copy, s0, QUARTER)
+        weave_x(nc.scalar.copy, LAST, BLOCK)
+        weave_x(nc.vector.tensor_copy, LAST - BLOCK, BLOCK)
 
         w1_columns = w1_raw[:].rearrange("p j (g t h r) -> p t g h j r", t=SLOTS, h=2, r=4)
         w1_codes = aligned([P, H], U32, "w1_codes")
         w1_scales = aligned([P, H], U8, "w1_scales")
-        w1_dealt = [aligned([P, SLOTS * P], BF16, "w1_dealt%d" % t) for t in range(2)]
+        w1_dealt = [aligned([P, SLOTS * P], BF16, "w1_dealt%d" % t) for t in range(SLOTS - 1)]
 
         def deal_w1(copy, t):
-            dealt = nodes(w1_dealt[min(t, 2)], max(t - 2, 0) * P, P)
-            copy(dealt.rearrange("p (g h r j) -> p g h j r", h=2, r=4, j=SLOTS), w1_columns[:, t])
+            copy(w1_dealt[t][:].rearrange("p (g h r j) -> p g h j r", h=2, r=4, j=SLOTS), w1_columns[:, t])
 
         deal_w1(nc.scalar.copy, 0)
         deal_w1(nc.scalar.copy, 1)
+        deal_w1(nc.scalar.copy, 2)
 
         def quantise_w1(t, slots):
             cols = slice(t * P, (t + slots) * P)
@@ -145,13 +159,12 @@ def tile_picked_treeup_relu_lo_kernel(tc, xT, w1, w2, share, offs, par, out_0, o
         x_scales.append(aligned([P, HALF], U8, "x_scales1"))
         quantise(x_codes[1][:], x_scales[1][:], x_woven[1][:])
         quantise_w1(1, 1)
-        w1_dealt.append(aligned([P, 2 * SLOTS * P], BF16, "w1_dealt2", on="w1_dealt1"))
-        deal_w1(nc.vector.tensor_copy, 2)
+        w1_dealt.append(aligned([P, SLOTS * P], BF16, "w1_dealt3", on="w1_dealt1"))
         deal_w1(nc.vector.tensor_copy, 3)
+        quantise_w1(2, 1)
 
-        w2_codes = aligned([P, H], U32, "w2_codes")
         w2_scales = aligned([P, H], U8, "w2_scales")
-        quantise_w1(2, 2)
+        quantise_w1(3, 1)
         w2_first = aligned([P, 2 * P * SLOTS], BF16, "w2_first")
         deal_w2(nc.vector.tensor_copy, w2_first, 1)
 
@@ -185,10 +198,11 @@ def tile_picked_treeup_relu_lo_kernel(tc, xT, w1, w2, share, offs, par, out_0, o
         for t in range(2):
             wide = aligned([P, HALF], F32, "taken_wide%d" % t)
             take_and_add(wide[:], t, 0, HALF)
-        quantise_w2(w2_first, 1)
         for t, s0 in ((2, 0), (2, QUARTER), (3, 0), (3, QUARTER)):
-            narrow = keep.tile([P, QUARTER], F32, name="taken_narrow%d_%d" % (t, s0))
+            narrow = aligned([P, QUARTER], F32, "taken_narrow%d_%d" % (t, s0))
             take_and_add(narrow[:], t, s0, QUARTER)
+        w2_codes = aligned([P, H], U32, "w2_codes", on="taken_narrow3_0")
+        quantise_w2(w2_first, 1)
 
         def round_and_turn(b, pair, back):
             nc.scalar.copy(pair[:].rearrange("s (u p e) -> s u p e", u=2, e=2), sums[b][:].rearrange("s (u e) p -> s u p e", e=2))

@@ -91,11 +91,6 @@ def tile_picked_treeup_relu_lo_kernel(tc, xT, w1, w2, share, offs, par, out_0, o
             nc.sync.dma_start(w2_raw[:, t, :], w2_view[t])
         nc.sync.dma_start(par_sb[:], par)
 
-        warm_in = keep.tile([P, 1], F32, name="warm_in")
-        warm_out = keep.tile([P, 1], F32, name="warm_out")
-        nc.vector.memset(warm_in[:], 0.0)
-        nc.scalar.activation(warm_out[:], warm_in[:], COPY)
-
         identity = keep.tile([P, P], F32, name="identity")
         make_identity(nc, identity[:])
 
@@ -312,6 +307,7 @@ def tile_picked_treeup_relu_lo_kernel(tc, xT, w1, w2, share, offs, par, out_0, o
         y_before_last = keep.tile([P, SLOTS, BLOCK], F32, name="y_before_last")
         multiply(*codes_of(LAST - BLOCK, z_seventh), y_before_last[:], 0)
         store_rows(nc.sync, LAST - BLOCK, y_before_last)
+        weave_banks(HALF + BLOCK)
 
         y_last = keep.tile([P, SLOTS, BLOCK], F32, name="y_last")
         z_codes, z_scales = codes_of(LAST, add_block(3, place))
@@ -321,8 +317,6 @@ def tile_picked_treeup_relu_lo_kernel(tc, xT, w1, w2, share, offs, par, out_0, o
 
         for s0 in range(0, S - QUARTER, QUARTER):
             quantise_y(s0, QUARTER)
-            if s0 == QUARTER:
-                weave_rows(HALF + BLOCK, rows(y_rows[2], 1))
         store_words(0, S - QUARTER)
         weave_rows(LAST - BLOCK, y_before_last[:])
         weave_rows(LAST, y_last[:])

@@ -25,6 +25,7 @@ HALF = S // 2
 QUARTER = S // 4
 BLOCK = 128
 BANKS = 8
+EARLY = S - QUARTER
 LAST = S - BLOCK
 
 
@@ -50,6 +51,12 @@ def tile_picked_treeup_relu_lo_kernel(tc, xT, w1, w2, share, offs, par, out_0, o
         keep = ctx.enter_context(tc.tile_pool(name="keep", bufs=1))
         psum = ctx.enter_context(tc.psum_pool(name="psum", bufs=1))
 
+        def tile(shape, dtype, name, on=None):
+            return keep.tile(shape, dtype, name=name, tag=on or name, align_bytes=64)
+
+        def bank(number, shape):
+            return psum.tile(shape, F32, name="bank", tag="bank%d" % number)
+
         def quantise(codes, scales, values):
             nc.vector.quantize_mx(out=codes.bitcast(FP8X4), scales=scales, in_=values)
 
@@ -58,31 +65,18 @@ def tile_picked_treeup_relu_lo_kernel(tc, xT, w1, w2, share, offs, par, out_0, o
                 out=out, lhsT=w_codes.bitcast(FP8X4), lhsT_scale=w_scales, rhs=codes.bitcast(FP8X4), rhs_scale=scales, start=True, stop=True
             )
 
-        def deal_w2(copy, dealt, half):
-            columns = w2_raw[:].rearrange("p j (m u e) -> p u m j e", u=2, e=2)
-            copy(dealt[:].rearrange("p (e m j) -> p m j e", e=2, j=SLOTS), columns[:, half])
-
-        def quantise_w2(dealt, half):
-            cols = slice(half * H // 2, (half + 1) * H // 2)
-            quantise(w2_codes[:, cols], w2_scales[:, cols], dealt[:])
-
-        banks_taken = []
-
-        def next_bank(shape):
-            banks_taken.append(shape)
-            return psum.tile(shape, F32, name="bank", tag="bank%d" % (len(banks_taken) % BANKS))
-
         offs_sb = keep.tile([P, S // LIST_COL], U16, name="offs_sb")
         par_sb = keep.tile([P, S // LIST_COL], U16, name="par_sb")
-        x_rows = [keep.tile([P, T], F32, name="x_rows%d" % t) for t in range(SLOTS)]
-        w1_raw = keep.tile([P, SLOTS, H], F32, name="w1_raw")
-        w2_raw = keep.tile([P, SLOTS, H], F32, name="w2_raw")
-        share_sb = keep.tile([P, S], F32, name="share_sb")
+        x_rows = [tile([P, T], F32, "x_rows%d" % t) for t in range(SLOTS)]
+        w1_raw = tile([P, SLOTS, H], F32, "w1_raw")
+        w2_raw = tile([P, SLOTS, H], F32, "w2_raw")
+        share_early = [tile([P, 4], F32, "share_first"), tile([P, 2], F32, "share_third")]
+        share_late = tile([P, QUARTER // P], F32, "share_late")
         x_view = xT.rearrange("(p t) s -> t p s", t=SLOTS)
         nc.sync.dma_start(x_rows[0][:], x_view[0])
         nc.sync.dma_start(offs_sb[:], offs)
-        share_cols = keep.tile([P, S // P], F32, name="share_cols")
-        nc.sync.dma_start(share_cols[:], share[0].rearrange("(p b) -> p b", p=P))
+        nc.sync.dma_start(share_early[0][:], share[0, :HALF].rearrange("(p b) -> p b", p=P))
+        nc.sync.dma_start(share_early[1][:], share[0, EARLY:].rearrange("(p b) -> p b", p=P))
         for t in range(1, SLOTS):
             nc.sync.dma_start(x_rows[t][:], x_view[t])
         nc.sync.dma_start(w1_raw[:], w1.rearrange("(p j) c -> p j c", j=SLOTS))
@@ -90,22 +84,21 @@ def tile_picked_treeup_relu_lo_kernel(tc, xT, w1, w2, share, offs, par, out_0, o
         for t in range(SLOTS):
             nc.sync.dma_start(w2_raw[:, t, :], w2_view[t])
         nc.sync.dma_start(par_sb[:], par)
+        nc.sync.dma_start(share_late[:], share[0, HALF:EARLY].rearrange("(b p) -> p b", p=P), allow_slow_non_contiguous=True)
 
-        identity = keep.tile([P, P], F32, name="identity")
+        identity = tile([P, P], F32, "identity")
         make_identity(nc, identity[:])
 
-        share_view = share_sb[:].rearrange("p (n u b) -> p u n b", u=2, b=4)
-        for u in range(2):
-            spread = next_bank([P, 4, P])
-            for b in range(4):
-                column = share_cols[:, 4 * u + b : 4 * u + b + 1]
-                nc.tensor.transpose(spread[:, b, :], column.to_broadcast([P, P]), identity[:])
-            nc.scalar.copy(share_view[:, u], spread[:].rearrange("p b n -> p n b"))
+        share_row = tile([P, S], F32, "share_row")
+        for u, columns in enumerate(share_early):
+            width = columns.shape[1]
+            spread = bank(u, [P, width, P])
+            for b in range(width):
+                nc.tensor.transpose(spread[:, b, :], columns[:, b : b + 1].to_broadcast([P, P]), identity[:])
+            part = share_row[:, u * EARLY : u * EARLY + width * P]
+            nc.scalar.copy(part.rearrange("p (n b) -> p n b", b=width), spread[:].rearrange("p b n -> p n b"))
 
-        def aligned(shape, dtype, name, on=None):
-            return keep.tile(shape, dtype, name=name, tag=on or name, align_bytes=64)
-
-        picked = aligned([P, SLOTS, S], BF16, "picked")
+        picked = tile([P, SLOTS, S], BF16, "picked")
 
         def pick_on_vector(t, s0, count):
             nc.vector.tensor_copy(picked[:, t, s0 : s0 + count], x_rows[t][:].indirect(entries(offs_sb, s0, count)))
@@ -120,7 +113,7 @@ def tile_picked_treeup_relu_lo_kernel(tc, xT, w1, w2, share, offs, par, out_0, o
         for s0 in range(QUARTER, S, QUARTER):
             pick_on_scalar(SLOTS - 1, s0, QUARTER)
 
-        x_woven = [aligned([P, SLOTS * HALF], BF16, "x_woven%d" % u) for u in range(2)]
+        x_woven = [tile([P, SLOTS * HALF], BF16, "x_woven%d" % u) for u in range(2)]
 
         def weave_x(copy, s0, count):
             copy(woven(nodes(x_woven[s0 // HALF], s0 % HALF, count)), planar(picked[:, :, s0 : s0 + count]))
@@ -131,126 +124,148 @@ def tile_picked_treeup_relu_lo_kernel(tc, xT, w1, w2, share, offs, par, out_0, o
         weave_x(nc.vector.tensor_copy, LAST - BLOCK, BLOCK)
 
         w1_columns = w1_raw[:].rearrange("p j (g t h r) -> p t g h j r", t=SLOTS, h=2, r=4)
-        w1_codes = aligned([P, H], U32, "w1_codes")
-        w1_scales = aligned([P, H], U8, "w1_scales")
-        w1_dealt = [aligned([P, SLOTS * P], BF16, "w1_dealt%d" % t) for t in range(SLOTS - 1)]
+        w1_codes = tile([P, H], U32, "w1_codes")
+        w1_scales = tile([P, H], U8, "w1_scales")
+        w1_dealt = [tile([P, SLOTS * P], BF16, "w1_dealt%d" % t) for t in range(SLOTS - 1)]
 
         def deal_w1(copy, t):
             copy(w1_dealt[t][:].rearrange("p (g h r j) -> p g h j r", h=2, r=4, j=SLOTS), w1_columns[:, t])
 
-        deal_w1(nc.scalar.copy, 0)
-        deal_w1(nc.scalar.copy, 1)
-        deal_w1(nc.scalar.copy, 2)
-
-        def quantise_w1(t, slots):
-            cols = slice(t * P, (t + slots) * P)
+        def quantise_w1(t):
+            cols = slice(t * P, (t + 1) * P)
             quantise(w1_codes[:, cols], w1_scales[:, cols], w1_dealt[t][:])
 
-        x_codes = [aligned([P, HALF], U32, "x_codes0")]
-        x_scales = [aligned([P, HALF], U8, "x_scales0")]
+        def deal_w2(copy, dealt, half):
+            columns = w2_raw[:].rearrange("p j (m u e) -> p u m j e", u=2, e=2)
+            copy(dealt[:].rearrange("p (e m j) -> p m j e", e=2, j=SLOTS), columns[:, half])
+
+        def quantise_w2(dealt, half):
+            cols = slice(half * H // 2, (half + 1) * H // 2)
+            quantise(w2_codes[:, cols], w2_scales[:, cols], dealt[:])
+
+        for t in range(SLOTS - 1):
+            deal_w1(nc.scalar.copy, t)
+        x_codes = [tile([P, HALF], U32, "x_codes0")]
+        x_scales = [tile([P, HALF], U8, "x_scales%d" % u) for u in range(2)]
         quantise(x_codes[0][:], x_scales[0][:], x_woven[0][:])
-        quantise_w1(0, 1)
-        x_codes.append(aligned([P, HALF], U32, "x_codes1", on="w1_dealt0"))
-        x_scales.append(aligned([P, HALF], U8, "x_scales1"))
+        quantise_w1(0)
+        x_codes.append(tile([P, HALF], U32, "x_codes1", on="w1_dealt0"))
         quantise(x_codes[1][:], x_scales[1][:], x_woven[1][:])
-        quantise_w1(1, 1)
-        w1_dealt.append(aligned([P, SLOTS * P], BF16, "w1_dealt3", on="w1_dealt1"))
+        quantise_w1(1)
+        w1_dealt.append(tile([P, SLOTS * P], BF16, "w1_dealt3", on="w1_dealt1"))
         deal_w1(nc.vector.tensor_copy, 3)
-        quantise_w1(2, 1)
+        quantise_w1(2)
+        quantise_w1(3)
+        w2_upper = tile([P, 2 * P * SLOTS], BF16, "w2_upper")
+        deal_w2(nc.vector.tensor_copy, w2_upper, 1)
 
-        w2_scales = aligned([P, H], U8, "w2_scales")
-        quantise_w1(3, 1)
-        w2_first = aligned([P, 2 * P * SLOTS], BF16, "w2_first")
-        deal_w2(nc.vector.tensor_copy, w2_first, 1)
-
-        h_rows = [keep.tile([P, S], F32, name="h_rows%d" % t) for t in range(SLOTS)]
-        h_late = keep.tile([P, SLOTS, HALF], F32, name="h_late")
+        h_rows = [tile([P, S], F32, "h_rows%d" % t) for t in range(SLOTS)]
+        planes = tile([P, 2 * SLOTS, HALF], F32, "planes")
+        own = [planes[:, :SLOTS, :], planes[:, SLOTS:, :]]
+        taken_last = planes[:, 2 : 2 + SLOTS, :QUARTER]
         for t in range(SLOTS):
             w_cols = slice(t * P, (t + 1) * P)
             for u in range(2):
                 cols = slice(u * HALF, (u + 1) * HALF)
-                bank = next_bank([P, HALF])
-                product(bank[:], w1_codes[:, w_cols], w1_scales[:, w_cols], x_codes[u][:], x_scales[u][:])
-                nc.scalar.activation(h_rows[t][:, cols], bank[:], RELU)
-            nc.sync.dma_start(h_late[:, t, :], h_rows[t][:, HALF:])
+                sums = bank(2 * t + u, [P, HALF])
+                product(sums[:], w1_codes[:, w_cols], w1_scales[:, w_cols], x_codes[u][:], x_scales[u][:])
+                nc.scalar.activation(h_rows[t][:, cols], sums[:], RELU)
+                skip = QUARTER if (t, u) == (SLOTS - 1, 0) else 0
+                nc.sync.dma_start(own[u][:, t, skip:], h_rows[t][:, u * HALF + skip : (u + 1) * HALF])
 
-        w2_second = keep.tile([P, 2 * P * SLOTS], BF16, name="w2_second", tag="w1_codes", align_bytes=64)
-        deal_w2(nc.scalar.copy, w2_second, 0)
+        w2_lower = tile([P, 2 * P * SLOTS], BF16, "w2_lower", on="w1_codes")
+        deal_w2(nc.scalar.copy, w2_lower, 0)
 
         def take(out, t, s0, count):
-            nc.vector.tensor_tensor(out, h_rows[t][:].indirect(entries(par_sb, s0, count)), share_sb[:, s0 : s0 + count], MULT)
+            nc.vector.tensor_tensor(out, h_rows[t][:].indirect(entries(par_sb, s0, count)), share_row[:, s0 : s0 + count], MULT)
 
-        sums = [next_bank([P, SLOTS, P]) for b in range(HALF // BLOCK)]
-
-        def take_and_add(taken, t, s0, count):
-            take(taken, t, s0, count)
-            for b0 in range(0, count, BLOCK):
-                place = sums[(s0 + b0) // BLOCK][:, t, :]
-                own = h_rows[t][:, s0 + b0 : s0 + b0 + BLOCK]
-                nc.tensor.matmul(place, own, identity[:], start=True, stop=False, is_transpose=True)
-                nc.tensor.matmul(place, taken[:, b0 : b0 + BLOCK], identity[:], start=False, stop=True, is_transpose=True)
-
-        for t in range(2):
-            wide = aligned([P, HALF], F32, "taken_wide%d" % t)
-            take_and_add(wide[:], t, 0, HALF)
-        for t, s0 in ((2, 0), (2, QUARTER), (3, 0), (3, QUARTER)):
-            narrow = aligned([P, QUARTER], F32, "taken_narrow%d_%d" % (t, s0))
-            take_and_add(narrow[:], t, s0, QUARTER)
-        w2_codes = aligned([P, H], U32, "w2_codes", on="taken_narrow3_0")
-        quantise_w2(w2_first, 1)
-
-        def round_and_turn(b, pair, back):
-            nc.scalar.copy(pair[:].rearrange("s (u p e) -> s u p e", u=2, e=2), sums[b][:].rearrange("s (u e) p -> s u p e", e=2))
-            for u in range(2):
-                nc.tensor.transpose(back[:, u, :], pair[:].bitcast(F32)[:, u * P : (u + 1) * P], identity[:])
-
-        def weave_words(back, z_part):
-            nc.scalar.copy(z_part.bitcast(F32).rearrange("p (b s u) -> p b s u", s=BLOCK, u=2), back.rearrange("p b u s -> p b s u"))
-
-        z_first = [aligned([P, SLOTS * BLOCK], BF16, "z_first%d" % b) for b in range(2)]
-        z_second = aligned([P, SLOTS * QUARTER], BF16, "z_second")
-        pairs = [aligned([P, H], BF16, "pair%d" % b) for b in range(3)]
-        back_first = next_bank([P, 2, 2, BLOCK])
-        backs = [next_bank([P, 1, 2, BLOCK]) for b in range(2)]
-        round_and_turn(0, pairs[0], back_first[:, 0])
-        round_and_turn(1, pairs[1], back_first[:, 1])
-        round_and_turn(2, pairs[2], backs[0][:, 0])
-        for b in range(2):
-            weave_words(back_first[:, b : b + 1], z_first[b][:])
-        round_and_turn(3, pairs[1], backs[1][:, 0])
-        for b in range(2):
-            weave_words(backs[b][:], nodes(z_second, b * BLOCK, BLOCK))
+        taken_first = tile([P, SLOTS, HALF], F32, "taken_first")
+        for t in range(SLOTS):
+            if t == SLOTS - 1:
+                nc.vector.tensor_copy(own[0][:, t, :QUARTER], h_rows[t][:, :QUARTER])
+            take(taken_first[:, t, :], t, 0, HALF)
+        w2_codes = tile([P, H], U32, "w2_codes")
+        w2_scales = tile([P, H], U8, "w2_scales")
+        quantise_w2(w2_upper, 1)
 
         y_view = out_0.rearrange("(p t) s -> p t s", t=SLOTS)
         words_view = out_1[0].rearrange("p c r -> p (c r)").bitcast(I32)
-        y_woven = keep.tile([P, SLOTS * S], BF16, name="y_woven", align_bytes=64)
-        y_codes = keep.tile([P, S], U32, name="y_codes", align_bytes=64)
-        y_scales = keep.tile([P, S], U8, name="y_scales", align_bytes=64)
-        y_banks = {}
+        y_woven = tile([P, SLOTS * S], BF16, "y_woven")
+        y_codes = tile([P, S], U32, "y_codes")
+        y_scales = tile([P, S], U8, "y_scales")
 
-        def quantise_z(s0, count, z_part, on=None):
-            z_codes = aligned([P, count], U32, "z_codes%d" % s0, on=on)
-            z_scales = keep.tile([P, count], U8, name="z_scales%d" % s0, align_bytes=64)
-            quantise(z_codes[:], z_scales[:], z_part)
+        def own_part(s0, count):
+            return own[s0 // HALF][:, :, s0 % HALF : s0 % HALF + count]
+
+        def add_early(taken, s0):
+            count = taken.shape[2]
+            z_part = tile([P, SLOTS * count], BF16, "z_early%d" % s0)
+            nc.vector.tensor_tensor(woven(z_part[:]), planar(taken), planar(own_part(s0, count)), ADD)
+            return z_part
+
+        def codes_of(s0, z_part):
+            count = z_part.shape[1] // SLOTS
+            z_codes = tile([P, count], U32, "z_codes%d" % s0)
+            z_scales = tile([P, count], U8, "z_scales%d" % s0)
+            quantise(z_codes[:], z_scales[:], z_part[:])
             return z_codes, z_scales
 
-        def multiply(z_codes, z_scales, y_part, first_slot):
-            bank = next_bank([P, y_part.shape[1], BLOCK])
-            for e in range(y_part.shape[1]):
+        def multiply(z_mx, s0, y_part, first_slot, number):
+            z_codes, z_scales = z_mx
+            slots, count = y_part.shape[1], y_part.shape[2]
+            sums = bank(number, [P, slots, count])
+            for e in range(slots):
                 w_cols = slice((first_slot + e) * P, (first_slot + e + 1) * P)
-                product(bank[:, e, :], w2_codes[:, w_cols], w2_scales[:, w_cols], z_codes, z_scales)
-            nc.scalar.copy(y_part, bank[:])
-            return bank
+                product(sums[:, e, :], w2_codes[:, w_cols], w2_scales[:, w_cols], z_codes[:, s0 : s0 + count], z_scales[:, s0 : s0 + count])
+            nc.scalar.copy(y_part, sums[:])
+            return sums
 
-        def weave_banks(*starts):
-            for s0 in starts:
-                nc.scalar.copy(nodes(y_woven, s0, BLOCK).rearrange("p (s t) -> p s t", t=SLOTS), y_banks[s0][:].rearrange("p t s -> p s t"))
+        def by_blocks(s0, z_mx, banks, queue):
+            count = z_mx[0].shape[1]
+            y_rows = tile([P, SLOTS, count], F32, "y_rows%d" % s0)
+            sums = [multiply(z_mx, b * BLOCK, y_rows[:, :, b * BLOCK : (b + 1) * BLOCK], 0, number) for b, number in enumerate(banks)]
+            queue.dma_start(y_view[:, :, s0 : s0 + count], y_rows[:])
+            return y_rows, sums
 
-        def store_rows(queue, s0, y_rows):
-            queue.dma_start(y_view[:, :, s0 : s0 + y_rows.shape[2]], y_rows[:])
+        def by_slots(s0, z_mx, banks, queue):
+            count = z_mx[0].shape[1]
+            y_rows = tile([P, SLOTS, count], F32, "y_rows%d" % s0)
+            for u, number in enumerate(banks):
+                multiply(z_mx, 0, y_rows[:, 2 * u : 2 * u + 2, :], 2 * u, number)
+            queue.dma_start(y_view[:, :, s0 : s0 + count], y_rows[:])
+            return y_rows
 
-        def weave_rows(s0, y_rows):
-            nc.vector.tensor_copy(woven(nodes(y_woven, s0, BLOCK)), planar(y_rows))
+        def weave_bank(s0, sums):
+            nc.scalar.copy(nodes(y_woven, s0, BLOCK).rearrange("p (s t) -> p s t", t=SLOTS), sums[:].rearrange("p t s -> p s t"))
+
+        def fetch(gather, fetched, t, s0):
+            gather(fetched[t], h_rows[t][:].indirect(entries(par_sb, s0, QUARTER)))
+
+        def gather_on_scalar(out, window):
+            nc.scalar.activation(out, window, COPY)
+
+        def turn(turned, fetched, t):
+            for e in range(2):
+                nc.tensor.transpose(turned[e][:, t, :], fetched[:, e * BLOCK : (e + 1) * BLOCK], identity[:])
+
+        def scale_and_turn_back(turned, b, number, on=None):
+            scaled = tile([P, SLOTS, P], F32, "scaled%d" % b, on=on)
+            nc.scalar.activation(scaled[:], turned[:], COPY, scale=share_late[:, b : b + 1])
+            back = bank(number, [P, SLOTS, BLOCK])
+            for t in range(SLOTS):
+                nc.tensor.transpose(back[:, t, :], scaled[:, t, :], identity[:])
+            return back
+
+        def add_late(z_part, back, b):
+            nc.vector.tensor_tensor(woven(z_part), planar(back[:]), planar(own_part(HALF + b * BLOCK, BLOCK)), ADD)
+
+        def weave_on_gpsimd(y_rows, name, on=None):
+            y_part = tile([P, SLOTS * QUARTER], BF16, name, on=on)
+            nc.gpsimd.tensor_scalar(y_part[:].rearrange("p (s t) -> p s t", t=SLOTS), y_rows[:].rearrange("p t s -> p s t"), 1.0, 0.0, MULT, ADD)
+            return y_part
+
+        def weave(copy, s0, rows):
+            copy(woven(nodes(y_woven, s0, rows.shape[2])), planar(rows))
 
         def quantise_y(s0, count):
             quantise(y_codes[:, s0 : s0 + count], y_scales[:, s0 : s0 + count], nodes(y_woven, s0, count))
@@ -258,70 +273,51 @@ def tile_picked_treeup_relu_lo_kernel(tc, xT, w1, w2, share, offs, par, out_0, o
         def store_words(s0, count):
             nc.sync.dma_start(words_view[:, s0 : s0 + count], y_codes[:, s0 : s0 + count].bitcast(I32))
 
-        def take_block(b, place):
-            for t in range(SLOTS):
-                take(place[:, t, :], t, HALF + b * BLOCK, BLOCK)
-            return place
+        fetched_all = tile([P, SLOTS, QUARTER], F32, "fetched", on="w2_raw")
+        fetched = [fetched_all[:, t, :] for t in range(SLOTS)]
+        turned = [bank(number, [P, SLOTS, P]) for number in (0, 1)]
+        for t in range(SLOTS):
+            fetch(gather_on_scalar, fetched, t, HALF)
+            turn(turned, fetched[t], t)
 
-        def add_block(b, place):
-            z_block = aligned([P, SLOTS * BLOCK], BF16, "z_added%d" % b)
-            nc.vector.tensor_tensor(woven(z_block[:]), planar(place), planar(h_late[:, :, b * BLOCK : (b + 1) * BLOCK]), ADD)
-            return z_block
-
-        def codes_of(s0, z_block, on=None):
-            z_codes, z_scales = quantise_z(s0, BLOCK, z_block[:], on)
-            return z_codes[:], z_scales[:]
-
-        def place_on(name, b):
-            return aligned([P, SLOTS, BLOCK], F32, "place%d" % b, on=name)[:]
-
-        def rows(tile, e):
-            return tile[:, :, e * BLOCK : (e + 1) * BLOCK]
-
-        y_rows = [keep.tile([P, SLOTS, QUARTER], F32, name="y_rows%d" % c) for c in range(3)]
-        place = take_block(0, w2_raw[:, :, :BLOCK])
-        quantise_w2(w2_second, 0)
-        z_fifth = add_block(0, place)
+        z_first = add_early(taken_first[:, :, :BLOCK], 0)
+        quantise_w2(w2_lower, 0)
+        y_first, first_sums = by_blocks(0, codes_of(0, z_first), (2,), nc.sync)
+        z_next = add_early(taken_first[:, :, BLOCK:QUARTER], BLOCK)
+        take(taken_last[:, 0, :], 0, EARLY, QUARTER)
+        next_mx = codes_of(BLOCK, z_next)
+        z_second = add_early(taken_first[:, :, QUARTER:], QUARTER)
+        take(taken_last[:, 1, :], 1, EARLY, QUARTER)
+        second_mx = codes_of(QUARTER, z_second)
+        backs = [scale_and_turn_back(turned[0], 0, 4, on="z_codes0"), scale_and_turn_back(turned[1], 1, 5, on="z_scales0")]
+        y_next, next_sums = by_blocks(BLOCK, next_mx, (3,), nc.sync)
+        weave_bank(0, first_sums[0])
+        weave_bank(BLOCK, next_sums[0])
+        y_second, sums = by_blocks(QUARTER, second_mx, (6, 7), nc.sync)
         for b in range(2):
-            y_banks[b * BLOCK] = multiply(*codes_of(b * BLOCK, z_first[b]), rows(y_rows[0], b), 0)
-        store_rows(nc.sync, 0, y_rows[0])
-        weave_banks(0, BLOCK)
-
-        place = take_block(1, place_on("z_first0", 1))
-        fifth = codes_of(HALF, z_fifth, "z_first1")
-        z_sixth = add_block(1, place)
-        z_codes, z_scales = quantise_z(QUARTER, QUARTER, z_second[:])
+            weave_bank(QUARTER + b * BLOCK, sums[b])
+        z_turned = tile([P, SLOTS * QUARTER], BF16, "z_turned")
         for b in range(2):
-            block = slice(b * BLOCK, (b + 1) * BLOCK)
-            y_banks[QUARTER + b * BLOCK] = multiply(z_codes[:, block], z_scales[:, block], rows(y_rows[1], b), 0)
-        store_rows(nc.sync, QUARTER, y_rows[1])
-        weave_banks(QUARTER, QUARTER + BLOCK)
+            add_late(nodes(z_turned, b * BLOCK, BLOCK), backs[b], b)
+        take(taken_last[:, 2, :], 2, EARLY, QUARTER)
+        y_turned, sums = by_blocks(HALF, codes_of(HALF, z_turned), (0, 1), nc.sync)
+        weave_bank(HALF, sums[0])
+        take(taken_last[:, 3, :], 3, EARLY, QUARTER)
+        quantise_y(0, QUARTER)
+        store_words(0, QUARTER)
+        z_before_last = add_early(taken_last[:, :, :BLOCK], EARLY)
+        z_last = add_early(taken_last[:, :, BLOCK:], LAST)
+        y_before_last, sums = by_blocks(EARLY, codes_of(EARLY, z_before_last), (2,), nc.sync)
+        y_last = by_slots(LAST, codes_of(LAST, z_last), (3, 4), nc.scalar)
 
-        y_banks[HALF] = multiply(*fifth, rows(y_rows[2], 0), 0)
-        y_banks[HALF + BLOCK] = multiply(*codes_of(HALF + BLOCK, z_sixth), rows(y_rows[2], 1), 0)
-        store_rows(nc.sync, HALF, y_rows[2])
-        weave_banks(HALF)
-
-        z_seventh = add_block(2, take_block(2, place_on("z_second", 2)))
-        place = take_block(3, place_on("z_added1", 3))
-        y_before_last = keep.tile([P, SLOTS, BLOCK], F32, name="y_before_last")
-        multiply(*codes_of(LAST - BLOCK, z_seventh), y_before_last[:], 0)
-        store_rows(nc.sync, LAST - BLOCK, y_before_last)
-        weave_banks(HALF + BLOCK)
-
-        y_last = keep.tile([P, SLOTS, BLOCK], F32, name="y_last")
-        z_codes, z_scales = codes_of(LAST, add_block(3, place))
-        for first_slot in (0, 2):
-            multiply(z_codes, z_scales, y_last[:, first_slot : first_slot + 2, :], first_slot)
-        store_rows(nc.scalar, LAST, y_last)
-
-        for s0 in range(0, S - QUARTER, QUARTER):
-            quantise_y(s0, QUARTER)
-        store_words(0, S - QUARTER)
-        weave_rows(LAST - BLOCK, y_before_last[:])
-        weave_rows(LAST, y_last[:])
-        quantise_y(S - QUARTER, QUARTER)
-        store_words(S - QUARTER, QUARTER)
+        weave(nc.vector.tensor_copy, HALF + BLOCK, y_turned[:, :, BLOCK:])
+        quantise_y(QUARTER, QUARTER)
+        quantise_y(HALF, QUARTER)
+        store_words(QUARTER, HALF)
+        weave(nc.vector.tensor_copy, EARLY, y_before_last[:])
+        weave(nc.vector.tensor_copy, LAST, y_last[:])
+        quantise_y(EARLY, QUARTER)
+        store_words(EARLY, QUARTER)
 
         scales_view = out_2[0].bitcast(I32)
         for q in range(4):

@@ -70,13 +70,12 @@ def tile_picked_treeup_relu_lo_kernel(tc, xT, w1, w2, share, offs, par, out_0, o
         x_rows = [tile([P, T], F32, "x_rows%d" % t) for t in range(SLOTS)]
         w1_raw = tile([P, SLOTS, H], F32, "w1_raw")
         w2_raw = tile([P, SLOTS, H], F32, "w2_raw")
-        share_early = [tile([P, 4], F32, "share_first"), tile([P, 2], F32, "share_third")]
+        share_cols = tile([P, S // P], F32, "share_cols")
         share_late = tile([P, QUARTER // P], F32, "share_late")
         x_view = xT.rearrange("(p t) s -> t p s", t=SLOTS)
         nc.sync.dma_start(x_rows[0][:], x_view[0])
         nc.sync.dma_start(offs_sb[:], offs)
-        nc.sync.dma_start(share_early[0][:], share[0, :HALF].rearrange("(p b) -> p b", p=P))
-        nc.sync.dma_start(share_early[1][:], share[0, EARLY:].rearrange("(p b) -> p b", p=P))
+        nc.sync.dma_start(share_cols[:], share[0].rearrange("(p b) -> p b", p=P))
         for t in range(1, SLOTS):
             nc.sync.dma_start(x_rows[t][:], x_view[t])
         nc.sync.dma_start(w1_raw[:], w1.rearrange("(p j) c -> p j c", j=SLOTS))
@@ -84,19 +83,21 @@ def tile_picked_treeup_relu_lo_kernel(tc, xT, w1, w2, share, offs, par, out_0, o
         for t in range(SLOTS):
             nc.sync.dma_start(w2_raw[:, t, :], w2_view[t])
         nc.sync.dma_start(par_sb[:], par)
-        nc.sync.dma_start(share_late[:], share[0, HALF:EARLY].rearrange("(b p) -> p b", p=P), allow_slow_non_contiguous=True)
 
         identity = tile([P, P], F32, "identity")
         make_identity(nc, identity[:])
 
         share_row = tile([P, S], F32, "share_row")
-        for u, columns in enumerate(share_early):
-            width = columns.shape[1]
-            spread = bank(u, [P, width, P])
-            for b in range(width):
-                nc.tensor.transpose(spread[:, b, :], columns[:, b : b + 1].to_broadcast([P, P]), identity[:])
-            part = share_row[:, u * EARLY : u * EARLY + width * P]
-            nc.scalar.copy(part.rearrange("p (n b) -> p n b", b=width), spread[:].rearrange("p b n -> p n b"))
+        share_view = share_row[:].rearrange("p (n u b) -> p u n b", u=2, b=4)
+        for u in range(2):
+            spread = bank(u, [P, 4, P])
+            for b in range(4):
+                nc.tensor.transpose(spread[:, b, :], share_cols[:, 4 * u + b : 4 * u + b + 1].to_broadcast([P, P]), identity[:])
+            nc.scalar.copy(share_view[:, u], spread[:].rearrange("p b n -> p n b"))
+        upright = bank(2, [P, 2, P])
+        for b in range(2):
+            nc.tensor.transpose(upright[:, b, :], share_row[:, HALF + b * BLOCK : HALF + (b + 1) * BLOCK], identity[:])
+        nc.scalar.copy(share_late[:], upright[:, :, 0])
 
         picked = tile([P, SLOTS, S], BF16, "picked")
 
@@ -191,7 +192,6 @@ def tile_picked_treeup_relu_lo_kernel(tc, xT, w1, w2, share, offs, par, out_0, o
         y_view = out_0.rearrange("(p t) s -> p t s", t=SLOTS)
         words_view = out_1[0].rearrange("p c r -> p (c r)").bitcast(I32)
         y_woven = tile([P, SLOTS * S], BF16, "y_woven")
-        y_codes = tile([P, S], U32, "y_codes")
         y_scales = tile([P, S], U8, "y_scales")
 
         def own_part(s0, count):
@@ -203,9 +203,9 @@ def tile_picked_treeup_relu_lo_kernel(tc, xT, w1, w2, share, offs, par, out_0, o
             nc.vector.tensor_tensor(woven(z_part[:]), planar(taken), planar(own_part(s0, count)), ADD)
             return z_part
 
-        def codes_of(s0, z_part):
+        def codes_of(s0, z_part, on=None):
             count = z_part.shape[1] // SLOTS
-            z_codes = tile([P, count], U32, "z_codes%d" % s0)
+            z_codes = tile([P, count], U32, "z_codes%d" % s0, on=on)
             z_scales = tile([P, count], U8, "z_scales%d" % s0)
             quantise(z_codes[:], z_scales[:], z_part[:])
             return z_codes, z_scales
@@ -267,11 +267,12 @@ def tile_picked_treeup_relu_lo_kernel(tc, xT, w1, w2, share, offs, par, out_0, o
         def weave(copy, s0, rows):
             copy(woven(nodes(y_woven, s0, rows.shape[2])), planar(rows))
 
-        def quantise_y(s0, count):
-            quantise(y_codes[:, s0 : s0 + count], y_scales[:, s0 : s0 + count], nodes(y_woven, s0, count))
+        def quantise_y(codes, s0):
+            count = codes.shape[1]
+            quantise(codes, y_scales[:, s0 : s0 + count], nodes(y_woven, s0, count))
 
-        def store_words(s0, count):
-            nc.sync.dma_start(words_view[:, s0 : s0 + count], y_codes[:, s0 : s0 + count].bitcast(I32))
+        def store_words(codes, s0):
+            nc.sync.dma_start(words_view[:, s0 : s0 + codes.shape[1]], codes[:].bitcast(I32))
 
         fetched_all = tile([P, SLOTS, QUARTER], F32, "fetched", on="w2_raw")
         fetched = [fetched_all[:, t, :] for t in range(SLOTS)]
@@ -289,7 +290,7 @@ def tile_picked_treeup_relu_lo_kernel(tc, xT, w1, w2, share, offs, par, out_0, o
         z_second = add_early(taken_first[:, :, QUARTER:], QUARTER)
         take(taken_last[:, 1, :], 1, EARLY, QUARTER)
         second_mx = codes_of(QUARTER, z_second)
-        backs = [scale_and_turn_back(turned[0], 0, 4, on="z_codes0"), scale_and_turn_back(turned[1], 1, 5, on="z_scales0")]
+        backs = [scale_and_turn_back(turned[0], 0, 4), scale_and_turn_back(turned[1], 1, 5)]
         y_next, next_sums = by_blocks(BLOCK, next_mx, (3,), nc.sync)
         weave_bank(0, first_sums[0])
         weave_bank(BLOCK, next_sums[0])
@@ -303,21 +304,24 @@ def tile_picked_treeup_relu_lo_kernel(tc, xT, w1, w2, share, offs, par, out_0, o
         y_turned, sums = by_blocks(HALF, codes_of(HALF, z_turned), (0, 1), nc.sync)
         weave_bank(HALF, sums[0])
         take(taken_last[:, 3, :], 3, EARLY, QUARTER)
-        quantise_y(0, QUARTER)
-        store_words(0, QUARTER)
+        codes_first = tile([P, QUARTER], U32, "codes_first", on="z_turned")
+        quantise_y(codes_first[:], 0)
+        store_words(codes_first, 0)
         z_before_last = add_early(taken_last[:, :, :BLOCK], EARLY)
         z_last = add_early(taken_last[:, :, BLOCK:], LAST)
         y_before_last, sums = by_blocks(EARLY, codes_of(EARLY, z_before_last), (2,), nc.sync)
         y_last = by_slots(LAST, codes_of(LAST, z_last), (3, 4), nc.scalar)
 
+        codes_middle = tile([P, HALF], U32, "codes_middle", on="planes")
         weave(nc.vector.tensor_copy, HALF + BLOCK, y_turned[:, :, BLOCK:])
-        quantise_y(QUARTER, QUARTER)
-        quantise_y(HALF, QUARTER)
-        store_words(QUARTER, HALF)
+        quantise_y(codes_middle[:, :QUARTER], QUARTER)
+        quantise_y(codes_middle[:, QUARTER:], HALF)
+        store_words(codes_middle, QUARTER)
         weave(nc.vector.tensor_copy, EARLY, y_before_last[:])
         weave(nc.vector.tensor_copy, LAST, y_last[:])
-        quantise_y(EARLY, QUARTER)
-        store_words(EARLY, QUARTER)
+        codes_last = tile([P, QUARTER], U32, "codes_last")
+        quantise_y(codes_last[:], EARLY)
+        store_words(codes_last, EARLY)
 
         scales_view = out_2[0].bitcast(I32)
         for q in range(4):

@@ -111,18 +111,17 @@ def tile_picked_treeup_relu_lo_kernel(tc, xT, w1, w2, share, offs, par, out_0, o
             pick_on_vector(t, 0, S - QUARTER)
             pick_on_scalar(t, S - QUARTER, QUARTER)
         pick_on_vector(SLOTS - 1, 0, QUARTER)
-        for s0 in range(QUARTER, S, QUARTER):
-            pick_on_scalar(SLOTS - 1, s0, QUARTER)
+        pick_on_scalar(SLOTS - 1, QUARTER, QUARTER)
+        pick_on_scalar(SLOTS - 1, HALF, HALF)
 
         x_woven = [tile([P, SLOTS * HALF], BF16, "x_woven%d" % u) for u in range(2)]
 
         def weave_x(copy, s0, count):
             copy(woven(nodes(x_woven[s0 // HALF], s0 % HALF, count)), planar(picked[:, :, s0 : s0 + count]))
 
-        for s0 in range(0, S - QUARTER, QUARTER):
-            weave_x(nc.vector.tensor_copy, s0, QUARTER)
+        weave_x(nc.vector.tensor_copy, 0, HALF)
         weave_x(nc.scalar.copy, LAST, BLOCK)
-        weave_x(nc.vector.tensor_copy, LAST - BLOCK, BLOCK)
+        weave_x(nc.vector.tensor_copy, HALF, HALF - BLOCK)
 
         w1_columns = w1_raw[:].rearrange("p j (g t h r) -> p t g h j r", t=SLOTS, h=2, r=4)
         w1_codes = tile([P, H], U32, "w1_codes")
@@ -301,24 +300,25 @@ def tile_picked_treeup_relu_lo_kernel(tc, xT, w1, w2, share, offs, par, out_0, o
         for b in range(2):
             add_late(nodes(z_turned, b * BLOCK, BLOCK), backs[b], b)
         take(taken_last[:, 2, :], 2, EARLY, QUARTER)
+        take(taken_last[:, 3, :], 3, EARLY, QUARTER)
         y_turned, sums = by_blocks(HALF, codes_of(HALF, z_turned), (0, 1), nc.sync)
         weave_bank(HALF, sums[0])
-        take(taken_last[:, 3, :], 3, EARLY, QUARTER)
-        codes_first = tile([P, QUARTER], U32, "codes_first", on="z_turned")
+        z_last = add_early(taken_last, EARLY)
+        codes_first = tile([P, QUARTER], U32, "codes_first", on="share_row")
         quantise_y(codes_first[:], 0)
         store_words(codes_first, 0)
-        z_before_last = add_early(taken_last[:, :, :BLOCK], EARLY)
-        z_last = add_early(taken_last[:, :, BLOCK:], LAST)
-        y_before_last, sums = by_blocks(EARLY, codes_of(EARLY, z_before_last), (2,), nc.sync)
-        y_last = by_slots(LAST, codes_of(LAST, z_last), (3, 4), nc.scalar)
+        last_mx = codes_of(EARLY, z_last)
+        y_late = [tile([P, SLOTS, BLOCK], F32, "y_late%d" % b) for b in range(2)]
+        for b, queue in enumerate((nc.sync, nc.scalar)):
+            multiply(last_mx, b * BLOCK, y_late[b][:], 0, 2 + b)
+            queue.dma_start(y_view[:, :, EARLY + b * BLOCK : EARLY + (b + 1) * BLOCK], y_late[b][:])
 
         codes_middle = tile([P, HALF], U32, "codes_middle", on="planes")
         weave(nc.vector.tensor_copy, HALF + BLOCK, y_turned[:, :, BLOCK:])
-        quantise_y(codes_middle[:, :QUARTER], QUARTER)
-        quantise_y(codes_middle[:, QUARTER:], HALF)
+        weave(nc.vector.tensor_copy, EARLY, y_late[0][:])
+        quantise_y(codes_middle[:], QUARTER)
         store_words(codes_middle, QUARTER)
-        weave(nc.vector.tensor_copy, EARLY, y_before_last[:])
-        weave(nc.vector.tensor_copy, LAST, y_last[:])
+        weave(nc.vector.tensor_copy, LAST, y_late[1][:])
         codes_last = tile([P, QUARTER], U32, "codes_last")
         quantise_y(codes_last[:], EARLY)
         store_words(codes_last, EARLY)

@@ -293,32 +293,29 @@ def tile_picked_treeup_relu_lo_kernel(tc, xT, w1, w2, share, offs, par, out_0, o
         y_next, next_sums = by_blocks(BLOCK, next_mx, (3,), nc.sync)
         weave_bank(0, first_sums[0])
         weave_bank(BLOCK, next_sums[0])
-        y_second, sums = by_blocks(QUARTER, second_mx, (6, 7), nc.sync)
-        for b in range(2):
-            weave_bank(QUARTER + b * BLOCK, sums[b])
+        y_second, second_sums = by_blocks(QUARTER, second_mx, (6, 7), nc.sync)
         z_turned = tile([P, SLOTS * QUARTER], BF16, "z_turned")
         for b in range(2):
             add_late(nodes(z_turned, b * BLOCK, BLOCK), backs[b], b)
         take(taken_last[:, 2, :], 2, EARLY, QUARTER)
-        take(taken_last[:, 3, :], 3, EARLY, QUARTER)
         y_turned, sums = by_blocks(HALF, codes_of(HALF, z_turned), (0, 1), nc.sync)
-        weave_bank(HALF, sums[0])
-        z_last = add_early(taken_last, EARLY)
-        codes_first = tile([P, QUARTER], U32, "codes_first", on="share_row")
+        for b in range(2):
+            weave_bank(QUARTER + b * BLOCK, second_sums[b])
+        take(taken_last[:, 3, :], 3, EARLY, QUARTER)
+        codes_first = tile([P, QUARTER], U32, "codes_first", on="z_turned")
         quantise_y(codes_first[:], 0)
         store_words(codes_first, 0)
-        last_mx = codes_of(EARLY, z_last)
-        y_late = [tile([P, SLOTS, BLOCK], F32, "y_late%d" % b) for b in range(2)]
-        for b, queue in enumerate((nc.sync, nc.scalar)):
-            multiply(last_mx, b * BLOCK, y_late[b][:], 0, 2 + b)
-            queue.dma_start(y_view[:, :, EARLY + b * BLOCK : EARLY + (b + 1) * BLOCK], y_late[b][:])
+        z_before_last = add_early(taken_last[:, :, :BLOCK], EARLY)
+        z_last = add_early(taken_last[:, :, BLOCK:], LAST)
+        y_before_last, sums = by_blocks(EARLY, codes_of(EARLY, z_before_last), (2,), nc.sync)
+        y_last = by_slots(LAST, codes_of(LAST, z_last), (3, 4), nc.scalar)
 
         codes_middle = tile([P, HALF], U32, "codes_middle", on="planes")
-        weave(nc.vector.tensor_copy, HALF + BLOCK, y_turned[:, :, BLOCK:])
-        weave(nc.vector.tensor_copy, EARLY, y_late[0][:])
+        weave(nc.vector.tensor_copy, HALF, y_turned[:])
+        weave(nc.vector.tensor_copy, EARLY, y_before_last[:])
         quantise_y(codes_middle[:], QUARTER)
         store_words(codes_middle, QUARTER)
-        weave(nc.vector.tensor_copy, LAST, y_late[1][:])
+        weave(nc.vector.tensor_copy, LAST, y_last[:])
         codes_last = tile([P, QUARTER], U32, "codes_last")
         quantise_y(codes_last[:], EARLY)
         store_words(codes_last, EARLY)

@@ -301,21 +301,23 @@ def tile_picked_treeup_relu_lo_kernel(tc, xT, w1, w2, share, offs, par, out_0, o
         y_turned, sums = by_blocks(HALF, codes_of(HALF, z_turned), (0, 1), nc.sync)
         for b in range(2):
             weave_bank(QUARTER + b * BLOCK, second_sums[b])
-        take(taken_last[:, 3, :], 3, EARLY, QUARTER)
-        codes_first = tile([P, QUARTER], U32, "codes_first", on="z_turned")
-        quantise_y(codes_first[:], 0)
-        store_words(codes_first, 0)
+        for b in range(2):
+            take(taken_last[:, 3, b * BLOCK : (b + 1) * BLOCK], 3, EARLY + b * BLOCK, BLOCK)
         z_before_last = add_early(taken_last[:, :, :BLOCK], EARLY)
         z_last = add_early(taken_last[:, :, BLOCK:], LAST)
         y_before_last, sums = by_blocks(EARLY, codes_of(EARLY, z_before_last), (2,), nc.sync)
-        y_last = by_slots(LAST, codes_of(LAST, z_last), (3, 4), nc.scalar)
+        y_last, sums = by_blocks(LAST, codes_of(LAST, z_last), (3,), nc.sync)
+        nc.scalar.copy(nodes(y_woven, LAST, BLOCK // 2).rearrange("p (s t) -> p s t", t=SLOTS), sums[0][:, :, : BLOCK // 2].rearrange("p t s -> p s t"))
 
+        codes_first = tile([P, QUARTER], U32, "codes_first", on="z_early%d" % EARLY)
+        quantise_y(codes_first[:], 0)
+        store_words(codes_first, 0)
         codes_middle = tile([P, HALF], U32, "codes_middle", on="planes")
         weave(nc.vector.tensor_copy, HALF, y_turned[:])
         weave(nc.vector.tensor_copy, EARLY, y_before_last[:])
         quantise_y(codes_middle[:], QUARTER)
         store_words(codes_middle, QUARTER)
-        weave(nc.vector.tensor_copy, LAST, y_last[:])
+        weave(nc.vector.tensor_copy, LAST + BLOCK // 2, y_last[:, :, BLOCK // 2 :])
         codes_last = tile([P, QUARTER], U32, "codes_last")
         quantise_y(codes_last[:], EARLY)
         store_words(codes_last, EARLY)

@@ -24,7 +24,6 @@ LIST_COL = 16
 HALF = S // 2
 QUARTER = S // 4
 BLOCK = 128
-BANKS = 8
 EARLY = S - QUARTER
 LAST = S - BLOCK
 
@@ -52,7 +51,7 @@ def tile_picked_treeup_relu_lo_kernel(tc, xT, w1, w2, share, offs, par, out_0, o
         psum = ctx.enter_context(tc.psum_pool(name="psum", bufs=1))
 
         def tile(shape, dtype, name, on=None):
-            return keep.tile(shape, dtype, name=name, tag=on or name, align_bytes=64)
+            return keep.tile(shape, dtype, name=name, tag=on or name, align_bytes=256)
 
         def bank(number, shape):
             return psum.tile(shape, F32, name="bank", tag="bank%d" % number)
@@ -226,14 +225,6 @@ def tile_picked_treeup_relu_lo_kernel(tc, xT, w1, w2, share, offs, par, out_0, o
             queue.dma_start(y_view[:, :, s0 : s0 + count], y_rows[:])
             return y_rows, sums
 
-        def by_slots(s0, z_mx, banks, queue):
-            count = z_mx[0].shape[1]
-            y_rows = tile([P, SLOTS, count], F32, "y_rows%d" % s0)
-            for u, number in enumerate(banks):
-                multiply(z_mx, 0, y_rows[:, 2 * u : 2 * u + 2, :], 2 * u, number)
-            queue.dma_start(y_view[:, :, s0 : s0 + count], y_rows[:])
-            return y_rows
-
         def weave_bank(s0, sums):
             nc.scalar.copy(nodes(y_woven, s0, BLOCK).rearrange("p (s t) -> p s t", t=SLOTS), sums[:].rearrange("p t s -> p s t"))
 
@@ -257,11 +248,6 @@ def tile_picked_treeup_relu_lo_kernel(tc, xT, w1, w2, share, offs, par, out_0, o
 
         def add_late(z_part, back, b):
             nc.vector.tensor_tensor(woven(z_part), planar(back[:]), planar(own_part(HALF + b * BLOCK, BLOCK)), ADD)
-
-        def weave_on_gpsimd(y_rows, name, on=None):
-            y_part = tile([P, SLOTS * QUARTER], BF16, name, on=on)
-            nc.gpsimd.tensor_scalar(y_part[:].rearrange("p (s t) -> p s t", t=SLOTS), y_rows[:].rearrange("p t s -> p s t"), 1.0, 0.0, MULT, ADD)
-            return y_part
 
         def weave(copy, s0, rows):
             copy(woven(nodes(y_woven, s0, rows.shape[2])), planar(rows))

@@ -24,8 +24,9 @@ LIST_COL = 16
 HALF = S // 2
 QUARTER = S // 4
 BLOCK = 128
-EARLY = S - QUARTER
-LAST = S - BLOCK
+TURNED = S - QUARTER
+EARLY = HALF
+LAST = EARLY + BLOCK
 
 
 def entries(list_tile, start, count):
@@ -95,7 +96,7 @@ def tile_picked_treeup_relu_lo_kernel(tc, xT, w1, w2, share, offs, par, out_0, o
             nc.scalar.copy(share_view[:, u], spread[:].rearrange("p b n -> p n b"))
         upright = bank(2, [P, 2, P])
         for b in range(2):
-            nc.tensor.transpose(upright[:, b, :], share_row[:, HALF + b * BLOCK : HALF + (b + 1) * BLOCK], identity[:])
+            nc.tensor.transpose(upright[:, b, :], share_row[:, TURNED + b * BLOCK : TURNED + (b + 1) * BLOCK], identity[:])
         nc.scalar.copy(share_late[:], upright[:, :, 0])
 
         picked = tile([P, SLOTS, S], BF16, "picked")
@@ -119,7 +120,7 @@ def tile_picked_treeup_relu_lo_kernel(tc, xT, w1, w2, share, offs, par, out_0, o
             copy(woven(nodes(x_woven[s0 // HALF], s0 % HALF, count)), planar(picked[:, :, s0 : s0 + count]))
 
         weave_x(nc.vector.tensor_copy, 0, HALF)
-        weave_x(nc.scalar.copy, LAST, BLOCK)
+        weave_x(nc.scalar.copy, S - BLOCK, BLOCK)
         weave_x(nc.vector.tensor_copy, HALF, HALF - BLOCK)
 
         w1_columns = w1_raw[:].rearrange("p j (g t h r) -> p t g h j r", t=SLOTS, h=2, r=4)
@@ -161,7 +162,7 @@ def tile_picked_treeup_relu_lo_kernel(tc, xT, w1, w2, share, offs, par, out_0, o
         h_rows = [tile([P, S], F32, "h_rows%d" % t) for t in range(SLOTS)]
         planes = tile([P, 2 * SLOTS, HALF], F32, "planes")
         own = [planes[:, :SLOTS, :], planes[:, SLOTS:, :]]
-        taken_last = planes[:, 2 : 2 + SLOTS, :QUARTER]
+        taken_last = planes[:, 2 : 2 + SLOTS, QUARTER:]
         for t in range(SLOTS):
             w_cols = slice(t * P, (t + 1) * P)
             for u in range(2):
@@ -225,6 +226,12 @@ def tile_picked_treeup_relu_lo_kernel(tc, xT, w1, w2, share, offs, par, out_0, o
             queue.dma_start(y_view[:, :, s0 : s0 + count], y_rows[:])
             return y_rows, sums
 
+        def pair_of_blocks(s0, z_mxs, banks):
+            y_rows = tile([P, SLOTS, QUARTER], F32, "y_rows%d" % s0)
+            sums = [multiply(z_mxs[b], 0, y_rows[:, :, b * BLOCK : (b + 1) * BLOCK], 0, banks[b]) for b in range(2)]
+            nc.sync.dma_start(y_view[:, :, s0 : s0 + QUARTER], y_rows[:])
+            return y_rows, sums
+
         def weave_bank(s0, sums):
             nc.scalar.copy(nodes(y_woven, s0, BLOCK).rearrange("p (s t) -> p s t", t=SLOTS), sums[:].rearrange("p t s -> p s t"))
 
@@ -247,7 +254,7 @@ def tile_picked_treeup_relu_lo_kernel(tc, xT, w1, w2, share, offs, par, out_0, o
             return back
 
         def add_late(z_part, back, b):
-            nc.vector.tensor_tensor(woven(z_part), planar(back[:]), planar(own_part(HALF + b * BLOCK, BLOCK)), ADD)
+            nc.vector.tensor_tensor(woven(z_part), planar(back[:]), planar(own_part(TURNED + b * BLOCK, BLOCK)), ADD)
 
         def weave(copy, s0, rows):
             copy(woven(nodes(y_woven, s0, rows.shape[2])), planar(rows))
@@ -263,46 +270,50 @@ def tile_picked_treeup_relu_lo_kernel(tc, xT, w1, w2, share, offs, par, out_0, o
         fetched = [fetched_all[:, t, :] for t in range(SLOTS)]
         turned = [bank(number, [P, SLOTS, P]) for number in (0, 1)]
         for t in range(SLOTS):
-            fetch(gather_on_scalar, fetched, t, HALF)
+            fetch(gather_on_scalar, fetched, t, TURNED)
             turn(turned, fetched[t], t)
 
         z_first = add_early(taken_first[:, :, :BLOCK], 0)
         quantise_w2(w2_lower, 0)
         y_first, first_sums = by_blocks(0, codes_of(0, z_first), (2,), nc.sync)
-        z_next = add_early(taken_first[:, :, BLOCK:QUARTER], BLOCK)
+        z_blocks = [z_first] + [add_early(taken_first[:, :, b * BLOCK : (b + 1) * BLOCK], b * BLOCK) for b in (1, 2)]
+        next_mx = codes_of(BLOCK, z_blocks[1])
+        z_blocks.append(add_early(taken_first[:, :, 3 * BLOCK :], 3 * BLOCK))
+        second_mx = [codes_of(2 * BLOCK, z_blocks[2])]
         take(taken_last[:, 0, :], 0, EARLY, QUARTER)
-        next_mx = codes_of(BLOCK, z_next)
-        z_second = add_early(taken_first[:, :, QUARTER:], QUARTER)
+        second_mx.append(codes_of(3 * BLOCK, z_blocks[3]))
         take(taken_last[:, 1, :], 1, EARLY, QUARTER)
-        second_mx = codes_of(QUARTER, z_second)
         backs = [scale_and_turn_back(turned[0], 0, 4), scale_and_turn_back(turned[1], 1, 5)]
         y_next, next_sums = by_blocks(BLOCK, next_mx, (3,), nc.sync)
+        y_second, second_sums = pair_of_blocks(QUARTER, second_mx, (6, 7))
         weave_bank(0, first_sums[0])
         weave_bank(BLOCK, next_sums[0])
-        y_second, second_sums = by_blocks(QUARTER, second_mx, (6, 7), nc.sync)
-        z_turned = tile([P, SLOTS * QUARTER], BF16, "z_turned")
+        z_turned = [tile([P, SLOTS * BLOCK], BF16, "z_turned%d" % b) for b in range(2)]
         for b in range(2):
-            add_late(nodes(z_turned, b * BLOCK, BLOCK), backs[b], b)
+            add_late(z_turned[b][:], backs[b], b)
+        turned_mx = [codes_of(TURNED, z_turned[0])]
         take(taken_last[:, 2, :], 2, EARLY, QUARTER)
-        y_turned, sums = by_blocks(HALF, codes_of(HALF, z_turned), (0, 1), nc.sync)
+        turned_mx.append(codes_of(TURNED + BLOCK, z_turned[1]))
+        y_turned, sums = pair_of_blocks(TURNED, turned_mx, (0, 1))
         for b in range(2):
             weave_bank(QUARTER + b * BLOCK, second_sums[b])
         for b in range(2):
             take(taken_last[:, 3, b * BLOCK : (b + 1) * BLOCK], 3, EARLY + b * BLOCK, BLOCK)
         z_before_last = add_early(taken_last[:, :, :BLOCK], EARLY)
         z_last = add_early(taken_last[:, :, BLOCK:], LAST)
-        y_before_last, sums = by_blocks(EARLY, codes_of(EARLY, z_before_last), (2,), nc.sync)
-        y_last, sums = by_blocks(LAST, codes_of(LAST, z_last), (3,), nc.sync)
-        nc.scalar.copy(nodes(y_woven, LAST, BLOCK // 2).rearrange("p (s t) -> p s t", t=SLOTS), sums[0][:, :, : BLOCK // 2].rearrange("p t s -> p s t"))
+        y_end, sums = pair_of_blocks(EARLY, [codes_of(EARLY, z_before_last), codes_of(LAST, z_last)], (2, 3))
+        y_before_last, y_last = y_end[:, :, :BLOCK], y_end[:, :, BLOCK:]
+        nc.scalar.copy(nodes(y_woven, LAST, BLOCK // 2).rearrange("p (s t) -> p s t", t=SLOTS), sums[1][:, :, : BLOCK // 2].rearrange("p t s -> p s t"))
 
         codes_first = tile([P, QUARTER], U32, "codes_first", on="z_early%d" % EARLY)
         quantise_y(codes_first[:], 0)
         store_words(codes_first, 0)
-        codes_middle = tile([P, HALF], U32, "codes_middle", on="planes")
-        weave(nc.vector.tensor_copy, HALF, y_turned[:])
-        weave(nc.vector.tensor_copy, EARLY, y_before_last[:])
-        quantise_y(codes_middle[:], QUARTER)
-        store_words(codes_middle, QUARTER)
+        weave(nc.vector.tensor_copy, TURNED, y_turned[:])
+        codes_middle = tile([P, 2, QUARTER], U32, "codes_middle", on="planes")
+        quantise_y(codes_middle[:, 0, :], QUARTER)
+        quantise_y(codes_middle[:, 1, :], TURNED)
+        nc.sync.dma_start(words_view.rearrange("p (u c) -> p u c", u=2)[:, :, QUARTER:], codes_middle[:].bitcast(I32))
+        weave(nc.vector.tensor_copy, EARLY, y_before_last)
         weave(nc.vector.tensor_copy, LAST + BLOCK // 2, y_last[:, :, BLOCK // 2 :])
         codes_last = tile([P, QUARTER], U32, "codes_last")
         quantise_y(codes_last[:], EARLY)

@@ -160,8 +160,8 @@ def tile_picked_treeup_relu_lo_kernel(tc, xT, w1, w2, share, offs, par, out_0, o
         deal_w2(nc.vector.tensor_copy, w2_upper, 1)
 
         h_rows = [tile([P, S], F32, "h_rows%d" % t) for t in range(SLOTS)]
-        planes = tile([P, 2 * SLOTS, HALF], F32, "planes")
-        own = [planes[:, :SLOTS, :], planes[:, SLOTS:, :]]
+        planes = tile([P, 2 * SLOTS + 2, HALF], F32, "planes")
+        own = [planes[:, :SLOTS, :], planes[:, SLOTS + 2 :, :]]
         taken_last = planes[:, 2 : 2 + SLOTS, QUARTER:]
         for t in range(SLOTS):
             w_cols = slice(t * P, (t + 1) * P)
@@ -190,16 +190,15 @@ def tile_picked_treeup_relu_lo_kernel(tc, xT, w1, w2, share, offs, par, out_0, o
 
         y_view = out_0.rearrange("(p t) s -> p t s", t=SLOTS)
         words_view = out_1[0].rearrange("p c r -> p (c r)").bitcast(I32)
-        y_woven = tile([P, SLOTS * S], BF16, "y_woven")
         y_scales = tile([P, S], U8, "y_scales")
 
         def own_part(s0, count):
             return own[s0 // HALF][:, :, s0 % HALF : s0 % HALF + count]
 
-        def add_early(taken, s0):
-            count = taken.shape[2]
-            z_part = tile([P, SLOTS * count], BF16, "z_early%d" % s0)
-            nc.vector.tensor_tensor(woven(z_part[:]), planar(taken), planar(own_part(s0, count)), ADD)
+        def add_early(taken, s0, z_part=None):
+            if z_part is None:
+                z_part = tile([P, SLOTS * BLOCK], BF16, "z_early%d" % s0)[:]
+            nc.vector.tensor_tensor(woven(z_part), planar(taken), planar(own_part(s0, BLOCK)), ADD)
             return z_part
 
         def codes_of(s0, z_part, on=None):
@@ -266,7 +265,7 @@ def tile_picked_treeup_relu_lo_kernel(tc, xT, w1, w2, share, offs, par, out_0, o
         def store_words(codes, s0):
             nc.sync.dma_start(words_view[:, s0 : s0 + codes.shape[1]], codes[:].bitcast(I32))
 
-        fetched_all = tile([P, SLOTS, QUARTER], F32, "fetched", on="w2_raw")
+        fetched_all = tile([P, SLOTS + 1, QUARTER], F32, "fetched", on="w2_raw")
         fetched = [fetched_all[:, t, :] for t in range(SLOTS)]
         turned = [bank(number, [P, SLOTS, P]) for number in (0, 1)]
         for t in range(SLOTS):
@@ -278,46 +277,41 @@ def tile_picked_treeup_relu_lo_kernel(tc, xT, w1, w2, share, offs, par, out_0, o
         y_first, first_sums = by_blocks(0, codes_of(0, z_first), (2,), nc.sync)
         z_blocks = [z_first] + [add_early(taken_first[:, :, b * BLOCK : (b + 1) * BLOCK], b * BLOCK) for b in (1, 2)]
         next_mx = codes_of(BLOCK, z_blocks[1])
-        z_blocks.append(add_early(taken_first[:, :, 3 * BLOCK :], 3 * BLOCK))
+        z_blocks.append(add_early(taken_first[:, :, 3 * BLOCK :], 3 * BLOCK, taken_last[:, 2, :].bitcast(BF16)))
         second_mx = [codes_of(2 * BLOCK, z_blocks[2])]
         take(taken_last[:, 0, :], 0, EARLY, QUARTER)
         second_mx.append(codes_of(3 * BLOCK, z_blocks[3]))
         take(taken_last[:, 1, :], 1, EARLY, QUARTER)
+        plain = [fetched_all[:, SLOTS, :]]
+        gather_on_scalar(plain[0], h_rows[2][:].indirect(entries(par_sb, EARLY, QUARTER)))
         backs = [scale_and_turn_back(turned[0], 0, 4), scale_and_turn_back(turned[1], 1, 5)]
-        y_next, next_sums = by_blocks(BLOCK, next_mx, (3,), nc.sync)
-        y_second, second_sums = pair_of_blocks(QUARTER, second_mx, (6, 7))
-        weave_bank(0, first_sums[0])
-        weave_bank(BLOCK, next_sums[0])
+        plain.append(tile([P, QUARTER], F32, "plain3", on="scaled0")[:])
+        gather_on_scalar(plain[1], h_rows[3][:].indirect(entries(par_sb, EARLY, QUARTER)))
+        for t in (2, 3):
+            nc.gpsimd.tensor_tensor(taken_last[:, t, :], plain[t - 2], share_row[:, EARLY : EARLY + QUARTER], MULT)
+        y_next, sums = by_blocks(BLOCK, next_mx, (3,), nc.sync)
+        y_second, sums = pair_of_blocks(QUARTER, second_mx, (6, 7))
         z_turned = [tile([P, SLOTS * BLOCK], BF16, "z_turned%d" % b) for b in range(2)]
         for b in range(2):
             add_late(z_turned[b][:], backs[b], b)
-        turned_mx = [codes_of(TURNED, z_turned[0])]
-        take(taken_last[:, 2, :], 2, EARLY, QUARTER)
-        turned_mx.append(codes_of(TURNED + BLOCK, z_turned[1]))
-        y_turned, sums = pair_of_blocks(TURNED, turned_mx, (0, 1))
+        y_turned, sums = pair_of_blocks(TURNED, [codes_of(TURNED + b * BLOCK, z_turned[b]) for b in range(2)], (0, 1))
+        z_last = [add_early(taken_last[:, :, b * BLOCK : (b + 1) * BLOCK], EARLY + b * BLOCK) for b in range(2)]
+        y_end, sums = pair_of_blocks(EARLY, [codes_of(EARLY + b * BLOCK, z_last[b]) for b in range(2)], (2, 3))
+        y_woven = tile([P, SLOTS * S], BF16, "y_woven", on="planes")
         for b in range(2):
-            weave_bank(QUARTER + b * BLOCK, second_sums[b])
-        for b in range(2):
-            take(taken_last[:, 3, b * BLOCK : (b + 1) * BLOCK], 3, EARLY + b * BLOCK, BLOCK)
-        z_before_last = add_early(taken_last[:, :, :BLOCK], EARLY)
-        z_last = add_early(taken_last[:, :, BLOCK:], LAST)
-        y_end, sums = pair_of_blocks(EARLY, [codes_of(EARLY, z_before_last), codes_of(LAST, z_last)], (2, 3))
-        y_before_last, y_last = y_end[:, :, :BLOCK], y_end[:, :, BLOCK:]
-        nc.scalar.copy(nodes(y_woven, LAST, BLOCK // 2).rearrange("p (s t) -> p s t", t=SLOTS), sums[1][:, :, : BLOCK // 2].rearrange("p t s -> p s t"))
+            weave_bank(EARLY + b * BLOCK, sums[b])
 
-        codes_first = tile([P, QUARTER], U32, "codes_first", on="z_early%d" % EARLY)
+        weave(nc.vector.tensor_copy, 0, y_first[:])
+        weave(nc.vector.tensor_copy, BLOCK, y_next[:])
+        weave(nc.vector.tensor_copy, QUARTER, y_second[:])
+        codes_first = tile([P, HALF], U32, "codes_first")
+        weave(nc.vector.tensor_copy, TURNED, y_turned[:])
         quantise_y(codes_first[:], 0)
         store_words(codes_first, 0)
-        weave(nc.vector.tensor_copy, TURNED, y_turned[:])
-        codes_middle = tile([P, 2, QUARTER], U32, "codes_middle", on="planes")
-        quantise_y(codes_middle[:, 0, :], QUARTER)
-        quantise_y(codes_middle[:, 1, :], TURNED)
-        nc.sync.dma_start(words_view.rearrange("p (u c) -> p u c", u=2)[:, :, QUARTER:], codes_middle[:].bitcast(I32))
-        weave(nc.vector.tensor_copy, EARLY, y_before_last)
-        weave(nc.vector.tensor_copy, LAST + BLOCK // 2, y_last[:, :, BLOCK // 2 :])
-        codes_last = tile([P, QUARTER], U32, "codes_last")
-        quantise_y(codes_last[:], EARLY)
-        store_words(codes_last, EARLY)
+        codes_last = tile([P, HALF], U32, "codes_last")
+        quantise_y(codes_last[:, QUARTER:], TURNED)
+        quantise_y(codes_last[:, :QUARTER], EARLY)
+        store_words(codes_last, HALF)
 
         scales_view = out_2[0].bitcast(I32)
         for q in range(4):

from contextlib import ExitStack

import concourse.mybir as mybir
from concourse.masks import make_identity

K, T, S, H = 512, 2048, 1024, 512
FLOPS = 2 * K * H * S + 2 * H * H * S

F32 = mybir.dt.float32
BF16 = mybir.dt.bfloat16
I32 = mybir.dt.int32
U32 = mybir.dt.uint32
U16 = mybir.dt.uint16
U8 = mybir.dt.uint8
FP8X4 = mybir.dt.float8_e4m3fn_x4
MULT = mybir.AluOpType.mult
ADD = mybir.AluOpType.add
COPY = mybir.ActivationFunctionType.Copy
RELU = mybir.ActivationFunctionType.Relu

P = 128
SLOTS = 4
LIST_COL = 16
HALF = S // 2
QUARTER = S // 4
BLOCK = 128
TURNED = S - QUARTER
EARLY = HALF
LAST = EARLY + BLOCK


def entries(list_tile, start, count):
    return list_tile[:, start // LIST_COL : (start + count) // LIST_COL]


def woven(ap):
    return ap.rearrange("p (c i t) -> p c t i", i=4, t=SLOTS)


def planar(ap):
    return ap.rearrange("p t (c i) -> p c t i", i=4)


def nodes(woven_tile, start, count):
    return woven_tile[:, SLOTS * start : SLOTS * (start + count)]


def tile_picked_treeup_relu_lo_kernel(tc, xT, w1, w2, share, offs, par, out_0, out_1, out_2):
    nc = tc.nc
    with ExitStack() as ctx:
        keep = ctx.enter_context(tc.tile_pool(name="keep", bufs=1))
        psum = ctx.enter_context(tc.psum_pool(name="psum", bufs=1))

        def tile(shape, dtype, name, on=None):
            return keep.tile(shape, dtype, name=name, tag=on or name, align_bytes=256)

        def bank(number, shape):
            return psum.tile(shape, F32, name="bank", tag="bank%d" % number)

        def quantise(codes, scales, values):
            nc.vector.quantize_mx(out=codes.bitcast(FP8X4), scales=scales, in_=values)

        def product(out, w_codes, w_scales, codes, scales):
            nc.tensor.matmul_mx(
                out=out, lhsT=w_codes.bitcast(FP8X4), lhsT_scale=w_scales, rhs=codes.bitcast(FP8X4), rhs_scale=scales, start=True, stop=True
            )

        offs_sb = keep.tile([P, S // LIST_COL], U16, name="offs_sb")
        par_sb = keep.tile([P, S // LIST_COL], U16, name="par_sb")
        x_rows = [tile([P, T], F32, "x_rows%d" % t) for t in range(SLOTS)]
        w1_raw = tile([P, SLOTS, H], F32, "w1_raw")
        w2_raw = tile([P, SLOTS, H], F32, "w2_raw")
        share_cols = tile([P, S // P], F32, "share_cols")
        share_late = tile([P, QUARTER // P], F32, "share_late")
        x_view = xT.rearrange("(p t) s -> t p s", t=SLOTS)
        nc.sync.dma_start(x_rows[0][:], x_view[0])
        nc.sync.dma_start(offs_sb[:], offs)
        nc.sync.dma_start(share_cols[:], share[0].rearrange("(p b) -> p b", p=P))
        for t in range(1, SLOTS):
            nc.sync.dma_start(x_rows[t][:], x_view[t])
        nc.sync.dma_start(w1_raw[:], w1.rearrange("(p j) c -> p j c", j=SLOTS))
        w2_view = w2.rearrange("(g t r) c -> t g r c", t=SLOTS, r=8)
        for t in range(SLOTS):
            nc.sync.dma_start(w2_raw[:, t, :], w2_view[t])
        nc.sync.dma_start(par_sb[:], par)

        identity = tile([P, P], F32, "identity")
        make_identity(nc, identity[:])

        share_row = tile([P, S], F32, "share_row")
        share_view = share_row[:].rearrange("p (n u b) -> p u n b", u=2, b=4)
        for u in range(2):
            spread = bank(u, [P, 4, P])
            for b in range(4):
                nc.tensor.transpose(spread[:, b, :], share_cols[:, 4 * u + b : 4 * u + b + 1].to_broadcast([P, P]), identity[:])
            nc.scalar.copy(share_view[:, u], spread[:].rearrange("p b n -> p n b"))
        upright = bank(2, [P, 2, P])
        for b in range(2):
            nc.tensor.transpose(upright[:, b, :], share_row[:, TURNED + b * BLOCK : TURNED + (b + 1) * BLOCK], identity[:])
        nc.scalar.copy(share_late[:], upright[:, :, 0])

        picked = tile([P, SLOTS, S], BF16, "picked")

        def pick_on_vector(t, s0, count):
            nc.vector.tensor_copy(picked[:, t, s0 : s0 + count], x_rows[t][:].indirect(entries(offs_sb, s0, count)))

        def pick_on_scalar(t, s0, count):
            nc.scalar.activation(picked[:, t, s0 : s0 + count], x_rows[t][:].indirect(entries(offs_sb, s0, count)), COPY)

        for t in range(SLOTS - 1):
            pick_on_vector(t, 0, S - QUARTER)
            pick_on_scalar(t, S - QUARTER, QUARTER)
        pick_on_vector(SLOTS - 1, 0, QUARTER)
        pick_on_scalar(SLOTS - 1, QUARTER, QUARTER)
        pick_on_scalar(SLOTS - 1, HALF, HALF)

        x_woven = [tile([P, SLOTS * HALF], BF16, "x_woven%d" % u) for u in range(2)]

        def weave_x(copy, s0, count):
            copy(woven(nodes(x_woven[s0 // HALF], s0 % HALF, count)), planar(picked[:, :, s0 : s0 + count]))

        weave_x(nc.vector.tensor_copy, 0, HALF)
        weave_x(nc.scalar.copy, S - BLOCK, BLOCK)
        weave_x(nc.vector.tensor_copy, HALF, HALF - BLOCK)

        w1_columns = w1_raw[:].rearrange("p j (g t h r) -> p t g h j r", t=SLOTS, h=2, r=4)
        w1_codes = tile([P, H], U32, "w1_codes")
        w1_scales = tile([P, H], U8, "w1_scales")
        w1_dealt = [tile([P, SLOTS * P], BF16, "w1_dealt%d" % t) for t in range(SLOTS - 1)]

        def deal_w1(copy, t):
            copy(w1_dealt[t][:].rearrange("p (g h r j) -> p g h j r", h=2, r=4, j=SLOTS), w1_columns[:, t])

        def quantise_w1(t):
            cols = slice(t * P, (t + 1) * P)
            quantise(w1_codes[:, cols], w1_scales[:, cols], w1_dealt[t][:])

        def deal_w2(copy, dealt, half):
            columns = w2_raw[:].rearrange("p j (m u e) -> p u m j e", u=2, e=2)
            copy(dealt[:].rearrange("p (e m j) -> p m j e", e=2, j=SLOTS), columns[:, half])

        def quantise_w2(dealt, half):
            cols = slice(half * H // 2, (half + 1) * H // 2)
            quantise(w2_codes[:, cols], w2_scales[:, cols], dealt[:])

        for t in range(SLOTS - 1):
            deal_w1(nc.scalar.copy, t)
        x_codes = [tile([P, HALF], U32, "x_codes0")]
        x_scales = [tile([P, HALF], U8, "x_scales%d" % u) for u in range(2)]
        quantise(x_codes[0][:], x_scales[0][:], x_woven[0][:])
        quantise_w1(0)
        x_codes.append(tile([P, HALF], U32, "x_codes1", on="w1_dealt0"))
        quantise(x_codes[1][:], x_scales[1][:], x_woven[1][:])
        quantise_w1(1)
        w1_dealt.append(tile([P, SLOTS * P], BF16, "w1_dealt3", on="w1_dealt1"))
        deal_w1(nc.vector.tensor_copy, 3)
        quantise_w1(2)
        quantise_w1(3)
        w2_upper = tile([P, 2 * P * SLOTS], BF16, "w2_upper")
        deal_w2(nc.vector.tensor_copy, w2_upper, 1)

        h_rows = [tile([P, S], F32, "h_rows%d" % t) for t in range(SLOTS)]
        planes = tile([P, 2 * SLOTS + 2, HALF], F32, "planes")
        own = [planes[:, :SLOTS, :], planes[:, SLOTS + 2 :, :]]
        taken_last = planes[:, 2 : 2 + SLOTS, QUARTER:]
        for t in range(SLOTS):
            w_cols = slice(t * P, (t + 1) * P)
            for u in range(2):
                cols = slice(u * HALF, (u + 1) * HALF)
                sums = bank(2 * t + u, [P, HALF])
                product(sums[:], w1_codes[:, w_cols], w1_scales[:, w_cols], x_codes[u][:], x_scales[u][:])
                nc.scalar.activation(h_rows[t][:, cols], sums[:], RELU)
                skip = QUARTER if (t, u) == (SLOTS - 1, 0) else 0
                nc.sync.dma_start(own[u][:, t, skip:], h_rows[t][:, u * HALF + skip : (u + 1) * HALF])

        w2_lower = tile([P, 2 * P * SLOTS], BF16, "w2_lower", on="w1_codes")
        deal_w2(nc.scalar.copy, w2_lower, 0)

        def take(out, t, s0, count):
            nc.vector.tensor_tensor(out, h_rows[t][:].indirect(entries(par_sb, s0, count)), share_row[:, s0 : s0 + count], MULT)

        taken_first = tile([P, SLOTS, HALF], F32, "taken_first")
        for t in range(SLOTS):
            if t == SLOTS - 1:
                nc.vector.tensor_copy(own[0][:, t, :QUARTER], h_rows[t][:, :QUARTER])
            take(taken_first[:, t, :], t, 0, HALF)
        w2_codes = tile([P, H], U32, "w2_codes")
        w2_scales = tile([P, H], U8, "w2_scales")
        quantise_w2(w2_upper, 1)

        y_view = out_0.rearrange("(p t) s -> p t s", t=SLOTS)
        words_view = out_1[0].rearrange("p c r -> p (c r)").bitcast(I32)
        y_scales = tile([P, S], U8, "y_scales")

        def own_part(s0, count):
            return own[s0 // HALF][:, :, s0 % HALF : s0 % HALF + count]

        def add_early(taken, s0, z_part=None):
            if z_part is None:
                z_part = tile([P, SLOTS * BLOCK], BF16, "z_early%d" % s0)[:]
            nc.vector.tensor_tensor(woven(z_part), planar(taken), planar(own_part(s0, BLOCK)), ADD)
            return z_part

        def codes_of(s0, z_part, on=None):
            count = z_part.shape[1] // SLOTS
            z_codes = tile([P, count], U32, "z_codes%d" % s0, on=on)
            z_scales = tile([P, count], U8, "z_scales%d" % s0)
            quantise(z_codes[:], z_scales[:], z_part[:])
            return z_codes, z_scales

        def multiply(z_mx, s0, y_part, first_slot, number):
            z_codes, z_scales = z_mx
            slots, count = y_part.shape[1], y_part.shape[2]
            sums = bank(number, [P, slots, count])
            for e in range(slots):
                w_cols = slice((first_slot + e) * P, (first_slot + e + 1) * P)
                product(sums[:, e, :], w2_codes[:, w_cols], w2_scales[:, w_cols], z_codes[:, s0 : s0 + count], z_scales[:, s0 : s0 + count])
            nc.scalar.copy(y_part, sums[:])
            return sums

        def by_blocks(s0, z_mx, banks, queue):
            count = z_mx[0].shape[1]
            y_rows = tile([P, SLOTS, count], F32, "y_rows%d" % s0)
            sums = [multiply(z_mx, b * BLOCK, y_rows[:, :, b * BLOCK : (b + 1) * BLOCK], 0, number) for b, number in enumerate(banks)]
            queue.dma_start(y_view[:, :, s0 : s0 + count], y_rows[:])
            return y_rows, sums

        def pair_of_blocks(s0, z_mxs, banks):
            y_rows = tile([P, SLOTS, QUARTER], F32, "y_rows%d" % s0)
            sums = [multiply(z_mxs[b], 0, y_rows[:, :, b * BLOCK : (b + 1) * BLOCK], 0, banks[b]) for b in range(2)]
            nc.sync.dma_start(y_view[:, :, s0 : s0 + QUARTER], y_rows[:])
            return y_rows, sums

        def weave_bank(s0, sums):
            nc.scalar.copy(nodes(y_woven, s0, BLOCK).rearrange("p (s t) -> p s t", t=SLOTS), sums[:].rearrange("p t s -> p s t"))

        def fetch(gather, fetched, t, s0):
            gather(fetched[t], h_rows[t][:].indirect(entries(par_sb, s0, QUARTER)))

        def gather_on_scalar(out, window):
            nc.scalar.activation(out, window, COPY)

        def turn(turned, fetched, t):
            for e in range(2):
                nc.tensor.transpose(turned[e][:, t, :], fetched[:, e * BLOCK : (e + 1) * BLOCK], identity[:])

        def scale_and_turn_back(turned, b, number, on=None):
            scaled = tile([P, SLOTS, P], F32, "scaled%d" % b, on=on)
            nc.scalar.activation(scaled[:], turned[:], COPY, scale=share_late[:, b : b + 1])
            back = bank(number, [P, SLOTS, BLOCK])
            for t in range(SLOTS):
                nc.tensor.transpose(back[:, t, :], scaled[:, t, :], identity[:])
            return back

        def add_late(z_part, back, b):
            nc.vector.tensor_tensor(woven(z_part), planar(back[:]), planar(own_part(TURNED + b * BLOCK, BLOCK)), ADD)

        def weave(copy, s0, rows):
            copy(woven(nodes(y_woven, s0, rows.shape[2])), planar(rows))

        def quantise_y(codes, s0):
            count = codes.shape[1]
            quantise(codes, y_scales[:, s0 : s0 + count], nodes(y_woven, s0, count))

        def store_words(codes, s0):
            nc.sync.dma_start(words_view[:, s0 : s0 + codes.shape[1]], codes[:].bitcast(I32))

        fetched_all = tile([P, SLOTS + 1, QUARTER], F32, "fetched", on="w2_raw")
        fetched = [fetched_all[:, t, :] for t in range(SLOTS)]
        turned = [bank(number, [P, SLOTS, P]) for number in (0, 1)]
        for t in range(SLOTS):
            fetch(gather_on_scalar, fetched, t, TURNED)
            turn(turned, fetched[t], t)

        z_first = add_early(taken_first[:, :, :BLOCK], 0)
        quantise_w2(w2_lower, 0)
        y_first, first_sums = by_blocks(0, codes_of(0, z_first), (2,), nc.sync)
        z_blocks = [z_first] + [add_early(taken_first[:, :, b * BLOCK : (b + 1) * BLOCK], b * BLOCK) for b in (1, 2)]
        next_mx = codes_of(BLOCK, z_blocks[1])
        z_blocks.append(add_early(taken_first[:, :, 3 * BLOCK :], 3 * BLOCK, taken_last[:, 2, :].bitcast(BF16)))
        second_mx = [codes_of(2 * BLOCK, z_blocks[2])]
        take(taken_last[:, 0, :], 0, EARLY, QUARTER)
        second_mx.append(codes_of(3 * BLOCK, z_blocks[3]))
        take(taken_last[:, 1, :], 1, EARLY, QUARTER)
        plain = [fetched_all[:, SLOTS, :]]
        gather_on_scalar(plain[0], h_rows[2][:].indirect(entries(par_sb, EARLY, QUARTER)))
        backs = [scale_and_turn_back(turned[0], 0, 4), scale_and_turn_back(turned[1], 1, 5)]
        plain.append(tile([P, QUARTER], F32, "plain3", on="scaled0")[:])
        gather_on_scalar(plain[1], h_rows[3][:].indirect(entries(par_sb, EARLY, QUARTER)))
        for t in (2, 3):
            nc.gpsimd.tensor_tensor(taken_last[:, t, :], plain[t - 2], share_row[:, EARLY : EARLY + QUARTER], MULT)
        y_next, sums = by_blocks(BLOCK, next_mx, (3,), nc.sync)
        y_second, sums = pair_of_blocks(QUARTER, second_mx, (6, 7))
        z_turned = [tile([P, SLOTS * BLOCK], BF16, "z_turned%d" % b) for b in range(2)]
        for b in range(2):
            add_late(z_turned[b][:], backs[b], b)
        y_turned, sums = pair_of_blocks(TURNED, [codes_of(TURNED + b * BLOCK, z_turned[b]) for b in range(2)], (0, 1))
        z_last = [add_early(taken_last[:, :, b * BLOCK : (b + 1) * BLOCK], EARLY + b * BLOCK) for b in range(2)]
        y_end, sums = pair_of_blocks(EARLY, [codes_of(EARLY + b * BLOCK, z_last[b]) for b in range(2)], (2, 3))
        y_woven = tile([P, SLOTS * S], BF16, "y_woven", on="planes")
        for b in range(2):
            weave_bank(EARLY + b * BLOCK, sums[b])

        weave(nc.vector.tensor_copy, 0, y_first[:])
        weave(nc.vector.tensor_copy, BLOCK, y_next[:])
        weave(nc.vector.tensor_copy, QUARTER, y_second[:])
        codes_first = tile([P, HALF], U32, "codes_first")
        weave(nc.vector.tensor_copy, TURNED, y_turned[:])
        quantise_y(codes_first[:], 0)
        store_words(codes_first, 0)
        codes_last = tile([P, HALF], U32, "codes_last")
        quantise_y(codes_last[:, QUARTER:], TURNED)
        quantise_y(codes_last[:, :QUARTER], EARLY)
        store_words(codes_last, HALF)

        scales_view = out_2[0].bitcast(I32)
        for q in range(4):
            queue = nc.sync if q % 2 == 0 else nc.scalar
            queue.dma_start(scales_view[4 * q : 4 * q + 4, :], y_scales[32 * q : 32 * q + 4, :].bitcast(I32))
